import numpy as np, ml_dtypes
CORES = [113,118,241,246]
N = 4
BF = ml_dtypes.bfloat16
def gentries(a):
    return np.ascontiguousarray(a.reshape(8, 16, -1).transpose(0, 2, 1)).reshape(8, -1)
def gtable(e):
    e = np.asarray(e); return np.ascontiguousarray(e.reshape(8, -1, 16).transpose(0, 2, 1)).reshape(128, -1).astype(np.int32)
W, K, TV, S, RO, QV = 1536, 384, 4, 3, 3, 17
CH = 16
def sgn(rng, *shape):
    return 2.0 * rng.integers(0, 2, shape) - 1.0
def pay(rng, *shape):
    return sgn(rng, *shape) * (0.5 + 0.5 * rng.random(shape))
def weights(rng, *shape):
    return (0.25 + 0.75 * rng.random(shape)) * (rng.random(shape) > 0.0625)
def names(rng):
    o = np.argsort(rng.random((N, 8, TV, W)), axis=-1)[..., :2 * K]
    return o[..., :K].copy(), o[..., K:].copy()
def plain(rng):
    th = pay(rng, N, 8, 16, W); va = 0.875 * th + pay(rng, N, 8, 16, W)
    a, b = names(rng)
    return th, va, pay(rng, N, 8, 16, K), weights(rng, N, 8, 16, K), a, b
def put(x):
    x = np.where(np.abs(x) < 2.0 ** -20, 0.0, x)
    return np.ascontiguousarray(x.reshape(N, 128, -1)).astype(np.float32).astype(BF)
def near(x):
    return np.where(np.abs(x) < 2.0 ** -20, 0.0, x).astype(np.float32).astype(BF).astype(np.float64)
def pack(th, va, yt, wt, a, b):
    return {"th": put(th), "va": put(va), "yt": put(yt), "wt": put(wt), "an": np.stack([gtable(v.reshape(8, TV * K)) for v in a]),
            "bn": np.ascontiguousarray(b.reshape(N, 8 * TV, K)).astype(np.int32)}
def residues(rng, x, g):
    th, va, yt, wt, a, b = x; n = 2 * (K // TV); top = TV * (TV - 1) // 2
    fac = np.concatenate([np.arange(1, TV), np.array([-top])])
    m = rng.integers(128, 192, (16, n)); k = rng.integers(1, 63 // top + 1, (16, n)) * (2 * rng.integers(0, 2, (16, n)) - 1); s = sgn(rng, 16, n) * 2.0 ** -8
    col = np.stack([rng.permutation(W)[:2 * K].reshape(TV, n) for q in range(N)])
    wt[:, g] = 0.0
    for q in range(N):
        for i in range(TV):
            th[q, g][:, col[q, i]] = s * m; va[q, g][:, col[q, i]] = s * (m - fac[i] * k)
    for r in range(N):
        js = rng.permutation(K).reshape(TV, K // TV)
        for i in range(TV):
            sl = rng.permutation(n)
            for t in range(TV):
                v = col[(r + S * t) % N, (i + t) % TV][sl]
                a[r, g, t, js[i]] = v[:K // TV]; b[r, g, t, js[i]] = v[K // TV:]
def first(tab, va, yt, wt, a, b):
    fa = np.zeros((TV, N, 16, K)); fb = np.zeros((TV, N, 16, K)); keep = []; tab = tab.copy()
    for t in range(TV):
        own = (np.arange(N) - S * t) % N; i1 = a[own, t][:, None, :]; i2 = b[own, t][:, None, :]
        p1 = np.take_along_axis(tab, i1, 2); p2 = np.take_along_axis(tab, i2, 2)
        er = p1 * p2 - yt[own]; w8 = 0.125 * wt[own]
        np.put_along_axis(tab, i1, p1 - w8 * er * p2, 2); np.put_along_axis(tab, i2, p2 - w8 * er * p1, 2)
        fa[t][own] = 0.125 * er * p2; fb[t][own] = 0.125 * er * p1
        keep.append((own, i1, i2, w8, p1, p2, er))
    dd = tab - va; hh = np.zeros((N, 16, K))
    for t in range(TV - 1, -1, -1):
        own, i1, i2, w8, p1, p2, er = keep[t]
        d1 = np.take_along_axis(dd, i1, 2); d2 = np.take_along_axis(dd, i2, 2); mm = p1 * p2 + er
        hh[own] = hh[own] - fa[t][own] * d1 - fb[t][own] * d2
        np.put_along_axis(dd, i1, d1 - w8 * (p2 * p2 * d1 + mm * d2), 2); np.put_along_axis(dd, i2, d2 - w8 * (mm * d1 + p1 * p1 * d2), 2)
    return hh, fa, fb
def knots(rng, x, g):
    th, va, yt, wt, a, b = x; M = min(K // 3, (W - 2 * K) // (2 * (TV - 1))); n = 2 * M * (TV - 1)
    cols = np.stack([rng.permutation(W) for q in range(N)]); prv = cols[:, :n].reshape(N, TV - 1, 2, M)
    js = np.stack([rng.permutation(K) for q in range(N)])
    for q in range(N):
        th[q, g][:, prv[q, :, 0].reshape(-1)] = sgn(rng, 16, n // 2) * (0.75 + 0.25 * rng.random((16, n // 2)))
        th[q, g][:, prv[q, :, 1].reshape(-1)] = 0.0625 * pay(rng, 16, n // 2)
        va[q, g][:, cols[q, :n]] = 0.0
    for r in range(N):
        for t in range(TV):
            q = (r + S * t) % N; v = rng.permutation(cols[q, n:]); k = 0 if t == 0 else M; i = js[r, k:]
            a[r, g, t, i] = v[:K - k]; b[r, g, t, i] = v[K - k:2 * (K - k)]
            if t > 0:
                a[r, g, t, js[r, :M]] = prv[q, t - 1, 0]; b[r, g, t, js[r, :M]] = prv[q, t - 1, 1]
    for z in (th, va, yt, wt): z[:, g] = near(z[:, g])
    hh, fa, fb = first(th[:, g], va[:, g], yt[:, g], wt[:, g], a[:, g], b[:, g])
    for r in range(N):
        o = js[r, :M]; rest = hh[r][:, o]
        for f, side in ((fb, 1), (fa, 0)):
            for t in range(1, TV):
                q = (r + S * t) % N; cf = f[t, r][:, o]
                v = near(np.clip(np.divide(-rest, cf), -2.0, 2.0))
                va[q, g][:, prv[q, t - 1, side]] = v; rest = rest + cf * v
def links(rng):
    n = 2 ** 19; one = np.float32; c = one(0.125)
    w0 = near(0.75 + 0.25 * rng.random(n)).astype(one); w1 = near(0.5 + 0.5 * rng.random(n)).astype(one)
    y0 = near(1.5 + 0.5 * rng.random(n)).astype(one); p = near(1.5 + 0.5 * rng.random(n)).astype(one)
    u1 = c * (w0 * (y0 * p)); pr = u1 * p; p64 = pr.astype(np.float64)
    y1 = near(np.minimum(1.0 + p64 + np.minimum(p64, 1.0 - p64) * rng.random(n), 2.0)).astype(one)
    er = pr - y1; u2 = u1 - c * (w1 * (er * p)); p2 = p - c * (w1 * (er * u1)); m = pr + er; wrong = one(2) * er + y1
    k = 0.125 * w1.astype(np.float64); s = 1.0 - k * p.astype(np.float64) * p.astype(np.float64); km = k * np.where(m == 0, one(1), m).astype(np.float64)
    vu = near(np.clip(u2 - np.divide(km * p2, s), -2.0, 2.0)).astype(one); d1 = u2 - vu
    vv = near(np.clip(p2 - np.divide(d1 * s, km), -2.0, 2.0)).astype(one); d2 = p2 - vv
    x1 = d1 - c * (w1 * ((p * p) * d1 + m * d2)); x2 = d1 - c * (w1 * ((p * p) * d1 + wrong * d2))
    hit = np.flatnonzero((x1 > 0) & (x2 <= 0))
    if len(hit) == 0: hit = np.array([int(np.argmin(np.abs(x1)))])
    i = hit[rng.integers(0, len(hit), (N, CH, 16))]; s1 = sgn(rng, N, CH, 16); s2 = sgn(rng, N, CH, 16)
    return s1 * y0[i], w0[i], s1 * y1[i], w1[i], s2 * p[i], s1 * s2 * vu[i], s2 * vv[i]
def halves(rng, x, g):
    th, va, yt, wt, a, b = x; y0, w0, y1, w1, p, vu, vv = links(rng); n = K - 2 * CH
    cols = np.stack([rng.permutation(W) for q in range(N)]); js = np.stack([rng.permutation(K) for q in range(N)])
    for q in range(N):
        u = cols[q, :CH]; v = cols[q, CH:2 * CH]; z = cols[q, 2 * CH:6 * CH]; r = (q - S) % N; j0 = js[q, :CH]; j1 = js[r, CH:2 * CH]
        th[q, g][:, z] = 0.0; va[q, g][:, z] = 0.0
        th[q, g][:, u] = 0.0; va[q, g][:, u] = vu[q].T
        th[q, g][:, v] = p[q].T; va[q, g][:, v] = vv[q].T
        yt[q, g][:, j0] = y0[q].T; wt[q, g][:, j0] = w0[q].T
        yt[r, g][:, j1] = y1[q].T; wt[r, g][:, j1] = w1[q].T
    for r in range(N):
        for t in range(TV):
            q = (r + S * t) % N; z = rng.permutation(cols[q, 2 * CH:6 * CH]); v = rng.permutation(cols[q, 6 * CH:])
            a[r, g, t, js[r, 2 * CH:]] = v[:n]; b[r, g, t, js[r, 2 * CH:]] = v[n:2 * n]
            for i in range(2):
                j = js[r, i * CH:(i + 1) * CH]; o = z[2 * CH * i:2 * CH * (i + 1)]
                if t == i: o = cols[q, :2 * CH]
                a[r, g, t, j] = o[:CH]; b[r, g, t, j] = o[CH:]
def setup_inputs(rng):
    return pack(*plain(rng))
def sized(rng, n):
    return sgn(rng, N, 8, 16, n) * (0.8 + 0.2 * rng.random((N, 8, 16, n))) * rng.choice(np.array([0.625, 0.8, 1.0]), (N, 8, 1, n))
def setup_inputs_spread(rng):
    u = rng.random((N, 8, 1, W))
    th = sized(rng, W)
    th = np.where(u < 0.03, 2.0 ** -20 * sgn(rng, N, 8, 16, W), np.where(u > 0.98, 0.0, th))
    va = 0.875 * th + sized(rng, W)
    va = np.where((u > 0.5) & (u < 0.53), 0.0, va)
    yt = sized(rng, K)
    yt = np.where((rng.random((N, 8, 1, K)) < 0.04) | (rng.random((N, 8, 16, K)) < 0.04), 0.0, yt)
    a, b = names(rng)
    return pack(th, va, yt, weights(rng, N, 8, 16, K), a, b)
def setup_inputs_ends(rng):
    o = np.concatenate([np.arange(K), np.arange(W - K, W)])[np.argsort(rng.random((N, 8, TV, 2 * K)), axis=-1)]
    for r in range(N):
        for g in range(8):
            for t in range(TV):
                v = o[r, g, t]; i, n1, n2 = (0, 0, W - 1) if g % 2 == 0 else (K - 1, W - 1, 0)
                for place, num in ((i, n1), (K + i, n2)):
                    s = int(np.flatnonzero(v == num)[0]); old = int(v[place]); v[place] = num; v[s] = old
    for r in range(N):
        for g in range(8):
            i, n1, n2 = (0, 0, W - 1) if g % 2 == 0 else (K - 1, W - 1, 0)
            o[r, g, :, i] = n1; o[r, g, :, K + i] = n2
    a, b = o[..., :K].copy(), o[..., K:].copy()
    th = 2.0 * sgn(rng, N, 8, 16, W); same = np.array([0.7, 0.75, 0.8, 0.85, 0.7, 0.75, 0.8, 0.85]).reshape(1, 8, 1, 1)
    va = th * np.where(rng.random(th.shape) < same, 1.0, -1.0)
    yt = 2.0 * sgn(rng, N, 8, 16, K); wt = 1.0 * rng.integers(0, 2, (N, 8, 16, K))
    s7 = sgn(rng, 16, 1); s0 = sgn(rng, 16, 1)
    for x in (th, va):
        one = x[:, 7, :1].copy(); x[:, 7] = one * s7; x[:, 0] = one[..., ::-1] * s0
    for x in (yt, wt):
        one = x[:, 7, :1].copy(); x[:, 7] = one; x[:, 0] = one
    a[:, 0] = W - 1 - a[:, 7]; b[:, 0] = W - 1 - b[:, 7]
    return pack(th, va, yt, wt, a, b)
def setup_inputs_corners(rng):
    th = sgn(rng, N, 8, 16, W); yt = sgn(rng, N, 8, 16, K); wt = rng.choice(np.array([0.0, 2.0 ** -20, 0.0625]), (N, 8, 16, K))
    a, b = names(rng); kap = np.zeros((N, 8, W)); kap[:, :2] = 2.0
    for r in range(N):
        todo = [(4, rng.permutation(K)[:1 + r % 3], 2.0), (6, np.array([0, 1, K // 2, K - 2, K - 1]), 2.0)]
        if r % 2 == 1: todo.append((0, rng.integers(0, K, 1), 0.0))
        for g0, js, val in todo:
            for g in (g0, g0 + 1):
                for t in range(TV):
                    q = (r + S * t) % N
                    kap[q, g, a[r, g, t, js]] = val; kap[q, g, b[r, g, t, js]] = val
                if val > 0: yt[r, g][:, js] = -th[r, g][:, a[r, g, 0, js]] * th[r, g][:, b[r, g, 0, js]]
    return pack(th, kap[:, :, None, :] * th, yt, wt, a, b)
def setup_inputs_crowd(rng):
    th0 = pay(rng, N, 2, W); va0 = 0.875 * th0 + pay(rng, N, 2, W); y0 = pay(rng, N, 2, K); w0 = weights(rng, N, 2, K)
    nm = np.argsort(rng.random((N, TV, W)), axis=-1)[..., :2 * K]; order = np.argsort(rng.random((N, 8, W)), axis=-1)
    cls = np.stack([rng.permutation((np.arange(16) >= n).astype(np.int64)) for n in (16, 16, 15, 1, 16, 0, 1, 15)]); sg = sgn(rng, 8, 16, 1)
    th = np.zeros((N, 8, 16, W)); va = np.zeros((N, 8, 16, W)); o = np.zeros((N, 8, TV, 2 * K), np.int64)
    for q in range(N):
        for g in range(8):
            th[q, g][:, order[q, g]] = sg[g] * th0[q][cls[g]]; va[q, g][:, order[q, g]] = sg[g] * va0[q][cls[g]]
            for t in range(TV): o[q, g, t] = order[(q + S * t) % N, g][nm[q, t]]
    return pack(th, va, y0[:, cls], w0[:, cls], o[..., :K].copy(), o[..., K:].copy())
def setup_inputs_calm(rng):
    th, va, yt, wt, a, b = plain(rng)
    th[:, :4] = sgn(rng, N, 4, 16, W); u = rng.random((N, 4, 16, W))
    va[:, :4] = th[:, :4] * np.where(u < 0.25, 0.0, np.where(u < 0.55, 1.0, 2.0))
    yt[:, :4] = sgn(rng, N, 4, 16, K); wt[:, :4] = 0.0
    th[:, 2] *= 2.0 ** -20; va[:, 2] *= 2.0 ** -20; yt[:, 2] *= 2.0 ** -12
    u = rng.random((N, 16, K))
    wt[:, 6] = np.where(u < 0.25, 2.0 ** -20, np.where(u < 0.5, np.exp2(-20 + 9 * rng.random((N, 16, K))), wt[:, 6]))
    for g in (5, 7): residues(rng, (th, va, yt, wt, a, b), g)
    for g in (4, 6): knots(rng, (th, va, yt, wt, a, b), g)
    halves(rng, (th, va, yt, wt, a, b), 0)
    return pack(th, va, yt, wt, a, b)
def check_ranges(d):
    bad = []
    for k, lo, hi, least in (("th", -2.0, 2.0, 2.0 ** -20), ("va", -2.0, 2.0, 2.0 ** -20), ("yt", -2.0, 2.0, 2.0 ** -12), ("wt", 0.0, 1.0, 2.0 ** -20)):
        v = np.asarray(d[k]).astype(np.float64); s = np.abs(v)
        if not np.all((v >= lo) & (v <= hi) & ((s == 0) | (s >= least))): bad.append("range of " + k)
    for k in ("an", "bn"):
        if np.min(d[k]) < 0 or np.max(d[k]) > W - 1: bad.append("range of " + k)
    a = np.stack([gentries(v) for v in np.asarray(d["an"])]).reshape(N, 8, TV, K); b = np.asarray(d["bn"]).reshape(N, 8, TV, K)
    o = np.sort(np.concatenate([a, b], axis=-1), axis=-1)
    if np.any(o[..., 1:] == o[..., :-1]): bad.append("names of a visit (an and bn) repeat")
    if not bad and rounds(d["th"], d["va"], d["yt"], d["wt"], d["an"], d["bn"], True)[2]: bad.append("a product under 2 ** -126")
    return bad
def tiny(A, B, e, w, da, db):
    m = A * B + e; one = np.float32(1)
    pairs = ((A, B), (B, B), (A, A), (e, B), (e, A), (w, e * B), (w, e * A), (e * B, da), (e * A, db), (B * B, da), (m, db), (m, da), (A * A, db),
             (one, (e * B) * da + (e * A) * db), (w, (B * B) * da + m * db), (w, m * da + (A * A) * db))
    return any(bool(np.any((u != 0) & (v != 0) & (np.abs(u * v) < 2.0 ** -123))) for u, v in pairs)
def rounds(th, va, yt, wt, an, bn, watch):
    a = np.stack([gentries(v) for v in an]).astype(np.int64).reshape(N, 8, TV, K); b = bn.astype(np.int64).reshape(N, 8, TV, K); low = False
    for rnd in range(RO):
        ft = np.float32 if rnd < RO - 1 else np.float64
        c = ft(0.125); tab = th.astype(ft).reshape(N, 8, 16, W)
        y = yt.astype(ft).reshape(N, 8, 16, K); w = wt.astype(ft).reshape(N, 8, 16, K); kept = []
        for t in range(TV):
            own = (np.arange(N) - S * t) % N
            ia = a[own, :, t][:, :, None, :]; ib = b[own, :, t][:, :, None, :]; ww = w[own]
            A = np.take_along_axis(tab, ia, 3); B = np.take_along_axis(tab, ib, 3)
            e = A * B - y[own]
            np.put_along_axis(tab, ia, A - c * (ww * (e * B)), 3)
            np.put_along_axis(tab, ib, B - c * (ww * (e * A)), 3)
            kept.append((own, ia, ib, ww, A, B, e))
        d = tab - va.astype(ft).reshape(N, 8, 16, W); h = np.zeros((N, 8, 16, K), ft)
        for t in range(TV - 1, -1, -1):
            own, ia, ib, ww, A, B, e = kept[t]
            da = np.take_along_axis(d, ia, 3); db = np.take_along_axis(d, ib, 3)
            if watch and rnd < RO - 1: low = low or tiny(A, B, e, ww, da, db)
            h[own] = h[own] - c * ((e * B) * da + (e * A) * db)
            m = A * B + e
            np.put_along_axis(d, ia, da - c * (ww * ((B * B) * da + m * db)), 3)
            np.put_along_axis(d, ib, db - c * (ww * (m * da + (A * A) * db)), 3)
        if rnd < RO - 1:
            up = np.sum((h > 0).astype(np.int64), axis=2)
            refused = up + np.roll(up, -1, axis=1) >= QV
            for r in range(N):
                for g in range(8):
                    p = np.flatnonzero(refused[r, g])
                    if len(p) > 1: b[r, g][:, p] = b[r, g][:, np.roll(p, 1)]
    return d, h, low
def reference(th, va, yt, wt, an, bn):
    d, h, low = rounds(th, va, yt, wt, an, bn, False)
    return {"yd": d.reshape(N, 128, W).astype(np.float32), "yh": h.reshape(N, 128, K).astype(np.float32)}

def check_inputs(d):
    bad = list(check_ranges(d))
    if not bad:
        for name, y in reference(**d).items():
            for q in range(N):
                v = np.abs(np.asarray(y[q], np.float64)); s = np.sqrt(np.mean(v * v))
                if v.max() > 12 * s or s < 2.0 ** -4: bad.append('%s of rank %d is uneven or too small' % (name, q))
    return bad

@@ -1,0 +1,709 @@
+from concourse.bass import DstId, RemoteDMATransfer
+from concourse.mybir import AluOpType as ALU, ActivationFunctionType as AF
+
+K, W, NR = 384, 1536, 4
+K2 = 2 * K
+F32, BF, I32, U16 = "float32", "bfloat16", "int32", "uint16"
+POS0 = 64
+CEN, INI = 192, -448.0
+
+SCRATCH = {
+    "an32": ("sbuf", [128, 96], I32), "bn32": ("sbuf", [128, 6, 16], I32),
+    "x2": ("sbuf", [128, 6, 32], F32), "y2": ("sbuf", [128, 6, 32], F32), "z2": ("sbuf", [128, 6, 16], F32),
+    "nm": ("sbuf", [128, 4, 48], U16), "ntl": ("sbuf", [128, 4, 48], U16),
+    "thb": ("sbuf", [128, W], BF), "vab": ("sbuf", [128, W], BF),
+    "wraw": ("sbuf", [128, K], BF), "yw": ("sbuf", [128, 4 * K2], BF),
+    "fw": ("sbuf", [128, W + 3 * K2], F32), "bw": ("sbuf", [128, W + 7 * K2], F32),
+    "nv": ("sbuf", [128, 3 * K2], F32), "va3": ("sbuf", [128, 3 * K], F32),
+    "ab": ("sbuf", [128, 4 * K2 + K], F32), "pp": ("sbuf", [128, K], F32),
+    "cf": ("sbuf", [128, 9 * K], F32), "btmp": ("sbuf", [128, K], F32),
+    "dd": ("sbuf", [128, 2 * K2], F32), "xs": ("sbuf", [128, K2], F32),
+    "t12": ("sbuf", [128, 4 * K2], F32), "ul": ("sbuf", [128, 4 * K], F32),
+    "rt": ("sbuf", [128, W], F32), "cs": ("sbuf", [128, 3 * K2], F32),
+    "pr": ("sbuf", [128, 6 * K2], F32), "pb": ("sbuf", [128, 6 * K], F32),
+    "of1": ("sbuf", [128, 6 * 48], U16), "ofb": ("sbuf", [128, 12 * 24], U16), "fin": ("sbuf", [128, 96], U16),
+    "rs": ("sbuf", [128, 4 * 24], U16), "rl": ("sbuf", [128, 16 * 24], U16),
+    "sg": ("sbuf", [128, 400], BF), "ls": ("sbuf", [128, 400], BF), "nx": ("sbuf", [128, 400], BF), "gx": ("sbuf", [128, K], BF),
+    "sm": ("sbuf", [128, 2 * 24], F32), "sx": ("sbuf", [128, 2 * 24], BF), "lm": ("sbuf", [128, 8], F32),
+    "hout": ("sbuf", [128, K], F32),
+    "ip": ("sbuf", [128, 8], I32), "col": ("sbuf", [128, 8], F32),
+    "ones": ("sbuf", [128, 128], BF), "idb": ("sbuf", [128, 128], BF), "idf": ("sbuf", [128, 128], F32), "ni8": ("sbuf", [128, 128], F32),
+    "id2": ("sbuf", [128, 128], F32), "nib": ("sbuf", [128, 128], BF),
+    "e15": ("sbuf", [128, 144], F32), "ew": ("sbuf", [128, 144], F32), "e2": ("sbuf", [128, 144], F32), "ewd": ("sbuf", [128, 144], BF),
+    "bi": ("sbuf", [128, 128], I32), "be": ("sbuf", [128, 128], BF), "bo": ("sbuf", [128, 128], BF),
+    "d1i": ("sbuf", [128, 385], F32), "d1f": ("sbuf", [128, 385], F32), "d1r": ("sbuf", [128, 385], F32),
+    "cwi": ("sbuf", [128, 24], F32), "cw": ("sbuf", [128, 24], BF), "zb": ("sbuf", [128, 385], BF),
+}
+for _b in range(8):
+    SCRATCH["b%d" % _b] = ("psum", [128, 512], F32)
+
+SEMAPHORES = (["cv", "cs_", "cp", "cg", "loc", "lu1", "lu2", "lu3"] + ["d%d" % i for i in range(48)]
+              + ["nm%d" % t for t in (1, 2, 3)] + ["yw%d" % t for t in (1, 2, 3)]
+              + ["u%d_%d" % (r, t) for r in range(3) for t in (1, 2, 3)]
+              + ["r%d_%d_%d" % (r, k, t) for r in range(2) for k in range(2) for t in (1, 2, 3)])
+
+
+def bits(engines):
+    m = 0
+    for e in engines:
+        m |= 1 << e
+    return m
+
+
+def spread(topo, cores, q):
+    src = cores[q]
+    eng = {t: topo.engines(src, cores[(q - t) % NR]) for t in (1, 2, 3)}
+    common = [e for e in eng[1] if e in eng[2] and e in eng[3]]
+    wide = [t for t in (1, 2, 3) if len(eng[t]) >= 2 * len(common)]
+    calls = [[(t, common)] for t in (1, 2, 3) if t not in wide[:1]]
+    if wide:
+        calls[0].append((wide[0], [e for e in eng[wide[0]] if e not in common][:len(common)]))
+    return calls
+
+
+def rank_program(g, core, T, topo):
+    q = T.rank_of(core)
+    if q is None:
+        return
+    cores = list(T.cores)
+    Q = {"v": g.vector, "s": g.scalar, "p": g.tensor, "g": g, "y": g.sync}
+    CS = {"v": "cv", "s": "cs_", "p": "cp", "g": "cg"}
+    cnt = {}
+    seen = {e: {} for e in Q}
+    lastw, reads, bank = {}, {}, {}
+    nd = [0]
+
+    def need(e, toks):
+        best = {}
+        for s, v in toks:
+            best[s] = max(best.get(s, 0), v)
+        for s, v in best.items():
+            if seen[e].get(s, 0) < v:
+                Q[e].wait_ge(T.sem[s], v)
+                seen[e][s] = v
+
+    def deps(e, r, w):
+        toks = []
+        for k in r:
+            if k in lastw:
+                toks.append(lastw[k])
+        for k in w:
+            if k in lastw:
+                toks.append(lastw[k])
+            toks += reads.get(k, [])
+        for k in list(r) + list(w):
+            if k[0] == "#":
+                toks += [t for o, t in bank.get(k, {}).items() if o != e]
+        need(e, toks)
+
+    def done(e, tok, r, w):
+        for k in r:
+            reads.setdefault(k, []).append(tok)
+        for k in w:
+            lastw[k] = tok
+            reads[k] = []
+        for k in list(r) + list(w):
+            if k[0] == "#":
+                bank.setdefault(k, {})[e] = tok
+
+    def op(e, fn, r=(), w=()):
+        deps(e, r, w)
+        s = CS[e]
+        fn().then_inc(T.sem[s], 1)
+        cnt[s] = cnt.get(s, 0) + 1
+        done(e, (s, cnt[s]), r, w)
+
+    def dma(e, out, in_, r=(), w=(), **kw):
+        deps(e, r, w)
+        s = "d%d" % nd[0]
+        nd[0] += 1
+        Q[e].dma_start(out, in_, **kw).then_inc(T.sem[s], 16)
+        cnt[s] = 16
+        done(e, (s, 16), r, w)
+
+    def send(trs, r, lsem="loc"):
+        deps("g", r, ())
+        ts = []
+        for d, eng, sem, srcs, dst in trs:
+            rid, pid = topo.addr(cores[d], core)
+            kw = dict(dst_ids=[DstId(rid=rid, pnc=pid)], dma_engine_mask=bits(eng), remote_sem=T.sem[sem])
+            if len(srcs) == 1:
+                ts.append(RemoteDMATransfer(src=srcs[0], dst=dst, **kw))
+            else:
+                ts.append(RemoteDMATransfer(srcs=srcs, dsts=[dst], alu_op=1, **kw))
+            cnt[lsem] = cnt.get(lsem, 0) + len(eng)
+        g.remote_dma_fused(ts, local_sem=T.sem[lsem])
+        if lsem != "loc":
+            done("g", (lsem, cnt[lsem]), r, ())
+
+    def lands(key, sem, n):
+        cnt[sem] = n
+        lastw[key] = (sem, n)
+        reads[key] = []
+
+    def to_hosts(src_of, dst_of, sem_of, rkeys, key_of):
+        for call in spread(topo, cores, q):
+            send([((q - t) % NR, eng, sem_of(t), [src_of(t)], dst_of(t)) for t, eng in call], rkeys)
+        for t in (1, 2, 3):
+            n = [len(eng) for call in spread(topo, cores, (q + t) % NR) for tt, eng in call if tt == t][0]
+            lands(key_of(t), sem_of(t), n)
+
+    V, S, PE = g.vector, g.scalar, g.tensor
+    B = [T["b%d" % i] for i in range(8)]
+
+    def bk(i, n=K):
+        return B[i][:, 0:n]
+
+    def blk(t, i, n=K):
+        return t[:, i * K:i * K + n]
+
+    def tt(out, a, b, o, r, w):
+        op("v", lambda: V.tensor_tensor(out, a, b, o), r, w)
+
+    def ts(out, a, s1, o0, r, w, s2=None, o1=None):
+        if o1 is None:
+            op("v", lambda: V.tensor_scalar(out, a, s1, None, o0), r, w)
+        else:
+            op("v", lambda: V.tensor_scalar(out, a, s1, s2, o0, o1), r, w)
+
+    def cp(out, a, r, w):
+        op("v", lambda: V.tensor_copy(out, a), r, w)
+
+    def ms(ap, c, w):
+        op("v", lambda: V.memset(ap, c), (), w)
+
+    def act(out, a, f, r, w, **kw):
+        op("s", lambda: S.activation(out, a, f, **kw), r, w)
+
+    def gat(e, out, win, off, r, w, neg=False):
+        a = win.indirect(off)
+        if e == "s":
+            act(out, a, AF.Copy, r, w, **({"scale": -1.0} if neg else {}))
+        elif neg:
+            ts(out, a, -1.0, ALU.mult, r, w)
+        else:
+            cp(out, a, r, w)
+
+    def mm(items, r, w, first=True, last=True):
+        def f():
+            ins = None
+            for i, (o, l, x) in enumerate(items):
+                ins = PE.matmul(o, l, x, first and i == 0, last and i == len(items) - 1)
+            return ins
+        op("p", f, r, w)
+
+    def iota(out, pat, base, cm, w, fl=True):
+        if fl:
+            op("g", lambda: g.iota(out, pat, base, cm, allow_small_or_imprecise_dtypes=True), (), w)
+        else:
+            op("g", lambda: g.iota(out, pat, base, cm), (), w)
+
+    def names(t, lo=0, hi=48):
+        return (T.nm if t == 0 else T.ntl)[:, t, lo:hi]
+
+    def nk(t):
+        return "n%d" % t
+
+    ORDER = [0, 1, 2, 3, 2, 1, 0]
+    LBASE = [0, 0, 0, W, W + K2, W + 2 * K2]
+
+    def cs_make(k):
+        iota(T.cs[:, (k % 3) * K2:(k % 3 + 1) * K2], [[1, K2]], POS0 + W + K2 * k, 0, ["cs%d" % (k % 3)])
+
+    def scat(k):
+        t = ORDER[k]
+        act(T.rt[:, :].indirect(names(t)), T.cs[:, (k % 3) * K2:(k % 3 + 1) * K2], AF.Silu, ["cs%d" % (k % 3), nk(t), "rt"], ["rt"])
+
+    def lvisit(li):
+        return li + 1 if li < 3 else li - 3
+
+    def gptr(li):
+        t = lvisit(li)
+        gat("s", T.pr[:, li * K2:(li + 1) * K2], T.rt[:, :], names(t), ["rt", nk(t)], ["pr%d" % (2 * li), "pr%d" % (2 * li + 1)])
+
+    def wrap(b, src, c0, n, r):
+        mm([(bk(b, n // 16), T.ew[:, 15 - i:143 - i], src[:, c0 + i:c0 + n:16]) for i in range(16)], list(r) + ["ew"], ["#%d" % b])
+
+    def conv(out, b, c0, n, base, w):
+        ts(out, B[b][:, c0:c0 + n], 0.25 - POS0 - base, ALU.add, ["#%d" % b], w)
+
+    def wrap1(li, b=7):
+        wrap(b, T.pr, li * K2, K2, ["pr%d" % (2 * li), "pr%d" % (2 * li + 1)])
+
+    def offa(li):
+        return T.of1[:, li * 48:li * 48 + 24], "oa%d" % li
+
+    def offb(rnd, li):
+        if rnd == 0:
+            return T.of1[:, li * 48 + 24:li * 48 + 48], "ob0_%d" % li
+        c = ((rnd - 1) * 6 + li) * 24
+        return T.ofb[:, c:c + 24], "ob%d_%d" % (rnd, li)
+
+    def perm(rnd, k, t):
+        if t == 0:
+            c = ((rnd - 1) * 2 + k) * 24
+            return T.rs[:, c:c + 24], "rs%d_%d" % (rnd, k)
+        c = (((rnd - 1) * 2 + k) * 4 + t) * 24
+        return T.rl[:, c:c + 24], "rl%d_%d_%d" % (rnd, k, t)
+
+    def ptab(rnd, li):
+        if rnd == 0:
+            return T.pr, (2 * li + 1) * K, "pr%d" % (2 * li + 1)
+        if rnd == 1:
+            return T.pb, li * K, "pb%d" % li
+        return T.pr, li * K, "pr%d" % li
+
+    def pupd(rnd, li):
+        s, c, k = ptab(rnd - 1, li)
+        d, c2, k2 = ptab(rnd, li)
+        o, ko = perm(rnd, 0, lvisit(li))
+        gat("s", d[:, c2:c2 + K], s[:, c:c + K], o, [k, ko], [k2])
+
+    def wrapb(rnd, li, n, b):
+        d, c, k = ptab(rnd, li)
+        wrap(b, d, c, n * K, [ptab(rnd, li + i)[2] for i in range(n)])
+
+    def convb(rnd, li, n, b):
+        for i in range(n):
+            o, k = offb(rnd, li + i)
+            conv(o, b, 24 * i, 24, LBASE[li + i], [k])
+
+    def Aof(t):
+        return blk(T.ab, 2 * t), "A%d" % t
+
+    def Bof(rnd, t):
+        if t == 0 and rnd % 2 == 1:
+            return blk(T.ab, 8), "B0x"
+        return blk(T.ab, 2 * t + 1), "B%d" % t
+
+    def VBof(rnd):
+        return blk(T.va3, 1 + rnd % 2), "vb%d" % (rnd % 2)
+
+    def ywof(t):
+        return blk(T.yw, 2 * t), blk(T.yw, 2 * t + 1), "yw%d" % t
+
+    def loadyw(t):
+        y, w, k = ywof(t)
+        mm([(bk(0), T.idb[:, :], y)], [k, "idb"], ["#0"])
+        if t < 3:
+            mm([(bk(2), T.idb[:, :], w)], [k, "idb"], ["#2"])
+
+    def fwin(t):
+        return T.fw[:, 0:W + K2 * t], ["fth"] + ["o%s%d" % (s, i) for i in range(t) for s in "ab"]
+
+    def dpos(t):
+        return W + K2 * (6 - t)
+
+    def bwin(t):
+        return T.bw[:, W + K2 * t:dpos(t)], ["di%d" % i for i in range(t, 3)] + ["do%s%d" % (s, i) for i in range(t + 1, 4) for s in "ab"]
+
+    def prefill(t):
+        dma("y", T.bw[:, W + K2 * t:W + K2 * (t + 1)], T.nv[:, K2 * t:K2 * (t + 1)], ["nv%d" % t], ["di%d" % t])
+
+    def accum(t):
+        dma("g", T.bw[:, W + K2 * t:W + K2 * (t + 1)], T.fw[:, W + K2 * t:W + K2 * (t + 1)], ["oa%d" % t, "ob%d" % t],
+            ["di%d" % t], accum_op=ALU.add)
+
+    def fgather(rnd, t, e):
+        win, wk = fwin(t)
+        (a, ka), (b, kb) = Aof(t), Bof(rnd, t)
+        ob, kob = offb(rnd, t - 1)
+        oa, koa = offa(t - 1)
+        gat(e, b, win, ob, wk + [kob], [kb])
+        gat(e, a, win, oa, wk + ["L" + koa], [ka])
+
+    def mreal(t):
+        y, w, kw = ywof(t)
+        mm([(bk(2), T.id2[:, :], T.pp[:, :]), (bk(2), T.nib[:, :], y)], ["id2", "nib", "pp", kw], ["#2"])
+
+    def fwd(rnd, t, pin, pr, mid=None, tail=None):
+        (a, ka), (b, kb) = Aof(t), Bof(rnd, t)
+        y, w, kw = ywof(t)
+        P = T.pp[:, :]
+        tt(P, pin[0], pin[1], ALU.mult, pr, ["pp"])
+        tt(bk(1), P, bk(0), ALU.subtract, ["pp", "#0"], ["#1"])
+        mid = mid or [None] * 3
+        if t == 3:
+            tt(bk(4), bk(1), a, ALU.mult, ["#1", ka], ["#4"])
+            tt(bk(3), bk(1), b, ALU.mult, ["#1", kb], ["#3"])
+            act(bk(0), b, AF.Square, [kb], ["#0"])
+            if rnd == 2:
+                mreal(t)
+            else:
+                tt(bk(2), bk(1), P, ALU.add, ["#1", "pp"], ["#2"])
+            act(bk(1), a, AF.Square, [ka], ["#1"])
+            tt(bk(6), bk(4), w, ALU.mult, ["#4", kw], ["#6"])
+            tt(bk(5), bk(3), w, ALU.mult, ["#3", kw], ["#5"])
+            if rnd == 2:
+                tt(bk(0), bk(0), w, ALU.mult, ["#0", kw], ["#0"])
+                act(bk(0), bk(0), AF.Identity, ["#0"], ["#0"], scale=-1.0, bias=1.0)
+            tt(bk(6), b, bk(6), ALU.subtract, ["#6", kb], ["#6"])
+            if rnd == 2:
+                tt(bk(1), bk(1), w, ALU.mult, ["#1", kw], ["#1"])
+                act(bk(1), bk(1), AF.Identity, ["#1"], ["#1"], scale=-1.0, bias=1.0)
+            tt(bk(5), a, bk(5), ALU.subtract, ["#5", ka], ["#5"])
+            if rnd == 2:
+                tt(bk(2), bk(2), w, ALU.mult, ["#2", kw], ["#2"])
+            vb, kvb = VBof(rnd)
+            tt(blk(T.dd, 3), bk(6), vb, ALU.subtract, ["#6", kvb], ["db1"])
+            tt(blk(T.dd, 2), bk(5), blk(T.va3, 0), ALU.subtract, ["#5", "va"], ["da1"])
+            return
+        eb, ea = blk(T.cf, 3 * t + 1), blk(T.cf, 3 * t + 2)
+        tt(ea, bk(1), a, ALU.mult, ["#1", ka], ["ea%d" % t])
+        tt(eb, bk(1), b, ALU.mult, ["#1", kb], ["eb%d" % t])
+        if rnd > 0:
+            need("y", [lastw["eb%d" % t]])
+            prefill(t)
+        if mid[0]:
+            mid[0]()
+        tt(bk(6), ea, bk(2), ALU.mult, ["#2", "ea%d" % t], ["#6"])
+        if mid[1]:
+            mid[1]()
+        tt(bk(5), eb, bk(2), ALU.mult, ["#2", "eb%d" % t], ["#5"])
+        if mid[2]:
+            mid[2]()
+        c = W + K2 * t
+        if rnd == 2:
+            mreal(t)
+            act(bk(4), a, AF.Square, [ka], ["#4"])
+            act(bk(3), b, AF.Square, [kb], ["#3"])
+        if rnd == 0:
+            tt(T.fw[:, c + K:c + K2], b, bk(6), ALU.subtract, ["#6", kb], ["ob%d" % t])
+        else:
+            tt(T.btmp[:, :], b, bk(6), ALU.subtract, ["#6", kb], ["btmp"])
+            o, ko = perm(rnd, 1, t)
+            gat("s", T.fw[:, c + K:c + K2], T.btmp[:, :], o, ["btmp", ko], ["ob%d" % t])
+        tt(T.fw[:, c:c + K], a, bk(5), ALU.subtract, ["#5", ka], ["oa%d" % t])
+        if tail:
+            tail()
+        if rnd == 2:
+            tt(a, bk(4), w, ALU.mult, ["#4", kw], [ka])
+            tt(b, bk(3), w, ALU.mult, ["#3", kw], [kb])
+            tt(blk(T.cf, 3 * t), bk(2), w, ALU.mult, ["#2", kw], ["m%d" % t])
+        elif t > 0:
+            tt(blk(T.cf, 3 * t), bk(1), P, ALU.add, ["#1", "pp"], ["m%d" % t])
+
+    def fvisit(rnd, t, e, tail=None):
+        fgather(rnd, t, e)
+        win, wk = fwin(t)
+        oa, koa = offa(t - 1)
+        b, kb = Bof(rnd, t)
+        fwd(rnd, t, (win.indirect(oa), b), wk + ["L" + koa, kb], tail=tail)
+
+    def bgather(rnd, t):
+        win, wk = bwin(t)
+        p = t % 2
+        oa, koa = offa(3 + t)
+        ob, kob = offb(rnd, 3 + t)
+        gat("s", blk(T.dd, 2 * p), win, oa, wk + ["L" + koa], ["da%d" % p])
+        if t > 0 or rnd == 2:
+            gat("s", blk(T.dd, 2 * p + 1), win, ob, wk + [kob], ["db%d" % p])
+
+    def uprod(rnd, t):
+        p = t % 2
+        tt(blk(T.t12, 2 * t), bk(3), blk(T.dd, 2 * p), ALU.mult, ["#3", "da%d" % p], ["t1_%d" % t])
+        tt(blk(T.t12, 2 * t + 1), bk(4), blk(T.dd, 2 * p + 1), ALU.mult, ["#4", "db%d" % p], ["t2_%d" % t])
+        if t > 0:
+            d = (q + t) % NR
+            send([(d, topo.engines(core, cores[d]), "u%d_%d" % (rnd, t), [blk(T.t12, 2 * t), blk(T.t12, 2 * t + 1)], blk(T.ul, t))],
+                 ["t1_%d" % t, "t2_%d" % t], "lu%d" % t)
+            lands("ul%d" % t, "u%d_%d" % (rnd, t), len(topo.engines(cores[(q - t) % NR], core)))
+            m_, km = (T.ni8, "ni8") if rnd == 2 and t < 3 else (T.idf, "idf")
+            mm([(bk(3), m_[:, :], blk(T.cf, 3 * (t - 1) + 1))], [km, "eb%d" % (t - 1)], ["#3"])
+            if t > 1 or rnd == 2:
+                mm([(bk(4), m_[:, :], blk(T.cf, 3 * (t - 1) + 2))], [km, "ea%d" % (t - 1)], ["#4"])
+
+    def bwd(rnd, t, early=None, sfill=None, tail=None):
+        p = t % 2
+        da, db, ka, kb = blk(T.dd, 2 * p), blk(T.dd, 2 * p + 1), "da%d" % p, "db%d" % p
+        y, w, kw = ywof(t)
+        more = t > 1 or (t == 1 and rnd == 2)
+        tt(bk(5), bk(0), da, ALU.mult, ["#0", ka], ["#5"])
+        tt(blk(T.xs, 1), bk(2), da, ALU.mult, ["#2", ka], ["xs1"])
+        tt(bk(6), bk(1), db, ALU.mult, ["#1", kb], ["#6"])
+        tt(blk(T.xs, 0), bk(2), db, ALU.mult, ["#2", kb], ["xs0"])
+        if more:
+            mm([(bk(2), T.idf[:, :], blk(T.cf, 3 * (t - 1)))], ["idf", "m%d" % (t - 1)], ["#2"])
+        if early:
+            early()
+        if sfill:
+            sfill()
+        if more:
+            (a, kaa), (b, kbb) = Aof(t - 1), Bof(rnd, t - 1)
+            if rnd == 2:
+                act(bk(0), b, AF.Identity, [kbb], ["#0"], scale=-1.0, bias=1.0)
+                act(bk(1), a, AF.Identity, [kaa], ["#1"], scale=-1.0, bias=1.0)
+            else:
+                act(bk(0), b, AF.Square, [kbb], ["#0"])
+                act(bk(1), a, AF.Square, [kaa], ["#1"])
+        c = dpos(t)
+        if rnd == 2:
+            tt(T.btmp[:, :], bk(6), blk(T.xs, 1), ALU.subtract, ["#6", "xs1"], ["btmp"])
+            o, ko = perm(rnd, 1, t)
+            gat("s", T.bw[:, c + K:c + K2], T.btmp[:, :], o, ["btmp", ko], ["dob%d" % t])
+            tt(T.bw[:, c:c + K], bk(5), blk(T.xs, 0), ALU.subtract, ["#5", "xs0"], ["doa%d" % t])
+            return
+        tt(bk(6), bk(6), blk(T.xs, 1), ALU.add, ["#6", "xs1"], ["#6"])
+        tt(bk(5), bk(5), blk(T.xs, 0), ALU.add, ["#5", "xs0"], ["#5"])
+        tt(bk(6), bk(6), w, ALU.mult, ["#6", kw], ["#6"])
+        tt(bk(5), bk(5), w, ALU.mult, ["#5", kw], ["#5"])
+        if rnd == 0:
+            tt(T.bw[:, c + K:c + K2], db, bk(6), ALU.subtract, ["#6", kb], ["dob%d" % t])
+        else:
+            tt(T.btmp[:, :], db, bk(6), ALU.subtract, ["#6", kb], ["btmp"])
+            o, ko = perm(rnd, 1, t)
+            gat("s", T.bw[:, c + K:c + K2], T.btmp[:, :], o, ["btmp", ko], ["dob%d" % t])
+        tt(T.bw[:, c:c + K], da, bk(5), ALU.subtract, ["#5", ka], ["doa%d" % t])
+        if tail:
+            tail()
+
+    def wrapd(b, src, c0, cen, r):
+        mm([(bk(b, 24), T.idb[:, :], cen)] + [(bk(b, 24), T.ewd[:, 15 - i:143 - i], src[:, c0 + i:c0 + K:16]) for i in range(16)],
+           list(r) + ["idb", "ewd"], ["#%d" % b])
+
+    def fix(rnd, k, b):
+        t_, x_ = T.sm[:, 24 * k:24 * k + 24], T.sx[:, 24 * k:24 * k + 24]
+        o, ko = perm(rnd, k, 0)
+        return [lambda: ts(t_, bk(b, 24), INI if k == 0 else -INI, ALU.is_equal, ["#%d" % b, "lm%d" % k], ["sm%d" % k], T.lm[:, 4 * k:4 * k + 1], ALU.mult),
+                lambda: tt(x_, bk(b, 24), t_, ALU.add, ["#%d" % b, "sm%d" % k], ["sx%d" % k]),
+                lambda: ts(o, x_, float(CEN), ALU.add, ["sx%d" % k], [ko])]
+
+    def sendperm(rnd, k):
+        o, ko = perm(rnd, k, 0)
+        to_hosts(lambda t: o, lambda t: perm(rnd, k, t)[0], lambda t: "r%d_%d_%d" % (rnd - 1, k, t), [ko], lambda t: perm(rnd, k, t)[1])
+
+    def vote(rnd):
+        win, wk = bwin(0)
+        ob, kob = offb(rnd, 3)
+        mm([(bk(1, 385), T.idb[:, :], T.zb[:, :])], ["idb", "zb"], ["#1"], last=False)
+        loadyw(0)
+        bgather(rnd, 0)
+        t2 = blk(T.t12, 1)
+        tt(t2, win.indirect(ob), blk(T.cf, 2), ALU.mult, wk + [kob, "ea0"], ["t2_0"])
+        tt(bk(5), bk(3), blk(T.dd, 0), ALU.mult, ["#3", "da0"], ["#5"])
+        u0 = blk(T.t12, 0)
+        tt(u0, bk(5), t2, ALU.add, ["#5", "t2_0"], ["t1_0"])
+        tt(bk(4), bk(4), blk(T.ul, 1), ALU.subtract, ["#4", "ul1"], ["#4"])
+        tt(T.sg[:, 1:385], u0, bk(4), ALU.is_lt, ["#4", "t1_0"], ["sg"])
+        mm([(bk(1, 385), T.be[:, :], T.sg[:, 1:386]), (bk(1, 385), T.bo[:, :], T.sg[:, 0:385])], ["be", "bo", "sg"], ["#1"], first=False)
+        op("v", lambda: V.tensor_tensor_scan(T.ls[:, 0:385], bk(1, 385), T.d1f[:, :], INI, ALU.max, ALU.min), ["#1", "d1f"], ["ls"])
+        wrapd(7, T.ls, 0, T.cw[:, :], ["ls", "cw"])
+        op("v", lambda: V.tensor_tensor_scan(T.nx[:, 399:14:-1], B[1][:, 384::-1], T.d1r[:, ::-1], INI, ALU.max, ALU.min), ["#1", "d1r"], ["nx"])
+        ts(T.lm[:, 0:1], T.ls[:, 384:385], -INI, ALU.add, ["ls"], ["lm0"])
+        f = fix(rnd + 1, 0, 7)
+        f[0]()
+        ts(T.lm[:, 4:5], T.nx[:, 15:16], -INI, ALU.add, ["nx"], ["lm1"], -1.0, ALU.mult)
+        f[1]()
+        f[2]()
+        sendperm(rnd + 1, 0)
+
+    def backward(rnd, fills):
+        def nh():
+            uprod(rnd, 1)
+            act(bk(4), blk(T.ul, 3), AF.Copy, ["ul3"], ["#4"], scale=-1.0)
+        for t in (3, 2, 1):
+            if t < 3:
+                bgather(rnd, t)
+            sf, tl = fills.get(t, (None, None))
+            if t == 1 and rnd < 2:
+                bwd(rnd, t, early=nh, sfill=sf, tail=tl)
+                tt(bk(4), bk(4), blk(T.ul, 2), ALU.subtract, ["#4", "ul2"], ["#4"])
+            else:
+                bwd(rnd, t, sfill=sf, tail=tl)
+                uprod(rnd, t)
+                if (t, "after") in fills:
+                    fills[(t, "after")]()
+
+    def conv1_(li, b=7):
+        conv(T.of1[:, li * 48:li * 48 + 48], b, 0, 48, LBASE[li], ["Loa%d" % li, "ob0_%d" % li])
+
+    dma("s", T.an32[:, :], T.an[:, :], (), ["an32"])
+    dma("y", T.bn32[:, :, :], T.bn[:, :], (), ["bn32"])
+    dma("y", T.thb[:, :], T.th[:, :], (), ["thb"])
+    dma("y", T.wraw[:, :], T.wt[:, :], (), ["wraw"])
+    dma("y", blk(T.yw, 0), T.yt[:, :], (), ["y0"])
+    dma("y", T.vab[:, :], T.va[:, :], (), ["vab"])
+    iota(T.ip[:, 0:1], [[0, 1]], 0, 1, ["ip"], fl=False)
+    iota(T.rt[:, 0:K2], [[1, K2]], POS0, 0, ["rt0"])
+    ms(T.ones[:, :], 1.0, ["ones"])
+    ms(T.e15[:, :], 0.0, ["e15"])
+    op("g", lambda: g.affine_select(T.idb[:, :], T.ones[:, :], [[-1, 128]], ALU.is_equal, 0.0, 0, 1), ["ones"], ["idb"])
+    ts(T.ip[:, 1:2], T.ip[:, 0:1], 4, ALU.logical_shift_right, ["ip"], ["ip1"], 1, ALU.bitwise_and)
+    ts(T.ip[:, 2:3], T.ip[:, 0:1], 1, ALU.bitwise_and, ["ip"], ["ip2"])
+    ts(T.ip[:, 3:4], T.ip[:, 0:1], 15, ALU.bitwise_and, ["ip"], ["ip3"])
+    ms(T.e15[:, 15::16], 1.0, ["e15"])
+    op("g", lambda: g.affine_select(T.ew[:, :], T.e15[:, :], [[1, 144]], ALU.is_equal, 0.0, -15, -1), ["e15"], ["ew"])
+    cp(T.col[:, 1:4], T.ip[:, 1:4], ["ip1", "ip2", "ip3"], ["col"])
+    ms(T.zb[:, :], -33792.0, ["zb"])
+    ts(T.col[:, 0:1], T.col[:, 1:2], -1.0, ALU.mult, ["col"], ["col0"], 1.0, ALU.add)
+    ms(T.sg[:, :], 0.0, ["sg"])
+    act(T.rt[:, K2:W], T.rt[:, 0:K2], AF.Silu, ["rt0"], ["rt"], bias=float(K2))
+    act(T.cs[:, 0:K2], T.rt[:, 0:K2], AF.Identity, ["rt0"], ["cs0"], bias=float(W))
+    ts(T.x2[:, :, 0:16], T.bn32[:, :, :], T.col[:, 0:1], ALU.mult, ["bn32", "col0"], ["x2a"])
+    ts(T.x2[:, :, 16:32], T.bn32[:, :, :], T.col[:, 1:2], ALU.mult, ["bn32", "col"], ["x2b"])
+    cp(T.nm[:, :, 0:24], T.an32[:, :], ["an32"], ["nma"])
+    op("v", lambda: V.transpose(T.y2[:, :, :], T.x2[:, :, :]), ["x2a", "x2b"], ["y2"])
+    tt(T.z2[:, :, :], T.y2[:, :, 0:16], T.y2[:, :, 16:32], ALU.add, ["y2"], ["z2"])
+    for c in range(6):
+        cp(T.nm[:, :, 24 + c:48:6], T.z2[:, c, :], ["z2"] + (["nma"] if c == 5 else []), ["n0"] if c == 5 else ["nmb%d" % c])
+    to_hosts(lambda t: T.nm[:, t, :], lambda t: T.ntl[:, t, :], lambda t: "nm%d" % t, ["n0"], nk)
+    scat(0)
+    act(T.cs[:, K2:2 * K2], T.cs[:, 0:K2], AF.Identity, ["cs0"], ["cs1"], bias=float(K2))
+    ts(blk(T.yw, 1), T.wraw[:, :], 0.125, ALU.mult, ["wraw", "y0"], ["yw0"])
+    dma("g", T.fw[:, 0:W], T.th[:, :], (), ["fth"])
+    to_hosts(lambda t: T.yw[:, 0:K2], lambda t: T.yw[:, t * K2:(t + 1) * K2], lambda t: "yw%d" % t, ["yw0"], lambda t: "yw%d" % t)
+    cs_make(2)
+    op("g", lambda: g.affine_select(T.e2[:, :], T.e15[:, :], [[1, 144]], ALU.is_equal, 0.0, -14, -1), ["e15"], ["e2"])
+    iota(T.bi[:, :], [[-16, 8], [0, 16]], 128, 1, ["bi"], fl=False)
+    iota(T.d1i[:, :], [[1, 385]], -CEN, 0, ["d1i"])
+    iota(T.cwi[:, :], [[16, 24]], -CEN, 0, ["cwi"])
+
+    loadyw(0)
+    gptr(0)
+    gat("v", Bof(0, 0)[0], T.thb[:, :], names(0, 24, 48), ["thb", "n0"], ["B0"])
+    gat("v", Aof(0)[0], T.thb[:, :], names(0, 0, 24), ["thb", "n0"], ["A0"])
+    fwd(0, 0, (T.thb[:, :].indirect(names(0, 0, 24)), Bof(0, 0)[0]), ["thb", "n0", "B0"])
+    scat(1)
+    gptr(1)
+    wrap1(0)
+    loadyw(1)
+    for t in range(3):
+        gat("v", T.nv[:, K2 * t:K2 * (t + 1)], T.vab[:, :], names(t), ["vab", nk(t)], ["nv%d" % t], neg=True)
+        prefill(t)
+    accum(0)
+    cs_make(3)
+    conv1_(0)
+    wrap1(1, 4)
+    scat(2)
+    gptr(2)
+    fvisit(0, 1, "v", tail=lambda: conv1_(1, 4))
+    accum(1)
+    cs_make(4)
+    cs_make(5)
+    loadyw(2)
+    wrap1(2)
+    scat(3)
+    gptr(5)
+
+    def consts():
+        conv1_(2)
+        ts(T.bi[:, :], T.bi[:, :], 127, ALU.bitwise_and, ["bi"], ["bi"])
+        cp(T.idf[:, :], T.idb[:, :], ["idb"], ["idf"])
+        ts(T.be[:, :], T.bi[:, :], 32.0, ALU.is_lt, ["bi"], ["be"], 2048.0, ALU.mult)
+        ts(T.bo[:, :], T.bi[:, :], 32.0, ALU.is_lt, ["bi"], ["bo"], 2048.0, ALU.mult)
+        tt(T.ewd[:, :], T.e2[:, :], T.ew[:, :], ALU.subtract, ["e2", "ew"], ["ewd"])
+        ms(T.be[:, 1::2], 0.0, ["be"])
+        ms(T.bo[:, 0::2], 0.0, ["bo"])
+        ts(T.cw[:, :], T.cwi[:, :], T.col[:, 3:4], ALU.add, ["cwi", "col"], ["cw"])
+    fvisit(0, 2, "v", tail=consts)
+    accum(2)
+    cs_make(6)
+    loadyw(3)
+    wrap1(5)
+    fgather(0, 3, "s")
+    gat("s", T.va3[:, 0:K2], T.vab[:, :], names(3), ["vab", "n3"], ["va", "vb0"])
+    ts(T.d1f[:, :], T.d1i[:, :], T.col[:, 2:3], ALU.subtract, ["d1i", "col"], ["d1f"])
+    fwd(0, 3, (fwin(3)[0].indirect(offa(2)[0]), Bof(0, 3)[0]), fwin(3)[1] + ["Loa2", "B3"])
+    conv1_(5)
+
+    def s3():
+        scat(4)
+        gptr(4)
+        wrap1(4)
+
+    def s2():
+        scat(5)
+        gptr(3)
+
+    def v3():
+        ts(T.d1r[:, :], T.d1i[:, :], T.col[:, 2:3], ALU.subtract, ["d1i", "col"], ["d1r"], -1.0, ALU.mult)
+
+    def v2():
+        conv1_(4)
+    backward(0, {3: (s3, v3), 2: (s2, v2), (2, "after"): lambda: wrap1(3), 1: (None, lambda: conv1_(3))})
+    vote(0)
+
+    for rnd in (1, 2):
+        rho, krho = perm(rnd, 0, 0)
+        (bo_, kbo), (bn_, kbn) = Bof(rnd - 1, 0), Bof(rnd, 0)
+        gat("s", bn_, bo_, rho, [kbo, krho], [kbn])
+        if rnd == 1:
+            wrapd(3, T.nx, 16, T.cw[:, :], ["nx", "cw"])
+        else:
+            o, ko = perm(1, 1, 0)
+            gat("s", T.gx[:, :], T.nx[:, 16:400], o, ["nx", ko], ["gx"])
+            wrapd(3, T.gx, 0, T.sx[:, 24:48], ["gx", "sx1"])
+        f = fix(rnd, 1, 3)
+
+        def last_fix(f=f, rnd=rnd):
+            f[2]()
+            sendperm(rnd, 1)
+        fwd(rnd, 0, (bo_.indirect(rho), Aof(0)[0]), [kbo, krho, "A0"], mid=[f[0], f[1], last_fix])
+        accum(0)
+        if rnd == 2:
+            dma("g", T.bw[:, 0:W], T.thb[:, :], ["thb"], ["dbase"], accum_op=ALU.add)
+        loadyw(1)
+        win, wk = fwin(1)
+        rho1, krho1 = perm(rnd, 0, 1)
+        gat("v" if rnd == 1 else "s", Aof(1)[0], win, offa(0)[0], wk + ["Loa0"], ["A1"])
+        gat("s", blk(T.xs, 0), win, offb(rnd - 1, 0)[0], wk + [offb(rnd - 1, 0)[1]], ["xs0"])
+        gat("s", Bof(rnd, 1)[0], blk(T.xs, 0), rho1, ["xs0", krho1], ["B1"])
+        pupd(rnd, 1)
+        wrapb(rnd, 1, 1, 7)
+        pupd(rnd, 2)
+        if rnd == 1:
+            pupd(rnd, 3)
+        fwd(rnd, 1, (blk(T.xs, 0).indirect(rho1), Aof(1)[0]), ["xs0", krho1, "A1"], tail=lambda: convb(rnd, 1, 1, 7))
+        accum(1)
+        loadyw(2)
+        wrapb(rnd, 2, 1, 7)
+        fgather(rnd, 2, "s")
+        if rnd == 2:
+            pupd(rnd, 3)
+        pupd(rnd, 4)
+        if rnd == 1:
+            pupd(rnd, 5)
+        fwd(rnd, 2, (fwin(2)[0].indirect(offa(1)[0]), Bof(rnd, 2)[0]), fwin(2)[1] + ["Loa1", "B2"], tail=lambda: convb(rnd, 2, 1, 7))
+        accum(2)
+        loadyw(3)
+        fgather(rnd, 3, "s")
+        if rnd == 2:
+            pupd(rnd, 5)
+        wrapb(rnd, 3, 3, 7)
+        o, ko = perm(rnd, 0, 3)
+        gat("s", VBof(rnd)[0], VBof(rnd - 1)[0], o, [VBof(rnd - 1)[1], ko], [VBof(rnd)[1]])
+        fwd(rnd, 3, (fwin(3)[0].indirect(offa(2)[0]), Bof(rnd, 3)[0]), fwin(3)[1] + ["Loa2", "B3"])
+        convb(rnd, 3, 3, 7)
+        if rnd == 1:
+            def f3():
+                scat(6)
+
+            def f2():
+                act(T.bw[:, 0:W], T.vab[:, :], AF.Copy, ["vab"], ["dbase"], scale=-1.0)
+
+                pupd(1, 0)
+
+            def g2():
+                conv(T.fin[:, :], 7, 0, 96, 0, ["fin"])
+                ts(T.ni8[:, :], T.idf[:, :], -0.125, ALU.mult, ["idf"], ["ni8"])
+                ts(T.id2[:, :], T.idf[:, :], 2.0, ALU.mult, ["idf"], ["id2"])
+                ts(T.nib[:, :], T.idb[:, :], -1.0, ALU.mult, ["idb"], ["nib"])
+            backward(rnd, {3: (f3, None), (3, "after"): lambda: wrap(7, T.rt, 0, W, ["rt"]), 2: (f2, g2), (2, "after"): lambda: wrapb(1, 0, 1, 7), 1: (None, lambda: convb(1, 0, 1, 7))})
+            vote(rnd)
+        else:
+            backward(rnd, {})
+
+    bgather(2, 0)
+    mm([(bk(7), T.ni8[:, :], blk(T.ul, t)) for t in (3, 2)], ["ni8", "ul3", "ul2"], ["#7"])
+    bwd(2, 0)
+    uprod(2, 0)
+    tt(bk(7), bk(7), blk(T.t12, 0), ALU.add, ["#7", "t1_0"], ["#7"])
+    tt(bk(7), bk(7), blk(T.t12, 1), ALU.add, ["#7", "t2_0"], ["#7"])
+    wk = ["dbase"] + ["di%d" % i for i in range(3)] + ["do%s%d" % (s, i) for i in range(4) for s in "ab"] + ["fin"]
+    for e, lo, hi in (("s", 0, 640), ("v", 1280, W), ("s", 640, 1280)):
+        gat(e, T.fw[:, lo:hi], T.bw[:, :], T.fin[:, lo // 16:hi // 16], wk, ["out%d" % lo] + (["fth"] if lo == 0 else []))
+        dma("y", T.yd[:, lo:hi], T.fw[:, lo:hi], ["out%d" % lo], ())
+    tt(T.hout[:, :], bk(7), blk(T.ul, 1), ALU.add, ["#7", "ul1"], ["hout"])
+    dma("y", T.yh[:, :], T.hout[:, :], ["hout"], ())
+    rest = [(s, v) for s, v in cnt.items() if max(seen[e].get(s, 0) for e in seen) < v]
+    need("y", rest)

@@ -2,30 +2,30 @@ from concourse.bass import DstId, RemoteDMATransfer
 from concourse.mybir import AluOpType as ALU, ActivationFunctionType as AF
 
 K, W, NR = 384, 1536, 4
-K2 = 2 * K
+K2, K3, K4, H = 2 * K, 3 * K, 4 * K, K // 2
 F32, BF, I32, U16 = "float32", "bfloat16", "int32", "uint16"
 POS0 = 64
 CEN, INI = 192, -448.0
+PE_E = True
 
 SCRATCH = {
     "an32": ("sbuf", [128, 96], I32), "bn32": ("sbuf", [128, 6, 16], I32),
     "x2": ("sbuf", [128, 6, 32], F32), "y2": ("sbuf", [128, 6, 32], F32), "z2": ("sbuf", [128, 6, 16], F32),
     "nm": ("sbuf", [128, 4, 48], U16), "ntl": ("sbuf", [128, 4, 48], U16),
     "thb": ("sbuf", [128, W], BF), "vab": ("sbuf", [128, W], BF),
-    "wraw": ("sbuf", [128, K], BF), "yw": ("sbuf", [128, 4 * K2], BF),
-    "fw": ("sbuf", [128, W + 3 * K2], F32), "bw": ("sbuf", [128, W + 7 * K2], F32),
-    "nv": ("sbuf", [128, 3 * K2], F32), "va3": ("sbuf", [128, 3 * K], F32),
-    "ab": ("sbuf", [128, 4 * K2 + K], F32), "pp": ("sbuf", [128, K], F32),
-    "cf": ("sbuf", [128, 9 * K], F32), "btmp": ("sbuf", [128, K], F32),
-    "dd": ("sbuf", [128, 2 * K2], F32), "xs": ("sbuf", [128, K2], F32),
-    "t12": ("sbuf", [128, 4 * K2], F32), "ul": ("sbuf", [128, 4 * K], F32),
-    "rt": ("sbuf", [128, W], F32), "cs": ("sbuf", [128, 3 * K2], F32),
-    "pr": ("sbuf", [128, 6 * K2], F32), "pb": ("sbuf", [128, 6 * K], F32),
+    "wraw": ("sbuf", [128, K], BF), "yw": ("sbuf", [128, 4 * K3], BF),
+    "fw": ("sbuf", [128, W + 3 * K3], F32), "bw": ("sbuf", [128, W + 3 * K3 + 3 * K4 + K2], F32),
+    "mw": ("sbuf", [128, 4 * K3], F32), "db": ("sbuf", [128, 2 * K3], F32), "da": ("sbuf", [128, K3], F32),
+    "tb": ("sbuf", [128, 6 * K], F32), "su": ("sbuf", [128, 24], U16), "r2": ("sbuf", [128, 2 * 24], U16),
+    "nv": ("sbuf", [128, 3 * K3], F32), "va3": ("sbuf", [128, 3 * K], BF),
+    "ea": ("sbuf", [128, 5 * K2], F32), "eb": ("sbuf", [128, 4 * K2], F32), "pp": ("sbuf", [128, K], F32),
+    "xs": ("sbuf", [128, K2], F32),
+    "t12": ("sbuf", [128, 2 * K2], F32), "ul": ("sbuf", [128, 3 * K], F32),
+    "rt": ("sbuf", [128, W], F32), "pr": ("sbuf", [128, 6 * K2], F32), "pb": ("sbuf", [128, 6 * K], F32),
     "of1": ("sbuf", [128, 6 * 48], U16), "ofb": ("sbuf", [128, 12 * 24], U16), "fin": ("sbuf", [128, 96], U16),
     "rs": ("sbuf", [128, 4 * 24], U16), "rl": ("sbuf", [128, 16 * 24], U16),
     "sg": ("sbuf", [128, 400], BF), "ls": ("sbuf", [128, 400], BF), "nx": ("sbuf", [128, 400], BF), "gx": ("sbuf", [128, K], BF),
     "sm": ("sbuf", [128, 2 * 24], F32), "sx": ("sbuf", [128, 2 * 24], BF), "lm": ("sbuf", [128, 8], F32),
-    "hout": ("sbuf", [128, K], F32),
     "ip": ("sbuf", [128, 8], I32), "col": ("sbuf", [128, 8], F32),
     "ones": ("sbuf", [128, 128], BF), "idb": ("sbuf", [128, 128], BF), "idf": ("sbuf", [128, 128], F32), "ni8": ("sbuf", [128, 128], F32),
     "id2": ("sbuf", [128, 128], F32), "nib": ("sbuf", [128, 128], BF),
@@ -82,6 +82,12 @@ def rank_program(g, core, T, topo):
                 Q[e].wait_ge(T.sem[s], v)
                 seen[e][s] = v
 
+    def halves(keys):
+        out = []
+        for k in keys:
+            out += [k + "a", k + "b"] if k[0] == "#" and len(k) == 2 else [k]
+        return out
+
     def deps(e, r, w):
         toks = []
         for k in r:
@@ -91,9 +97,9 @@ def rank_program(g, core, T, topo):
             if k in lastw:
                 toks.append(lastw[k])
             toks += reads.get(k, [])
-        for k in list(r) + list(w):
+        for k in r + w:
             if k[0] == "#":
-                toks += [t for o, t in bank.get(k, {}).items() if o != e]
+                toks += [t for o, t in bank.get(k[:2], {}).items() if o != e]
         need(e, toks)
 
     def done(e, tok, r, w):
@@ -102,11 +108,12 @@ def rank_program(g, core, T, topo):
         for k in w:
             lastw[k] = tok
             reads[k] = []
-        for k in list(r) + list(w):
+        for k in r + w:
             if k[0] == "#":
-                bank.setdefault(k, {})[e] = tok
+                bank.setdefault(k[:2], {})[e] = tok
 
     def op(e, fn, r=(), w=()):
+        r, w = halves(r), halves(w)
         deps(e, r, w)
         s = CS[e]
         fn().then_inc(T.sem[s], 1)
@@ -114,6 +121,7 @@ def rank_program(g, core, T, topo):
         done(e, (s, cnt[s]), r, w)
 
     def dma(e, out, in_, r=(), w=(), **kw):
+        r, w = list(r), list(w)
         deps(e, r, w)
         s = "d%d" % nd[0]
         nd[0] += 1
@@ -122,7 +130,7 @@ def rank_program(g, core, T, topo):
         done(e, (s, 16), r, w)
 
     def send(trs, r, lsem="loc"):
-        deps("g", r, ())
+        deps("g", list(r), [])
         ts = []
         for d, eng, sem, srcs, dst in trs:
             rid, pid = topo.addr(cores[d], core)
@@ -134,7 +142,7 @@ def rank_program(g, core, T, topo):
             cnt[lsem] = cnt.get(lsem, 0) + len(eng)
         g.remote_dma_fused(ts, local_sem=T.sem[lsem])
         if lsem != "loc":
-            done("g", (lsem, cnt[lsem]), r, ())
+            done("g", (lsem, cnt[lsem]), list(r), [])
 
     def lands(key, sem, n):
         cnt[sem] = n
@@ -157,6 +165,10 @@ def rank_program(g, core, T, topo):
     def blk(t, i, n=K):
         return t[:, i * K:i * K + n]
 
+    def slot(t, c0, s, r, h=None):
+        lo, hi = (0, K) if h is None else (h * H, (h + 1) * H)
+        return t[:, c0 + s + r * lo:c0 + r * hi:r]
+
     def tt(out, a, b, o, r, w):
         op("v", lambda: V.tensor_tensor(out, a, b, o), r, w)
 
@@ -171,6 +183,9 @@ def rank_program(g, core, T, topo):
 
     def ms(ap, c, w):
         op("v", lambda: V.memset(ap, c), (), w)
+
+    def scan(out, d0, d1, r, w):
+        op("v", lambda: V.tensor_tensor_scan(out, d0, d1, 0.0, ALU.mult, ALU.add), r, w)
 
     def act(out, a, f, r, w, **kw):
         op("s", lambda: S.activation(out, a, f, **kw), r, w)
@@ -198,6 +213,9 @@ def rank_program(g, core, T, topo):
         else:
             op("g", lambda: g.iota(out, pat, base, cm), (), w)
 
+    def gcopy(out, a, r, w):
+        op("g", lambda: g.affine_select(out, a, [[0, K]], ALU.is_ge, 0.0, 0, 0), r, w)
+
     def names(t, lo=0, hi=48):
         return (T.nm if t == 0 else T.ntl)[:, t, lo:hi]
 
@@ -205,14 +223,30 @@ def rank_program(g, core, T, topo):
         return "n%d" % t
 
     ORDER = [0, 1, 2, 3, 2, 1, 0]
-    LBASE = [0, 0, 0, W, W + K2, W + 2 * K2]
+    LBASE = [0, 0, 0, W, W + K3, W + 2 * K3]
+
+    def dpos(t):
+        return W + 3 * K3 + K4 * (3 - t)
+
+    def codes(k):
+        i = k % 3
+        return T.pb[:, i * K2:(i + 1) * K2], ["pb%d" % (2 * i), "pb%d" % (2 * i + 1)]
 
     def cs_make(k):
-        iota(T.cs[:, (k % 3) * K2:(k % 3 + 1) * K2], [[1, K2]], POS0 + W + K2 * k, 0, ["cs%d" % (k % 3)])
+        c, key = (k % 3) * K2, codes(k)[1]
+        if k == 6:
+            iota(T.pb[:, c:c + K2], [[1, K2]], POS0 + dpos(0), 0, key)
+            return
+        r, base = (2, W + K3 * k) if k < 3 else (3, dpos(6 - k))
+        iota(T.pb[:, c:c + K], [[r, K]], POS0 + base + r - 1, 0, key[:1])
+        iota(T.pb[:, c + K:c + K2], [[1, K]], POS0 + base + r * K, 0, key[1:])
 
-    def scat(k):
+    def scat(k, part=None):
         t = ORDER[k]
-        act(T.rt[:, :].indirect(names(t)), T.cs[:, (k % 3) * K2:(k % 3 + 1) * K2], AF.Silu, ["cs%d" % (k % 3), nk(t), "rt"], ["rt"])
+        if part is None:
+            act(T.rt[:, :].indirect(names(t)), codes(k)[0], AF.Silu, codes(k)[1] + [nk(t), "rt"], ["rt"])
+        else:
+            act(T.rt[:, :].indirect(names(t, 24 * part, 24 * part + 24)), blk(T.pb, 2 * (k % 3) + part), AF.Silu, codes(k)[1] + [nk(t), "rt"], ["rt"])
 
     def lvisit(li):
         return li + 1 if li < 3 else li - 3
@@ -230,21 +264,24 @@ def rank_program(g, core, T, topo):
     def wrap1(li, b=7):
         wrap(b, T.pr, li * K2, K2, ["pr%d" % (2 * li), "pr%d" % (2 * li + 1)])
 
-    def offa(li):
-        return T.of1[:, li * 48:li * 48 + 24], "oa%d" % li
+    def conv1(li, b=7):
+        conv(T.of1[:, li * 48:li * 48 + 48], b, 0, 48, LBASE[li], ["la%d" % li, "lb0_%d" % li])
 
-    def offb(rnd, li):
+    def half(t, c, h):
+        return t[:, c:c + 24] if h is None else t[:, c + 12 * h:c + 12 * h + 12]
+
+    def offa(li, h=None):
+        return half(T.of1, li * 48, h), "la%d" % li
+
+    def offb(rnd, li, h=None):
         if rnd == 0:
-            return T.of1[:, li * 48 + 24:li * 48 + 48], "ob0_%d" % li
-        c = ((rnd - 1) * 6 + li) * 24
-        return T.ofb[:, c:c + 24], "ob%d_%d" % (rnd, li)
+            return half(T.of1, li * 48 + 24, h), "lb0_%d" % li
+        return half(T.ofb, ((rnd - 1) * 6 + li) * 24, h), "lb%d_%d" % (rnd, li)
 
-    def perm(rnd, k, t):
+    def perm(rnd, k, t, h=None):
         if t == 0:
-            c = ((rnd - 1) * 2 + k) * 24
-            return T.rs[:, c:c + 24], "rs%d_%d" % (rnd, k)
-        c = (((rnd - 1) * 2 + k) * 4 + t) * 24
-        return T.rl[:, c:c + 24], "rl%d_%d_%d" % (rnd, k, t)
+            return half(T.rs, ((rnd - 1) * 2 + k) * 24, h), "rs%d_%d" % (rnd, k)
+        return half(T.rl, (((rnd - 1) * 2 + k) * 4 + t) * 24, h), "rl%d_%d_%d" % (rnd, k, t)
 
     def ptab(rnd, li):
         if rnd == 0:
@@ -268,194 +305,299 @@ def rank_program(g, core, T, topo):
             o, k = offb(rnd, li + i)
             conv(o, b, 24 * i, 24, LBASE[li + i], [k])
 
-    def Aof(t):
-        return blk(T.ab, 2 * t), "A%d" % t
+    def rec(rnd, t):
+        return 4 if t == 0 and rnd % 2 == 1 else t
 
-    def Bof(rnd, t):
-        if t == 0 and rnd % 2 == 1:
-            return blk(T.ab, 8), "B0x"
-        return blk(T.ab, 2 * t + 1), "B%d" % t
+    def EA(rnd, t, h=None):
+        return slot(T.ea, rec(rnd, t) * K2, 0, 2, h), "ea%d" % rec(rnd, t)
+
+    def Bof(rnd, t, h=None):
+        return slot(T.ea, rec(rnd, t) * K2, 1, 2, h), "B%d" % rec(rnd, t)
+
+    def EB(t, h=None):
+        return slot(T.eb, t * K2, 0, 2, h), "eb%d" % t
+
+    def Aof(t, h=None):
+        return slot(T.eb, t * K2, 1, 2, h), "A%d" % t
+
+    def hk(k, h=None):
+        return [k + "a", k + "b"] if h is None else [k + "ab"[h]]
+
+    def Y(t, h=None):
+        return slot(T.yw, t * K3, 0, 1, h)
+
+    def NW(t):
+        return slot(T.yw, t * K3 + K, 1, 2)
+
+    def mw(t, s):
+        return slot(T.mw, t * K3, s, 3)
+
+    def DB(t, s):
+        return slot(T.db, (t % 2) * K3, s, 3)
+
+    def DA(s):
+        return slot(T.da, 0, s, 3)
+
+    TB = slot(T.tb, 0, 5, 6)
 
     def VBof(rnd):
         return blk(T.va3, 1 + rnd % 2), "vb%d" % (rnd % 2)
 
-    def ywof(t):
-        return blk(T.yw, 2 * t), blk(T.yw, 2 * t + 1), "yw%d" % t
-
-    def loadyw(t):
-        y, w, k = ywof(t)
-        mm([(bk(0), T.idb[:, :], y)], [k, "idb"], ["#0"])
-        if t < 3:
-            mm([(bk(2), T.idb[:, :], w)], [k, "idb"], ["#2"])
-
     def fwin(t):
-        return T.fw[:, 0:W + K2 * t], ["fth"] + ["o%s%d" % (s, i) for i in range(t) for s in "ab"]
-
-    def dpos(t):
-        return W + K2 * (6 - t)
+        return T.fw[:, 0:W + K3 * t], ["fth"] + ["o%s%d" % (s, i) for i in range(t) for s in "ab"]
 
     def bwin(t):
-        return T.bw[:, W + K2 * t:dpos(t)], ["di%d" % i for i in range(t, 3)] + ["do%s%d" % (s, i) for i in range(t + 1, 4) for s in "ab"]
+        return T.bw[:, W + K3 * t:dpos(t)], ["di%d" % i for i in range(t, 3)] + ["do%s%d" % (s, i) for i in range(t + 1, 4) for s in "ab"]
+
+    def douts(t):
+        c = dpos(t)
+        if t == 0:
+            return T.bw[:, c:c + K], T.bw[:, c + K:c + K2]
+        return slot(T.bw, c, 2, 3), T.bw[:, c + K3:c + K4]
 
     def prefill(t):
-        dma("y", T.bw[:, W + K2 * t:W + K2 * (t + 1)], T.nv[:, K2 * t:K2 * (t + 1)], ["nv%d" % t], ["di%d" % t])
+        dma("y", T.bw[:, W + K3 * t:W + K3 * (t + 1)], T.nv[:, K3 * t:K3 * (t + 1)], ["nva%d" % t, "nvb%d" % t, "nvz%d" % t], ["di%d" % t])
 
     def accum(t):
-        dma("g", T.bw[:, W + K2 * t:W + K2 * (t + 1)], T.fw[:, W + K2 * t:W + K2 * (t + 1)], ["oa%d" % t, "ob%d" % t],
+        dma("g", T.bw[:, W + K3 * t:W + K3 * (t + 1)], T.fw[:, W + K3 * t:W + K3 * (t + 1)], ["oa%d" % t, "ob%d" % t],
             ["di%d" % t], accum_op=ALU.add)
+
+    def back(rnd, t, out, key):
+        if rnd == 0:
+            act(out, TB, AF.Copy, ["tb"], [key])
+        else:
+            o, ko = perm(rnd, 1, t)
+            gat("s", out, T.tb[:, :], o, ["tb", "tbz", ko], [key])
+
+    def pe_e(rnd):
+        return rnd == 2 and PE_E
+
+    def loady(rnd, t):
+        if pe_e(rnd):
+            for h in (0, 1):
+                mm([(bk(h, H), T.nib[:, :], Y(t, h))], ["yw%d" % t, "nib"], ["#%d" % h], last=False)
+        else:
+            mm([(bk(0), T.idb[:, :], Y(t))], ["yw%d" % t, "idb"], ["#0"])
 
     def fgather(rnd, t, e):
         win, wk = fwin(t)
-        (a, ka), (b, kb) = Aof(t), Bof(rnd, t)
-        ob, kob = offb(rnd, t - 1)
-        oa, koa = offa(t - 1)
-        gat(e, b, win, ob, wk + [kob], [kb])
-        gat(e, a, win, oa, wk + ["L" + koa], [ka])
+        for h in (0, 1):
+            ob, kob = offb(rnd, t - 1, h)
+            gat(e, Bof(rnd, t, h)[0], win, ob, wk + [kob], hk(Bof(rnd, t)[1], h))
+        gat(e, Aof(t)[0], win, offa(t - 1)[0], wk + [offa(t - 1)[1]], hk(Aof(t)[1]))
 
     def mreal(t):
-        y, w, kw = ywof(t)
-        mm([(bk(2), T.id2[:, :], T.pp[:, :]), (bk(2), T.nib[:, :], y)], ["id2", "nib", "pp", kw], ["#2"])
+        mm([(bk(2), T.id2[:, :], T.pp[:, :]), (bk(2), T.nib[:, :], Y(t))], ["id2", "nib", "ppa", "ppb", "yw%d" % t], ["#2"])
 
-    def fwd(rnd, t, pin, pr, mid=None, tail=None):
+    def coef2(t):
+        tt(mw(t, 1), bk(2), NW(t), ALU.mult, ["#2", "yw%d" % t], ["m%d" % t])
+
+    def fwd(rnd, t, pin, mid=(None, None, None), tail=None, sfill=None, between=None, pfill=None, before_back=None):
         (a, ka), (b, kb) = Aof(t), Bof(rnd, t)
-        y, w, kw = ywof(t)
-        P = T.pp[:, :]
-        tt(P, pin[0], pin[1], ALU.mult, pr, ["pp"])
-        tt(bk(1), P, bk(0), ALU.subtract, ["pp", "#0"], ["#1"])
-        mid = mid or [None] * 3
+        (ea, kea), (eb, keb) = EA(rnd, t), EB(t)
+        kw = "yw%d" % t
+        for h in (0, 1):
+            x, y, r = pin(h)
+            tt(slot(T.pp, 0, 0, 1, h), x, y, ALU.mult, r, hk("pp", h))
+            if pe_e(rnd):
+                mm([(bk(h, H), T.idf[:, :], slot(T.pp, 0, 0, 1, h))], hk("pp", h) + ["idf"], ["#%d" % h], first=False)
+        if rnd == 2 and t > 0:
+            coef2(t - 1)
+        if t == 3 or rnd == 0:
+            mm([(bk(2), T.idb[:, :], NW(t))], [kw, "idb"], ["#2"])
         if t == 3:
-            tt(bk(4), bk(1), a, ALU.mult, ["#1", ka], ["#4"])
-            tt(bk(3), bk(1), b, ALU.mult, ["#1", kb], ["#3"])
-            act(bk(0), b, AF.Square, [kb], ["#0"])
-            if rnd == 2:
-                mreal(t)
-            else:
-                tt(bk(2), bk(1), P, ALU.add, ["#1", "pp"], ["#2"])
-            act(bk(1), a, AF.Square, [ka], ["#1"])
-            tt(bk(6), bk(4), w, ALU.mult, ["#4", kw], ["#6"])
-            tt(bk(5), bk(3), w, ALU.mult, ["#3", kw], ["#5"])
-            if rnd == 2:
-                tt(bk(0), bk(0), w, ALU.mult, ["#0", kw], ["#0"])
-                act(bk(0), bk(0), AF.Identity, ["#0"], ["#0"], scale=-1.0, bias=1.0)
-            tt(bk(6), b, bk(6), ALU.subtract, ["#6", kb], ["#6"])
-            if rnd == 2:
-                tt(bk(1), bk(1), w, ALU.mult, ["#1", kw], ["#1"])
-                act(bk(1), bk(1), AF.Identity, ["#1"], ["#1"], scale=-1.0, bias=1.0)
-            tt(bk(5), a, bk(5), ALU.subtract, ["#5", ka], ["#5"])
-            if rnd == 2:
-                tt(bk(2), bk(2), w, ALU.mult, ["#2", kw], ["#2"])
-            vb, kvb = VBof(rnd)
-            tt(blk(T.dd, 3), bk(6), vb, ALU.subtract, ["#6", kvb], ["db1"])
-            tt(blk(T.dd, 2), bk(5), blk(T.va3, 0), ALU.subtract, ["#5", "va"], ["da1"])
-            return
-        eb, ea = blk(T.cf, 3 * t + 1), blk(T.cf, 3 * t + 2)
-        tt(ea, bk(1), a, ALU.mult, ["#1", ka], ["ea%d" % t])
-        tt(eb, bk(1), b, ALU.mult, ["#1", kb], ["eb%d" % t])
-        if rnd > 0:
-            need("y", [lastw["eb%d" % t]])
-            prefill(t)
+            for i in (6, 5):
+                mm([(bk(i), T.idb[:, :], T.zb[:, 0:K])], ["idb", "zb"], ["#%d" % i], last=False)
+        if pfill:
+            pfill()
+        if rnd == 2 and t < 3:
+            mreal(t)
+        if pe_e(rnd):
+            e = [(bk(h, H), "#%d" % h) for h in (0, 1)]
+        else:
+            e = [(slot(B[1], 0, 0, 1, h), "#1" + "ab"[h]) for h in (0, 1)]
+            for h in (0, 1):
+                tt(e[h][0], slot(T.pp, 0, 0, 1, h), slot(B[0], 0, 0, 1, h), ALU.subtract, hk("pp", h) + ["#0"], [e[h][1]])
         if mid[0]:
             mid[0]()
-        tt(bk(6), ea, bk(2), ALU.mult, ["#2", "ea%d" % t], ["#6"])
+        for h in (0, 1):
+            tt(EA(rnd, t, h)[0], e[h][0], Aof(t, h)[0], ALU.mult, [e[h][1]] + hk(ka, h), hk(kea, h))
         if mid[1]:
             mid[1]()
-        tt(bk(5), eb, bk(2), ALU.mult, ["#2", "eb%d" % t], ["#5"])
+        if pe_e(rnd):
+            for h in (0, 1):
+                tt(EB(t, h)[0], e[h][0], Bof(rnd, t, h)[0], ALU.mult, [e[h][1]] + hk(kb, h), hk(keb, h))
+        else:
+            tt(eb, bk(1), b, ALU.mult, ["#1"] + hk(kb), hk(keb))
         if mid[2]:
             mid[2]()
-        c = W + K2 * t
+        if t == 3:
+            vb, kvb = VBof(rnd)
+            sq = [(bk(0), "#0"), (bk(1), "#1")] if rnd == 2 else [(blk(T.xs, 0), "xs0"), (blk(T.xs, 1), "xs1")]
+            act(sq[0][0], b, AF.Square, hk(kb), [sq[0][1]])
+            act(sq[1][0], a, AF.Square, hk(ka), [sq[1][1]])
+            if sfill:
+                sfill()
+            tt(bk(3), ea, bk(2), ALU.mult, ["#2"] + hk(kea), ["#3"])
+            tt(bk(4), eb, bk(2), ALU.mult, ["#2"] + hk(keb), ["#4"])
+            if rnd == 2:
+                mreal(3)
+            tt(bk(6), b, bk(3), ALU.add, ["#3"] + hk(kb), ["#6"])
+            mm([(bk(6), T.nib[:, :], vb)], ["nib", kvb], ["#6"], first=False)
+            tt(bk(5), a, bk(4), ALU.add, ["#4"] + hk(ka), ["#5"])
+            mm([(bk(5), T.nib[:, :], blk(T.va3, 0))], ["nib", "va"], ["#5"], first=False)
+            if rnd == 2:
+                tt(b, bk(0), NW(3), ALU.mult, ["#0", kw], hk(kb))
+                act(b, b, AF.Identity, hk(kb), hk(kb), bias=1.0)
+                tt(a, bk(1), NW(3), ALU.mult, ["#1", kw], hk(ka))
+                act(a, a, AF.Identity, hk(ka), hk(ka), bias=1.0)
+                coef2(3)
+            else:
+                act(DB(3, 2), bk(6), AF.Copy, ["#6"], ["db1"])
+                act(DB(3, 0), bk(5), AF.Copy, ["#5"], ["da1"])
+                tt(mw(3, 1), bk(1), T.pp[:, :], ALU.add, ["#1", "ppa", "ppb"], ["m3"])
+            if tail:
+                tail()
+            return
+        if rnd > 0:
+            need("y", [lastw[keb + "b"]])
+            prefill(t)
         if rnd == 2:
-            mreal(t)
-            act(bk(4), a, AF.Square, [ka], ["#4"])
-            act(bk(3), b, AF.Square, [kb], ["#3"])
+            act(bk(3), b, AF.Square, hk(kb), ["#3"])
+            act(bk(4), a, AF.Square, hk(ka), ["#4"])
+        if sfill:
+            sfill()
+        zw = T.yw[:, t * K3 + K:(t + 1) * K3]
+        c = W + K3 * t
+        r = rec(rnd, t)
         if rnd == 0:
-            tt(T.fw[:, c + K:c + K2], b, bk(6), ALU.subtract, ["#6", kb], ["ob%d" % t])
+            tt(bk(3), ea, bk(2), ALU.mult, ["#2"] + hk(kea), ["#3"])
         else:
-            tt(T.btmp[:, :], b, bk(6), ALU.subtract, ["#6", kb], ["btmp"])
-            o, ko = perm(rnd, 1, t)
-            gat("s", T.fw[:, c + K:c + K2], T.btmp[:, :], o, ["btmp", ko], ["ob%d" % t])
-        tt(T.fw[:, c:c + K], a, bk(5), ALU.subtract, ["#5", ka], ["oa%d" % t])
+            scan(T.tb[:, 2::3], zw, T.ea[:, r * K2:(r + 1) * K2], [kw] + hk(kea) + hk(kb), ["tb"])
+            if before_back:
+                before_back()
+            back(rnd, t, T.fw[:, c + K2:c + K3], "ob%d" % t)
+        if between:
+            between()
+        scan(T.fw[:, c:c + K2], zw, T.eb[:, t * K2:(t + 1) * K2], [kw] + hk(keb) + hk(ka), ["oa%d" % t])
+        if rnd == 0:
+            tt(T.fw[:, c + K2:c + K3], b, bk(3), ALU.add, ["#3"] + hk(kb), ["ob%d" % t])
         if tail:
             tail()
         if rnd == 2:
-            tt(a, bk(4), w, ALU.mult, ["#4", kw], [ka])
-            tt(b, bk(3), w, ALU.mult, ["#3", kw], [kb])
-            tt(blk(T.cf, 3 * t), bk(2), w, ALU.mult, ["#2", kw], ["m%d" % t])
+            tt(b, bk(3), NW(t), ALU.mult, ["#3", kw], hk(kb))
+            tt(a, bk(4), NW(t), ALU.mult, ["#4", kw], hk(ka))
         elif t > 0:
-            tt(blk(T.cf, 3 * t), bk(1), P, ALU.add, ["#1", "pp"], ["m%d" % t])
+            tt(mw(t, 1), bk(1), T.pp[:, :], ALU.add, ["#1", "ppa", "ppb"], ["m%d" % t])
 
-    def fvisit(rnd, t, e, tail=None):
-        fgather(rnd, t, e)
+    def pin_win(rnd, t):
         win, wk = fwin(t)
-        oa, koa = offa(t - 1)
-        b, kb = Bof(rnd, t)
-        fwd(rnd, t, (win.indirect(oa), b), wk + ["L" + koa, kb], tail=tail)
+        return lambda h: (win.indirect(offa(t - 1, h)[0]), Bof(rnd, t, h)[0], wk + [offa(t - 1)[1]] + hk(Bof(rnd, t)[1], h))
 
     def bgather(rnd, t):
         win, wk = bwin(t)
         p = t % 2
-        oa, koa = offa(3 + t)
-        ob, kob = offb(rnd, 3 + t)
-        gat("s", blk(T.dd, 2 * p), win, oa, wk + ["L" + koa], ["da%d" % p])
+        gat("s", DB(t, 0), win, offa(3 + t)[0], wk + [offa(3 + t)[1]], ["da%d" % p])
         if t > 0 or rnd == 2:
-            gat("s", blk(T.dd, 2 * p + 1), win, ob, wk + [kob], ["db%d" % p])
+            ob, kob = offb(rnd, 3 + t)
+            gat("s", DB(t, 2), win, ob, wk + [kob], ["db%d" % p])
+        if t > 0 and rnd < 2:
+            gcopy(DA(2), DB(t, 0), ["da%d" % p], ["ca"])
+
+    def ubank(rnd, t):
+        return (5, 6) if t == 3 or (t == 1 and rnd < 2) else (3, 4)
+
+    def uload(rnd, t):
+        b1, b2 = ubank(rnd, t)
+        m_, km = (T.ni8, "ni8") if rnd == 2 and t < 2 else (T.idf, "idf")
+        mm([(bk(b1), m_[:, :], EB(t)[0])], [km] + hk(EB(t)[1]), ["#%d" % b1])
+        if t > 0 or rnd == 2:
+            mm([(bk(b2), m_[:, :], EA(rnd, t)[0])], [km] + hk(EA(rnd, t)[1]), ["#%d" % b2])
 
     def uprod(rnd, t):
         p = t % 2
-        tt(blk(T.t12, 2 * t), bk(3), blk(T.dd, 2 * p), ALU.mult, ["#3", "da%d" % p], ["t1_%d" % t])
-        tt(blk(T.t12, 2 * t + 1), bk(4), blk(T.dd, 2 * p + 1), ALU.mult, ["#4", "db%d" % p], ["t2_%d" % t])
+        b1, b2 = ubank(rnd, t)
+        x1, x2 = ((EB(3)[0], hk("eb3")), (EA(rnd, 3)[0], hk("ea3"))) if t == 3 else ((DB(t, 0), ["da%d" % p]), (DB(t, 2), ["db%d" % p]))
+        tt(blk(T.t12, 2 * p), bk(b1), x1[0], ALU.mult, ["#%d" % b1] + x1[1], ["t1_%d" % p])
+        tt(blk(T.t12, 2 * p + 1), bk(b2), x2[0], ALU.mult, ["#%d" % b2] + x2[1], ["t2_%d" % p])
         if t > 0:
             d = (q + t) % NR
-            send([(d, topo.engines(core, cores[d]), "u%d_%d" % (rnd, t), [blk(T.t12, 2 * t), blk(T.t12, 2 * t + 1)], blk(T.ul, t))],
-                 ["t1_%d" % t, "t2_%d" % t], "lu%d" % t)
+            send([(d, topo.engines(core, cores[d]), "u%d_%d" % (rnd, t), [blk(T.t12, 2 * p), blk(T.t12, 2 * p + 1)], blk(T.ul, t - 1))],
+                 ["t1_%d" % p, "t2_%d" % p], "lu%d" % t)
             lands("ul%d" % t, "u%d_%d" % (rnd, t), len(topo.engines(cores[(q - t) % NR], core)))
-            m_, km = (T.ni8, "ni8") if rnd == 2 and t < 3 else (T.idf, "idf")
-            mm([(bk(3), m_[:, :], blk(T.cf, 3 * (t - 1) + 1))], [km, "eb%d" % (t - 1)], ["#3"])
-            if t > 1 or rnd == 2:
-                mm([(bk(4), m_[:, :], blk(T.cf, 3 * (t - 1) + 2))], [km, "ea%d" % (t - 1)], ["#4"])
 
-    def bwd(rnd, t, early=None, sfill=None, tail=None):
+    def bscan(rnd, t, early=None, sfill=None, tail=None, between=None):
         p = t % 2
-        da, db, ka, kb = blk(T.dd, 2 * p), blk(T.dd, 2 * p + 1), "da%d" % p, "db%d" % p
-        y, w, kw = ywof(t)
-        more = t > 1 or (t == 1 and rnd == 2)
-        tt(bk(5), bk(0), da, ALU.mult, ["#0", ka], ["#5"])
-        tt(blk(T.xs, 1), bk(2), da, ALU.mult, ["#2", ka], ["xs1"])
-        tt(bk(6), bk(1), db, ALU.mult, ["#1", kb], ["#6"])
-        tt(blk(T.xs, 0), bk(2), db, ALU.mult, ["#2", kb], ["xs0"])
-        if more:
-            mm([(bk(2), T.idf[:, :], blk(T.cf, 3 * (t - 1)))], ["idf", "m%d" % (t - 1)], ["#2"])
+        ka, kb = "da%d" % p, "db%d" % p
+        if t == 3:
+            tt(DB(t, 1), bk(6), blk(T.xs, 1), ALU.mult, ["#6", "xs1"], ["pb_%d" % p])
+            tt(DA(1), bk(5), blk(T.xs, 0), ALU.mult, ["#5", "xs0"], ["pa"])
+        else:
+            tt(DA(1), bk(0), DB(t, 0), ALU.mult, ["#0", ka], ["pa"])
+            tt(DB(t, 1), bk(1), DB(t, 2), ALU.mult, ["#1", kb], ["pb_%d" % p])
+        if t == 3:
+            gcopy(DA(0), DB(t, 2), [kb], ["cb"])
+            act(DA(2), DB(t, 0), AF.Copy, [ka], ["ca"])
+        else:
+            act(DA(0), DB(t, 2), AF.Copy, [kb], ["cb"])
         if early:
             early()
+        m = T.mw[:, t * K3:(t + 1) * K3]
+        km = ["m%d" % t, "mz", "mw%d" % t]
+        scan(T.tb[:, 1::2], m, T.db[:, p * K3:(p + 1) * K3], km + [ka, kb, "pb_%d" % p], ["tb"])
+        if t > 1:
+            act(bk(0), Bof(rnd, t - 1)[0], AF.Square, hk(Bof(rnd, t - 1)[1]), ["#0"])
+            act(bk(1), Aof(t - 1)[0], AF.Square, hk(Aof(t - 1)[1]), ["#1"])
         if sfill:
             sfill()
-        if more:
-            (a, kaa), (b, kbb) = Aof(t - 1), Bof(rnd, t - 1)
-            if rnd == 2:
-                act(bk(0), b, AF.Identity, [kbb], ["#0"], scale=-1.0, bias=1.0)
-                act(bk(1), a, AF.Identity, [kaa], ["#1"], scale=-1.0, bias=1.0)
-            else:
-                act(bk(0), b, AF.Square, [kbb], ["#0"])
-                act(bk(1), a, AF.Square, [kaa], ["#1"])
+        back(rnd, t, douts(t)[1], "dob%d" % t)
+        if between:
+            between()
         c = dpos(t)
-        if rnd == 2:
-            tt(T.btmp[:, :], bk(6), blk(T.xs, 1), ALU.subtract, ["#6", "xs1"], ["btmp"])
-            o, ko = perm(rnd, 1, t)
-            gat("s", T.bw[:, c + K:c + K2], T.btmp[:, :], o, ["btmp", ko], ["dob%d" % t])
-            tt(T.bw[:, c:c + K], bk(5), blk(T.xs, 0), ALU.subtract, ["#5", "xs0"], ["doa%d" % t])
-            return
-        tt(bk(6), bk(6), blk(T.xs, 1), ALU.add, ["#6", "xs1"], ["#6"])
-        tt(bk(5), bk(5), blk(T.xs, 0), ALU.add, ["#5", "xs0"], ["#5"])
-        tt(bk(6), bk(6), w, ALU.mult, ["#6", kw], ["#6"])
-        tt(bk(5), bk(5), w, ALU.mult, ["#5", kw], ["#5"])
-        if rnd == 0:
-            tt(T.bw[:, c + K:c + K2], db, bk(6), ALU.subtract, ["#6", kb], ["dob%d" % t])
-        else:
-            tt(T.btmp[:, :], db, bk(6), ALU.subtract, ["#6", kb], ["btmp"])
-            o, ko = perm(rnd, 1, t)
-            gat("s", T.bw[:, c + K:c + K2], T.btmp[:, :], o, ["btmp", ko], ["dob%d" % t])
-        tt(T.bw[:, c:c + K], da, bk(5), ALU.subtract, ["#5", ka], ["doa%d" % t])
+        scan(T.bw[:, c:c + K3], m, T.da[:, :], km + ["ca", "cb", "pa"], ["doa%d" % t])
         if tail:
             tail()
+
+    def breal(t):
+        p = t % 2
+        if t == 3:
+            (c1, k1), (c3, k3), c2 = Bof(2, 3), Aof(3), mw(3, 1)
+            tt(blk(T.xs, 1), bk(5), c2, ALU.mult, ["#5", "m3"], ["xs1"])
+            tt(bk(4), bk(6), c2, ALU.mult, ["#6", "m3"], ["#4"])
+            tt(bk(3), bk(6), c3, ALU.mult, ["#6"] + hk(k3), ["#3"])
+            tt(blk(T.xs, 0), bk(5), c1, ALU.mult, ["#5"] + hk(k1), ["xs0"])
+            ba, bb = 4, 3
+        else:
+            da, db, ka, kb = DB(t, 0), DB(t, 2), "da%d" % p, "db%d" % p
+            tt(bk(5), bk(0), da, ALU.mult, ["#0", ka], ["#5"])
+            tt(blk(T.xs, 1), bk(2), da, ALU.mult, ["#2", ka], ["xs1"])
+            tt(bk(6), bk(1), db, ALU.mult, ["#1", kb], ["#6"])
+            tt(blk(T.xs, 0), bk(2), db, ALU.mult, ["#2", kb], ["xs0"])
+            ba, bb = 5, 6
+        if t > 0:
+            mm([(bk(2), T.idf[:, :], mw(t - 1, 1))], ["idf", "m%d" % (t - 1)], ["#2"])
+            act(bk(0), Bof(2, t - 1)[0], AF.Identity, hk(Bof(2, t - 1)[1]), ["#0"], bias=1.0)
+            act(bk(1), Aof(t - 1)[0], AF.Identity, hk(Aof(t - 1)[1]), ["#1"], bias=1.0)
+        tt(TB, bk(bb), blk(T.xs, 1), ALU.add, ["#%d" % bb, "xs1"], ["tb"])
+        back(2, t, douts(t)[1], "dob%d" % t)
+        tt(douts(t)[0], bk(ba), blk(T.xs, 0), ALU.add, ["#%d" % ba, "xs0"], ["doa%d" % t])
+
+    def backward(rnd, fills):
+        for t in (3, 2, 1):
+            sf, tl = fills.get(t, (None, None))
+            if t == 3:
+                uload(rnd, 2)
+            if t == 1:
+                act(bk(4), blk(T.ul, 2), AF.Copy, ["ul3"], ["#4"], scale=-1.0)
+            bscan(rnd, t, early=(lambda: uprod(rnd, 1)) if t == 1 else None, sfill=sf, tail=tl, between=fills.get((t, "between")))
+            if t > 1:
+                bgather(rnd, t - 1)
+                uprod(rnd, t)
+                uload(rnd, t - 2)
+            else:
+                tt(bk(4), bk(4), blk(T.ul, 1), ALU.subtract, ["#4", "ul2"], ["#4"])
+            if (t, "after") in fills:
+                fills[(t, "after")]()
 
     def wrapd(b, src, c0, cen, r):
         mm([(bk(b, 24), T.idb[:, :], cen)] + [(bk(b, 24), T.ewd[:, 15 - i:143 - i], src[:, c0 + i:c0 + K:16]) for i in range(16)],
@@ -466,65 +608,51 @@ def rank_program(g, core, T, topo):
         o, ko = perm(rnd, k, 0)
         return [lambda: ts(t_, bk(b, 24), INI if k == 0 else -INI, ALU.is_equal, ["#%d" % b, "lm%d" % k], ["sm%d" % k], T.lm[:, 4 * k:4 * k + 1], ALU.mult),
                 lambda: tt(x_, bk(b, 24), t_, ALU.add, ["#%d" % b, "sm%d" % k], ["sx%d" % k]),
-                lambda: ts(o, x_, float(CEN), ALU.add, ["sx%d" % k], [ko])]
+                (lambda: ts(o, x_, float(CEN), ALU.add, ["sx%d" % k], [ko])) if k == 0 else
+                (lambda: ts(o, x_, 6.0, ALU.mult, ["sx%d" % k], [ko], 6.0 * CEN + 5, ALU.add))]
 
     def sendperm(rnd, k):
         o, ko = perm(rnd, k, 0)
         to_hosts(lambda t: o, lambda t: perm(rnd, k, t)[0], lambda t: "r%d_%d_%d" % (rnd - 1, k, t), [ko], lambda t: perm(rnd, k, t)[1])
 
-    def vote(rnd):
+    def vote(rnd, sfill):
         win, wk = bwin(0)
         ob, kob = offb(rnd, 3)
         mm([(bk(1, 385), T.idb[:, :], T.zb[:, :])], ["idb", "zb"], ["#1"], last=False)
-        loadyw(0)
+        if not pe_e(rnd + 1):
+            loady(rnd + 1, 0)
         bgather(rnd, 0)
+        sfill()
         t2 = blk(T.t12, 1)
-        tt(t2, win.indirect(ob), blk(T.cf, 2), ALU.mult, wk + [kob, "ea0"], ["t2_0"])
-        tt(bk(5), bk(3), blk(T.dd, 0), ALU.mult, ["#3", "da0"], ["#5"])
+        tt(t2, win.indirect(ob), EA(rnd, 0)[0], ALU.mult, wk + [kob] + hk(EA(rnd, 0)[1]), ["t2_0"])
+        tt(bk(3), bk(3), DB(0, 0), ALU.mult, ["#3", "da0"], ["#3"])
         u0 = blk(T.t12, 0)
-        tt(u0, bk(5), t2, ALU.add, ["#5", "t2_0"], ["t1_0"])
-        tt(bk(4), bk(4), blk(T.ul, 1), ALU.subtract, ["#4", "ul1"], ["#4"])
+        tt(bk(4), bk(4), blk(T.ul, 0), ALU.subtract, ["#4", "ul1"], ["#4"])
+        tt(u0, bk(3), t2, ALU.add, ["#3", "t2_0"], ["t1_0"])
         tt(T.sg[:, 1:385], u0, bk(4), ALU.is_lt, ["#4", "t1_0"], ["sg"])
         mm([(bk(1, 385), T.be[:, :], T.sg[:, 1:386]), (bk(1, 385), T.bo[:, :], T.sg[:, 0:385])], ["be", "bo", "sg"], ["#1"], first=False)
         op("v", lambda: V.tensor_tensor_scan(T.ls[:, 0:385], bk(1, 385), T.d1f[:, :], INI, ALU.max, ALU.min), ["#1", "d1f"], ["ls"])
         wrapd(7, T.ls, 0, T.cw[:, :], ["ls", "cw"])
         op("v", lambda: V.tensor_tensor_scan(T.nx[:, 399:14:-1], B[1][:, 384::-1], T.d1r[:, ::-1], INI, ALU.max, ALU.min), ["#1", "d1r"], ["nx"])
+        if pe_e(rnd + 1):
+            loady(rnd + 1, 0)
         ts(T.lm[:, 0:1], T.ls[:, 384:385], -INI, ALU.add, ["ls"], ["lm0"])
         f = fix(rnd + 1, 0, 7)
         f[0]()
         ts(T.lm[:, 4:5], T.nx[:, 15:16], -INI, ALU.add, ["nx"], ["lm1"], -1.0, ALU.mult)
         f[1]()
+        ts(T.r2[:, rnd * 24:rnd * 24 + 24], T.sx[:, 0:24], 2.0, ALU.mult, ["sx0"], ["r2"], 2.0 * CEN + 1, ALU.add)
         f[2]()
         sendperm(rnd + 1, 0)
-
-    def backward(rnd, fills):
-        def nh():
-            uprod(rnd, 1)
-            act(bk(4), blk(T.ul, 3), AF.Copy, ["ul3"], ["#4"], scale=-1.0)
-        for t in (3, 2, 1):
-            if t < 3:
-                bgather(rnd, t)
-            sf, tl = fills.get(t, (None, None))
-            if t == 1 and rnd < 2:
-                bwd(rnd, t, early=nh, sfill=sf, tail=tl)
-                tt(bk(4), bk(4), blk(T.ul, 2), ALU.subtract, ["#4", "ul2"], ["#4"])
-            else:
-                bwd(rnd, t, sfill=sf, tail=tl)
-                uprod(rnd, t)
-                if (t, "after") in fills:
-                    fills[(t, "after")]()
-
-    def conv1_(li, b=7):
-        conv(T.of1[:, li * 48:li * 48 + 48], b, 0, 48, LBASE[li], ["Loa%d" % li, "ob0_%d" % li])
 
     dma("s", T.an32[:, :], T.an[:, :], (), ["an32"])
     dma("y", T.bn32[:, :, :], T.bn[:, :], (), ["bn32"])
     dma("y", T.thb[:, :], T.th[:, :], (), ["thb"])
     dma("y", T.wraw[:, :], T.wt[:, :], (), ["wraw"])
-    dma("y", blk(T.yw, 0), T.yt[:, :], (), ["y0"])
+    dma("y", Y(0), T.yt[:, :], (), ["y0"])
     dma("y", T.vab[:, :], T.va[:, :], (), ["vab"])
     iota(T.ip[:, 0:1], [[0, 1]], 0, 1, ["ip"], fl=False)
-    iota(T.rt[:, 0:K2], [[1, K2]], POS0, 0, ["rt0"])
+    iota(T.rt[:, 0:K], [[1, K]], POS0, 0, ["rt0"])
     ms(T.ones[:, :], 1.0, ["ones"])
     ms(T.e15[:, :], 0.0, ["e15"])
     op("g", lambda: g.affine_select(T.idb[:, :], T.ones[:, :], [[-1, 128]], ALU.is_equal, 0.0, 0, 1), ["ones"], ["idb"])
@@ -536,9 +664,14 @@ def rank_program(g, core, T, topo):
     cp(T.col[:, 1:4], T.ip[:, 1:4], ["ip1", "ip2", "ip3"], ["col"])
     ms(T.zb[:, :], -33792.0, ["zb"])
     ts(T.col[:, 0:1], T.col[:, 1:2], -1.0, ALU.mult, ["col"], ["col0"], 1.0, ALU.add)
+    ts(T.col[:, 4:5], T.col[:, 2:3], -1.0, ALU.mult, ["col"], ["col4"])
     ms(T.sg[:, :], 0.0, ["sg"])
-    act(T.rt[:, K2:W], T.rt[:, 0:K2], AF.Silu, ["rt0"], ["rt"], bias=float(K2))
-    act(T.cs[:, 0:K2], T.rt[:, 0:K2], AF.Identity, ["rt0"], ["cs0"], bias=float(W))
+    ms(slot(T.yw, K, 0, 2), 0.0, ["z0"])
+    cs_make(1)
+    act(T.rt[:, K:K2], T.rt[:, 0:K], AF.Silu, ["rt0"], ["rt1"], bias=float(K))
+    act(T.rt[:, K2:W], T.rt[:, 0:K2], AF.Identity, ["rt0", "rt1"], ["rt"], bias=float(K2))
+    act(T.pb[:, 0:K], T.rt[:, 0:K], AF.Identity, ["rt0"], ["pb0"], scale=2.0, bias=float(W + 1 - POS0))
+    act(T.pb[:, K:K2], T.rt[:, 0:K], AF.Identity, ["rt0"], ["pb1"], bias=float(W + K2))
     ts(T.x2[:, :, 0:16], T.bn32[:, :, :], T.col[:, 0:1], ALU.mult, ["bn32", "col0"], ["x2a"])
     ts(T.x2[:, :, 16:32], T.bn32[:, :, :], T.col[:, 1:2], ALU.mult, ["bn32", "col"], ["x2b"])
     cp(T.nm[:, :, 0:24], T.an32[:, :], ["an32"], ["nma"])
@@ -548,162 +681,180 @@ def rank_program(g, core, T, topo):
         cp(T.nm[:, :, 24 + c:48:6], T.z2[:, c, :], ["z2"] + (["nma"] if c == 5 else []), ["n0"] if c == 5 else ["nmb%d" % c])
     to_hosts(lambda t: T.nm[:, t, :], lambda t: T.ntl[:, t, :], lambda t: "nm%d" % t, ["n0"], nk)
     scat(0)
-    act(T.cs[:, K2:2 * K2], T.cs[:, 0:K2], AF.Identity, ["cs0"], ["cs1"], bias=float(K2))
-    ts(blk(T.yw, 1), T.wraw[:, :], 0.125, ALU.mult, ["wraw", "y0"], ["yw0"])
+    ts(NW(0), T.wraw[:, :], -0.125, ALU.mult, ["wraw", "y0", "z0"], ["yw0"])
     dma("g", T.fw[:, 0:W], T.th[:, :], (), ["fth"])
-    to_hosts(lambda t: T.yw[:, 0:K2], lambda t: T.yw[:, t * K2:(t + 1) * K2], lambda t: "yw%d" % t, ["yw0"], lambda t: "yw%d" % t)
+    to_hosts(lambda t: T.yw[:, 0:K3], lambda t: T.yw[:, t * K3:(t + 1) * K3], lambda t: "yw%d" % t, ["yw0"], lambda t: "yw%d" % t)
     cs_make(2)
+    for t in range(3):
+        iota(slot(T.nv, t * K3, 0, 2), [[0, K]], 0, 0, ["nvz%d" % t])
     op("g", lambda: g.affine_select(T.e2[:, :], T.e15[:, :], [[1, 144]], ALU.is_equal, 0.0, -14, -1), ["e15"], ["e2"])
     iota(T.bi[:, :], [[-16, 8], [0, 16]], 128, 1, ["bi"], fl=False)
     iota(T.d1i[:, :], [[1, 385]], -CEN, 0, ["d1i"])
     iota(T.cwi[:, :], [[16, 24]], -CEN, 0, ["cwi"])
 
-    loadyw(0)
+    def negw(t):
+        gcopy(mw(t, 2), NW(t), ["yw%d" % t], ["mw%d" % t])
+
+    loady(0, 0)
     gptr(0)
-    gat("v", Bof(0, 0)[0], T.thb[:, :], names(0, 24, 48), ["thb", "n0"], ["B0"])
-    gat("v", Aof(0)[0], T.thb[:, :], names(0, 0, 24), ["thb", "n0"], ["A0"])
-    fwd(0, 0, (T.thb[:, :].indirect(names(0, 0, 24)), Bof(0, 0)[0]), ["thb", "n0", "B0"])
+    gat("v", Bof(0, 0)[0], T.thb[:, :], names(0, 24, 48), ["thb", "n0"], hk("B0"))
+    gat("v", Aof(0)[0], T.thb[:, :], names(0, 0, 24), ["thb", "n0"], hk("A0"))
+    fwd(0, 0, lambda h: (T.thb[:, :].indirect(names(0, 12 * h, 12 * h + 12)), Bof(0, 0, h)[0], ["thb", "n0"] + hk("B0", h)))
     scat(1)
     gptr(1)
     wrap1(0)
-    loadyw(1)
+    loady(0, 1)
     for t in range(3):
-        gat("v", T.nv[:, K2 * t:K2 * (t + 1)], T.vab[:, :], names(t), ["vab", nk(t)], ["nv%d" % t], neg=True)
+        gat("v", slot(T.nv, t * K3, 1, 2), T.vab[:, :], names(t, 0, 24), ["vab", nk(t)], ["nva%d" % t], neg=True)
+        gat("v", T.nv[:, t * K3 + K2:(t + 1) * K3], T.vab[:, :], names(t, 24, 48), ["vab", nk(t)], ["nvb%d" % t], neg=True)
         prefill(t)
-    accum(0)
     cs_make(3)
-    conv1_(0)
+    accum(0)
+    ts(T.nib[:, :], T.idb[:, :], -1.0, ALU.mult, ["idb"], ["nib"])
+    cp(T.idf[:, :], T.idb[:, :], ["idb"], ["idf"])
+    conv1(0)
     wrap1(1, 4)
-    scat(2)
-    gptr(2)
-    fvisit(0, 1, "v", tail=lambda: conv1_(1, 4))
-    accum(1)
+    fgather(0, 1, "v")
+    fwd(0, 1, pin_win(0, 1), tail=lambda: conv1(1, 4), sfill=lambda: (scat(2), gptr(2)))
     cs_make(4)
+    accum(1)
     cs_make(5)
-    loadyw(2)
+    loady(0, 2)
     wrap1(2)
+
     scat(3)
     gptr(5)
+    scat(4)
 
     def consts():
-        conv1_(2)
         ts(T.bi[:, :], T.bi[:, :], 127, ALU.bitwise_and, ["bi"], ["bi"])
-        cp(T.idf[:, :], T.idb[:, :], ["idb"], ["idf"])
         ts(T.be[:, :], T.bi[:, :], 32.0, ALU.is_lt, ["bi"], ["be"], 2048.0, ALU.mult)
         ts(T.bo[:, :], T.bi[:, :], 32.0, ALU.is_lt, ["bi"], ["bo"], 2048.0, ALU.mult)
-        tt(T.ewd[:, :], T.e2[:, :], T.ew[:, :], ALU.subtract, ["e2", "ew"], ["ewd"])
         ms(T.be[:, 1::2], 0.0, ["be"])
         ms(T.bo[:, 0::2], 0.0, ["bo"])
-        ts(T.cw[:, :], T.cwi[:, :], T.col[:, 3:4], ALU.add, ["cwi", "col"], ["cw"])
-    fvisit(0, 2, "v", tail=consts)
+    fgather(0, 2, "v")
+    fwd(0, 2, pin_win(0, 2), tail=lambda: conv1(2))
+    gat("v", T.va3[:, 0:K2], T.vab[:, :], names(3), ["vab", "n3"], ["va", "vb0"])
+    iota(T.mw[:, K3::3], [[0, K3]], 0, 0, ["mz"])
     accum(2)
-    cs_make(6)
-    loadyw(3)
+    for t in (3, 2, 1):
+        negw(t)
+    loady(0, 3)
     wrap1(5)
     fgather(0, 3, "s")
-    gat("s", T.va3[:, 0:K2], T.vab[:, :], names(3), ["vab", "n3"], ["va", "vb0"])
-    ts(T.d1f[:, :], T.d1i[:, :], T.col[:, 2:3], ALU.subtract, ["d1i", "col"], ["d1f"])
-    fwd(0, 3, (fwin(3)[0].indirect(offa(2)[0]), Bof(0, 3)[0]), fwin(3)[1] + ["Loa2", "B3"])
-    conv1_(5)
+    gptr(4)
+    fwd(0, 3, pin_win(0, 3), tail=lambda: (conv1(5), wrap1(4)), sfill=lambda: scat(5, 0))
 
     def s3():
-        scat(4)
-        gptr(4)
-        wrap1(4)
+        scat(5, 1)
 
-    def s2():
-        scat(5)
+    def a3():
         gptr(3)
+        cs_make(6)
 
-    def v3():
-        ts(T.d1r[:, :], T.d1i[:, :], T.col[:, 2:3], ALU.subtract, ["d1i", "col"], ["d1r"], -1.0, ALU.mult)
+    def a2():
+        for s_ in (0, 4):
+            iota(slot(T.tb, 0, s_, 6), [[0, K]], 0, 0, ["tbz"])
 
-    def v2():
-        conv1_(4)
-    backward(0, {3: (s3, v3), 2: (s2, v2), (2, "after"): lambda: wrap1(3), 1: (None, lambda: conv1_(3))})
-    vote(0)
+    def v1():
+        consts()
+        tt(T.ewd[:, :], T.e2[:, :], T.ew[:, :], ALU.subtract, ["e2", "ew"], ["ewd"])
+        ts(T.cw[:, :], T.cwi[:, :], T.col[:, 3:4], ALU.add, ["cwi", "col"], ["cw"])
+
+    def late():
+        act(T.d1f[:, :], T.d1i[:, :], AF.Identity, ["d1i", "col4"], ["d1f"], bias=T.col[:, 4:5])
+        act(T.d1r[:, :], T.d1f[:, :], AF.Copy, ["d1f"], ["d1r"], scale=-1.0)
+        scat(6)
+    backward(0, {3: (s3, None), (3, "after"): a3, (2, "between"): lambda: (conv1(4), wrap1(3)), (2, "after"): a2,
+                 (1, "between"): lambda: conv1(3), 1: (None, v1)})
+    vote(0, late)
 
     for rnd in (1, 2):
-        rho, krho = perm(rnd, 0, 0)
-        (bo_, kbo), (bn_, kbn) = Bof(rnd - 1, 0), Bof(rnd, 0)
-        gat("s", bn_, bo_, rho, [kbo, krho], [kbn])
+        old = rec(rnd - 1, 0)
+        owin, ok = T.ea[:, old * K2:(old + 1) * K2], hk("B%d" % old) + hk("ea%d" % old) + ["r2"]
+        gat("s", Bof(rnd, 0)[0], owin, half(T.r2, (rnd - 1) * 24, None), ok, hk(Bof(rnd, 0)[1]))
         if rnd == 1:
             wrapd(3, T.nx, 16, T.cw[:, :], ["nx", "cw"])
         else:
-            o, ko = perm(1, 1, 0)
-            gat("s", T.gx[:, :], T.nx[:, 16:400], o, ["nx", ko], ["gx"])
-            wrapd(3, T.gx, 0, T.sx[:, 24:48], ["gx", "sx1"])
-        f = fix(rnd, 1, 3)
+            gat("s", T.gx[:, :], T.nx[:, 16:400], T.su[:, :], ["nx", "su"], ["gx"])
+        f = fix(rnd, 1, 3 if rnd == 1 else 7)
 
         def last_fix(f=f, rnd=rnd):
             f[2]()
             sendperm(rnd, 1)
-        fwd(rnd, 0, (bo_.indirect(rho), Aof(0)[0]), [kbo, krho, "A0"], mid=[f[0], f[1], last_fix])
+
+        def pin0(h):
+            return owin.indirect(half(T.r2, (rnd - 1) * 24, h)), Aof(0, h)[0], ok + hk("A0", h)
+        if rnd == 1:
+            fwd(rnd, 0, pin0, mid=[f[0], f[1], last_fix], pfill=lambda: (wrap(4, T.rt, 0, W, ["rt"])))
+        else:
+            fwd(rnd, 0, pin0, pfill=lambda: wrapd(7, T.gx, 0, T.sx[:, 24:48], ["gx", "sx1"]), before_back=lambda: (f[0](), f[1](), last_fix()))
         accum(0)
         if rnd == 2:
             dma("g", T.bw[:, 0:W], T.thb[:, :], ["thb"], ["dbase"], accum_op=ALU.add)
-        loadyw(1)
+        loady(rnd, 1)
         win, wk = fwin(1)
         rho1, krho1 = perm(rnd, 0, 1)
-        gat("v" if rnd == 1 else "s", Aof(1)[0], win, offa(0)[0], wk + ["Loa0"], ["A1"])
         gat("s", blk(T.xs, 0), win, offb(rnd - 1, 0)[0], wk + [offb(rnd - 1, 0)[1]], ["xs0"])
-        gat("s", Bof(rnd, 1)[0], blk(T.xs, 0), rho1, ["xs0", krho1], ["B1"])
+        if rnd == 1:
+            gat("v", Aof(1)[0], win, offa(0)[0], wk + ["la0"], hk("A1"))
+        else:
+            for h in (0, 1):
+                gat("s", Aof(1, h)[0], win, offa(0, h)[0], wk + ["la0"], hk("A1", h))
         pupd(rnd, 1)
-        wrapb(rnd, 1, 1, 7)
-        pupd(rnd, 2)
+        gat("s", Bof(rnd, 1)[0], blk(T.xs, 0), rho1, ["xs0", krho1], hk("B1"))
         if rnd == 1:
+            pupd(rnd, 2)
             pupd(rnd, 3)
-        fwd(rnd, 1, (blk(T.xs, 0).indirect(rho1), Aof(1)[0]), ["xs0", krho1, "A1"], tail=lambda: convb(rnd, 1, 1, 7))
+        fwd(rnd, 1, lambda h: (blk(T.xs, 0).indirect(perm(rnd, 0, 1, h)[0]), Aof(1, h)[0], ["xs0", krho1] + hk("A1", h)),
+            pfill=lambda: wrapb(rnd, 1, 1, 7), tail=lambda: convb(rnd, 1, 1, 7),
+            between=(lambda: conv(T.fin[:, :], 4, 0, 96, 0, ["fin"])) if rnd == 1 else None)
         accum(1)
-        loadyw(2)
-        wrapb(rnd, 2, 1, 7)
+        loady(rnd, 2)
         fgather(rnd, 2, "s")
-        if rnd == 2:
-            pupd(rnd, 3)
-        pupd(rnd, 4)
-        if rnd == 1:
-            pupd(rnd, 5)
-        fwd(rnd, 2, (fwin(2)[0].indirect(offa(1)[0]), Bof(rnd, 2)[0]), fwin(2)[1] + ["Loa1", "B2"], tail=lambda: convb(rnd, 2, 1, 7))
+        for li in ((4, 5) if rnd == 1 else (2, 3)):
+            pupd(rnd, li)
+        fwd(rnd, 2, pin_win(rnd, 2), pfill=lambda: wrapb(rnd, 2, 1, 7), between=(lambda: convb(rnd, 2, 1, 7)) if rnd == 1 else None,
+            tail=(lambda: convb(rnd, 2, 1, 7)) if rnd == 2 else None)
         accum(2)
-        loadyw(3)
+        loady(rnd, 3)
         fgather(rnd, 3, "s")
-        if rnd == 2:
-            pupd(rnd, 5)
-        wrapb(rnd, 3, 3, 7)
         o, ko = perm(rnd, 0, 3)
         gat("s", VBof(rnd)[0], VBof(rnd - 1)[0], o, [VBof(rnd - 1)[1], ko], [VBof(rnd)[1]])
-        fwd(rnd, 3, (fwin(3)[0].indirect(offa(2)[0]), Bof(rnd, 3)[0]), fwin(3)[1] + ["Loa2", "B3"])
-        convb(rnd, 3, 3, 7)
-        if rnd == 1:
-            def f3():
-                scat(6)
-
-            def f2():
-                act(T.bw[:, 0:W], T.vab[:, :], AF.Copy, ["vab"], ["dbase"], scale=-1.0)
-
-                pupd(1, 0)
-
-            def g2():
-                conv(T.fin[:, :], 7, 0, 96, 0, ["fin"])
-                ts(T.ni8[:, :], T.idf[:, :], -0.125, ALU.mult, ["idf"], ["ni8"])
-                ts(T.id2[:, :], T.idf[:, :], 2.0, ALU.mult, ["idf"], ["id2"])
-                ts(T.nib[:, :], T.idb[:, :], -1.0, ALU.mult, ["idb"], ["nib"])
-            backward(rnd, {3: (f3, None), (3, "after"): lambda: wrap(7, T.rt, 0, W, ["rt"]), 2: (f2, g2), (2, "after"): lambda: wrapb(1, 0, 1, 7), 1: (None, lambda: convb(1, 0, 1, 7))})
-            vote(rnd)
+        if rnd == 2:
+            pupd(rnd, 4)
+            pupd(rnd, 5)
+            fwd(rnd, 3, pin_win(rnd, 3))
+            wrapb(rnd, 3, 3, 7)
         else:
-            backward(rnd, {})
+            fwd(rnd, 3, pin_win(rnd, 3), pfill=lambda: wrapb(1, 3, 3, 7), tail=lambda: convb(1, 3, 3, 7), sfill=lambda: pupd(1, 0))
 
-    bgather(2, 0)
-    mm([(bk(7), T.ni8[:, :], blk(T.ul, t)) for t in (3, 2)], ["ni8", "ul3", "ul2"], ["#7"])
-    bwd(2, 0)
-    uprod(2, 0)
+            def g1():
+                convb(1, 0, 1, 7)
+                ts(T.su[:, :], T.sx[:, 24:48], float(CEN), ALU.add, ["sx1"], ["su"])
+                act(T.ni8[:, :], T.idf[:, :], AF.Copy, ["idf"], ["ni8"], scale=-0.125)
+                act(T.id2[:, :], T.idf[:, :], AF.Copy, ["idf"], ["id2"], scale=2.0)
+            backward(rnd, {(3, "after"): lambda: wrapb(1, 0, 1, 7), (1, "between"): g1})
+            vote(rnd, lambda: act(T.bw[:, 0:W], T.vab[:, :], AF.Copy, ["vab"], ["dbase"], scale=-1.0))
+
+    for t in (3, 2, 1, 0):
+        if t == 0:
+            mm([(bk(7), T.ni8[:, :], blk(T.ul, i - 1)) for i in (3, 2)], ["ni8", "ul3", "ul2"], ["#7"])
+        breal(t)
+        if t == 3:
+            convb(2, 3, 3, 7)
+        if t > 0:
+            bgather(2, t - 1)
+        uprod(2, t)
+        if t > 0:
+            uload(2, t - 1)
     tt(bk(7), bk(7), blk(T.t12, 0), ALU.add, ["#7", "t1_0"], ["#7"])
     tt(bk(7), bk(7), blk(T.t12, 1), ALU.add, ["#7", "t2_0"], ["#7"])
     wk = ["dbase"] + ["di%d" % i for i in range(3)] + ["do%s%d" % (s, i) for i in range(4) for s in "ab"] + ["fin"]
     for e, lo, hi in (("s", 0, 640), ("v", 1280, W), ("s", 640, 1280)):
         gat(e, T.fw[:, lo:hi], T.bw[:, :], T.fin[:, lo // 16:hi // 16], wk, ["out%d" % lo] + (["fth"] if lo == 0 else []))
         dma("y", T.yd[:, lo:hi], T.fw[:, lo:hi], ["out%d" % lo], ())
-    tt(T.hout[:, :], bk(7), blk(T.ul, 1), ALU.add, ["#7", "ul1"], ["hout"])
-    dma("y", T.yh[:, :], T.hout[:, :], ["hout"], ())
+    tt(T.pp[:, :], bk(7), blk(T.ul, 0), ALU.add, ["#7", "ul1"], ["ppa", "ppb"])
+    dma("y", T.yh[:, :], T.pp[:, :], ["ppa", "ppb"], ())
     rest = [(s, v) for s, v in cnt.items() if max(seen[e].get(s, 0) for e in seen) < v]
     need("y", rest)

@@ -6,7 +6,6 @@ K2, K3, K4, H = 2 * K, 3 * K, 4 * K, K // 2
 F32, BF, I32, U16 = "float32", "bfloat16", "int32", "uint16"
 POS0 = 64
 CEN, INI = 192, -448.0
-PE_E = True
 
 SCRATCH = {
     "an32": ("sbuf", [128, 96], I32), "bn32": ("sbuf", [128, 6, 16], I32),
@@ -16,23 +15,22 @@ SCRATCH = {
     "wraw": ("sbuf", [128, K], BF), "yw": ("sbuf", [128, 4 * K3], BF),
     "fw": ("sbuf", [128, W + 3 * K3], F32), "bw": ("sbuf", [128, W + 3 * K3 + 3 * K4 + K2], F32),
     "mw": ("sbuf", [128, 4 * K3], F32), "db": ("sbuf", [128, 2 * K3], F32), "da": ("sbuf", [128, K3], F32),
-    "tb": ("sbuf", [128, 6 * K], F32), "su": ("sbuf", [128, 24], U16), "r2": ("sbuf", [128, 2 * 24], U16),
+    "tb": ("sbuf", [128, 6 * K], F32), "su": ("sbuf", [128, 24], U16), "b0c": ("sbuf", [128, K], F32),
     "nv": ("sbuf", [128, 3 * K3], F32), "va3": ("sbuf", [128, 3 * K], BF),
-    "ea": ("sbuf", [128, 5 * K2], F32), "eb": ("sbuf", [128, 4 * K2], F32), "pp": ("sbuf", [128, K], F32),
+    "ea": ("sbuf", [128, 4 * K2], F32), "eb": ("sbuf", [128, 4 * K2], F32), "pp": ("sbuf", [128, K], F32),
     "xs": ("sbuf", [128, K2], F32),
-    "t12": ("sbuf", [128, 2 * K2], F32), "ul": ("sbuf", [128, 3 * K], F32),
+    "t12": ("sbuf", [128, 3 * K2], F32), "ul": ("sbuf", [128, 3 * K], F32),
     "rt": ("sbuf", [128, W], F32), "pr": ("sbuf", [128, 6 * K2], F32), "pb": ("sbuf", [128, 6 * K], F32),
     "of1": ("sbuf", [128, 6 * 48], U16), "ofb": ("sbuf", [128, 12 * 24], U16), "fin": ("sbuf", [128, 96], U16),
     "rs": ("sbuf", [128, 4 * 24], U16), "rl": ("sbuf", [128, 16 * 24], U16),
     "sg": ("sbuf", [128, 400], BF), "ls": ("sbuf", [128, 400], BF), "nx": ("sbuf", [128, 400], BF), "gx": ("sbuf", [128, K], BF),
-    "sm": ("sbuf", [128, 2 * 24], F32), "sx": ("sbuf", [128, 2 * 24], BF), "lm": ("sbuf", [128, 8], F32),
+    "sm": ("sbuf", [128, 2 * 24], F32), "sx": ("sbuf", [128, 24], BF), "lm": ("sbuf", [128, 8], F32),
     "ip": ("sbuf", [128, 8], I32), "col": ("sbuf", [128, 8], F32),
-    "ones": ("sbuf", [128, 128], BF), "idb": ("sbuf", [128, 128], BF), "idf": ("sbuf", [128, 128], F32), "ni8": ("sbuf", [128, 128], F32),
-    "id2": ("sbuf", [128, 128], F32), "nib": ("sbuf", [128, 128], BF),
-    "e15": ("sbuf", [128, 144], F32), "ew": ("sbuf", [128, 144], F32), "e2": ("sbuf", [128, 144], F32), "ewd": ("sbuf", [128, 144], BF),
-    "bi": ("sbuf", [128, 128], I32), "be": ("sbuf", [128, 128], BF), "bo": ("sbuf", [128, 128], BF),
-    "d1i": ("sbuf", [128, 385], F32), "d1f": ("sbuf", [128, 385], F32), "d1r": ("sbuf", [128, 385], F32),
-    "cwi": ("sbuf", [128, 24], F32), "cw": ("sbuf", [128, 24], BF), "zb": ("sbuf", [128, 385], BF),
+    "idb": ("sbuf", [128, 128], BF), "idf": ("sbuf", [128, 128], F32), "ni8": ("sbuf", [128, 128], F32),
+    "id2": ("sbuf", [128, 128], F32), "nif": ("sbuf", [128, 128], F32), "nib": ("sbuf", [128, 128], BF),
+    "ew": ("sbuf", [128, 144], F32), "ewd": ("sbuf", [128, 144], BF), "be": ("sbuf", [128, 128], BF), "bo": ("sbuf", [128, 128], BF),
+    "d1f": ("sbuf", [128, 385], F32), "d1r": ("sbuf", [128, 385], F32),
+    "cwi": ("sbuf", [128, 24], F32), "cw": ("sbuf", [128, 24], BF), "at": ("sbuf", [128, 48], F32), "zb": ("sbuf", [128, 385], BF),
 }
 for _b in range(8):
     SCRATCH["b%d" % _b] = ("psum", [128, 512], F32)
@@ -50,14 +48,17 @@ def bits(engines):
     return m
 
 
-def spread(topo, cores, q):
+def spread(topo, cores, q, part=None):
     src = cores[q]
     eng = {t: topo.engines(src, cores[(q - t) % NR]) for t in (1, 2, 3)}
     common = [e for e in eng[1] if e in eng[2] and e in eng[3]]
     wide = [t for t in (1, 2, 3) if len(eng[t]) >= 2 * len(common)]
     calls = [[(t, common)] for t in (1, 2, 3) if t not in wide[:1]]
     if wide:
-        calls[0].append((wide[0], [e for e in eng[wide[0]] if e not in common][:len(common)]))
+        own = [e for e in eng[wide[0]] if e not in common][:len(common)]
+        if part is not None:
+            own = own[part * len(own) // 2:(part + 1) * len(own) // 2]
+        calls[0].append((wide[0], own))
     return calls
 
 
@@ -88,15 +89,13 @@ def rank_program(g, core, T, topo):
             out += [k + "a", k + "b"] if k[0] == "#" and len(k) == 2 else [k]
         return out
 
-    def deps(e, r, w):
+    def deps(e, r, w, dmaq=False):
         toks = []
         for k in r:
             if k in lastw:
                 toks.append(lastw[k])
         for k in w:
-            if k in lastw:
-                toks.append(lastw[k])
-            toks += reads.get(k, [])
+            toks += ([lastw[k]] if k in lastw else []) + reads.get(k, [])
         for k in r + w:
             if k[0] == "#":
                 toks += [t for o, t in bank.get(k[:2], {}).items() if o != e]
@@ -122,7 +121,7 @@ def rank_program(g, core, T, topo):
 
     def dma(e, out, in_, r=(), w=(), **kw):
         r, w = list(r), list(w)
-        deps(e, r, w)
+        deps(e, r, w, True)
         s = "d%d" % nd[0]
         nd[0] += 1
         Q[e].dma_start(out, in_, **kw).then_inc(T.sem[s], 16)
@@ -149,11 +148,13 @@ def rank_program(g, core, T, topo):
         lastw[key] = (sem, n)
         reads[key] = []
 
-    def to_hosts(src_of, dst_of, sem_of, rkeys, key_of):
-        for call in spread(topo, cores, q):
-            send([((q - t) % NR, eng, sem_of(t), [src_of(t)], dst_of(t)) for t, eng in call], rkeys)
-        for t in (1, 2, 3):
-            n = [len(eng) for call in spread(topo, cores, (q + t) % NR) for tt, eng in call if tt == t][0]
+    def to_hosts(src_of, dst_of, sem_of, rkeys, key_of, only=None, part=None):
+        for call in spread(topo, cores, q, part):
+            call = {None: call, "near": call[1:], "far": call[:1]}[only]
+            if call:
+                send([((q - t) % NR, eng, sem_of(t), [src_of(t)], dst_of(t)) for t, eng in call], rkeys)
+        for t in (1, 2, 3) if only != "near" else ():
+            n = [len(eng) for call in spread(topo, cores, (q + t) % NR, part) for tt, eng in call if tt == t][0]
             lands(key_of(t), sem_of(t), n)
 
     V, S, PE = g.vector, g.scalar, g.tensor
@@ -223,7 +224,7 @@ def rank_program(g, core, T, topo):
         return "n%d" % t
 
     ORDER = [0, 1, 2, 3, 2, 1, 0]
-    LBASE = [0, 0, 0, W, W + K3, W + 2 * K3]
+    LBASE = [0, 0, 0, W, W, W]
 
     def dpos(t):
         return W + 3 * K3 + K4 * (3 - t)
@@ -244,9 +245,9 @@ def rank_program(g, core, T, topo):
     def scat(k, part=None):
         t = ORDER[k]
         if part is None:
-            act(T.rt[:, :].indirect(names(t)), codes(k)[0], AF.Silu, codes(k)[1] + [nk(t), "rt"], ["rt"])
+            act(T.rt[:, :].indirect(names(t)), codes(k)[0], AF.Silu, codes(k)[1] + [nk(t)], ["rt"])
         else:
-            act(T.rt[:, :].indirect(names(t, 24 * part, 24 * part + 24)), blk(T.pb, 2 * (k % 3) + part), AF.Silu, codes(k)[1] + [nk(t), "rt"], ["rt"])
+            act(T.rt[:, :].indirect(names(t, 24 * part, 24 * part + 24)), blk(T.pb, 2 * (k % 3) + part), AF.Silu, codes(k)[1] + [nk(t)], ["rt"])
 
     def lvisit(li):
         return li + 1 if li < 3 else li - 3
@@ -301,18 +302,14 @@ def rank_program(g, core, T, topo):
         wrap(b, d, c, n * K, [ptab(rnd, li + i)[2] for i in range(n)])
 
     def convb(rnd, li, n, b):
-        for i in range(n):
-            o, k = offb(rnd, li + i)
-            conv(o, b, 24 * i, 24, LBASE[li + i], [k])
-
-    def rec(rnd, t):
-        return 4 if t == 0 and rnd % 2 == 1 else t
+        c = ((rnd - 1) * 6 + li) * 24
+        conv(T.ofb[:, c:c + 24 * n], b, 0, 24 * n, LBASE[li], [offb(rnd, li + i)[1] for i in range(n)])
 
     def EA(rnd, t, h=None):
-        return slot(T.ea, rec(rnd, t) * K2, 0, 2, h), "ea%d" % rec(rnd, t)
+        return slot(T.ea, t * K2, 0, 2, h), "ea%d" % t
 
     def Bof(rnd, t, h=None):
-        return slot(T.ea, rec(rnd, t) * K2, 1, 2, h), "B%d" % rec(rnd, t)
+        return slot(T.ea, t * K2, 1, 2, h), "B%d" % t
 
     def EB(t, h=None):
         return slot(T.eb, t * K2, 0, 2, h), "eb%d" % t
@@ -332,11 +329,14 @@ def rank_program(g, core, T, topo):
     def mw(t, s):
         return slot(T.mw, t * K3, s, 3)
 
-    def DB(t, s):
-        return slot(T.db, (t % 2) * K3, s, 3)
+    def C3(t):
+        return (mw(0, 0), ["c30"]) if t == 0 else (Aof(t)[0], hk(Aof(t)[1]))
 
-    def DA(s):
-        return slot(T.da, 0, s, 3)
+    def DB(t, s, h=None):
+        return slot(T.db, (t % 2) * K3, s, 3, h)
+
+    def DA(s, h=None):
+        return slot(T.da, 0, s, 3, h)
 
     TB = slot(T.tb, 0, 5, 6)
 
@@ -347,7 +347,7 @@ def rank_program(g, core, T, topo):
         return T.fw[:, 0:W + K3 * t], ["fth"] + ["o%s%d" % (s, i) for i in range(t) for s in "ab"]
 
     def bwin(t):
-        return T.bw[:, W + K3 * t:dpos(t)], ["di%d" % i for i in range(t, 3)] + ["do%s%d" % (s, i) for i in range(t + 1, 4) for s in "ab"]
+        return T.bw[:, W:dpos(t)], ["di%d" % i for i in range(3)] + ["do%s%d" % (s, i) for i in range(t + 1, 4) for s in "ab"]
 
     def douts(t):
         c = dpos(t)
@@ -363,119 +363,104 @@ def rank_program(g, core, T, topo):
             ["di%d" % t], accum_op=ALU.add)
 
     def back(rnd, t, out, key):
-        if rnd == 0:
+        if rnd == 0 and t > 1:
+            gcopy(out, TB, ["tb"], [key])
+        elif rnd == 0:
             act(out, TB, AF.Copy, ["tb"], [key])
         else:
             o, ko = perm(rnd, 1, t)
             gat("s", out, T.tb[:, :], o, ["tb", "tbz", ko], [key])
 
-    def pe_e(rnd):
-        return rnd == 2 and PE_E
-
     def loady(rnd, t):
-        if pe_e(rnd):
-            for h in (0, 1):
-                mm([(bk(h, H), T.nib[:, :], Y(t, h))], ["yw%d" % t, "nib"], ["#%d" % h], last=False)
-        else:
-            mm([(bk(0), T.idb[:, :], Y(t))], ["yw%d" % t, "idb"], ["#0"])
+        mm([(bk(0), T.idb[:, :], Y(t))], ["yw%d" % t, "idb"], ["#0"])
+        if rnd == 0 or t == 3:
+            mm([(bk(2), T.idb[:, :], NW(t))], ["yw%d" % t, "idb"], ["#2"])
+
+    def Pof(rnd, t, h=None):
+        if rnd == 2 and t < 2:
+            return slot(T.mw, t * K3, 1, 3, h), hk("p%d" % t, h)
+        return slot(T.pp, 0, 0, 1, h), hk("pp", h)
 
     def fgather(rnd, t, e):
         win, wk = fwin(t)
-        for h in (0, 1):
+        for h in ((0, 1) if e == "s" else (None,)):
             ob, kob = offb(rnd, t - 1, h)
             gat(e, Bof(rnd, t, h)[0], win, ob, wk + [kob], hk(Bof(rnd, t)[1], h))
         gat(e, Aof(t)[0], win, offa(t - 1)[0], wk + [offa(t - 1)[1]], hk(Aof(t)[1]))
 
     def mreal(t):
-        mm([(bk(2), T.id2[:, :], T.pp[:, :]), (bk(2), T.nib[:, :], Y(t))], ["id2", "nib", "ppa", "ppb", "yw%d" % t], ["#2"])
+        i = (7, 7, 5, 4)[t]
+        mm([(bk(i), T.id2[:, :], Pof(2, t)[0]), (bk(i), T.nib[:, :], Y(t))], ["id2", "nib", "yw%d" % t] + Pof(2, t)[1], ["#%d" % i])
 
-    def coef2(t):
-        tt(mw(t, 1), bk(2), NW(t), ALU.mult, ["#2", "yw%d" % t], ["m%d" % t])
-
-    def fwd(rnd, t, pin, mid=(None, None, None), tail=None, sfill=None, between=None, pfill=None, before_back=None):
+    def fwd(rnd, t, pin, mid=None, tail=None, sfill=None, between=None, pfill=None):
         (a, ka), (b, kb) = Aof(t), Bof(rnd, t)
         (ea, kea), (eb, keb) = EA(rnd, t), EB(t)
         kw = "yw%d" % t
         for h in (0, 1):
             x, y, r = pin(h)
-            tt(slot(T.pp, 0, 0, 1, h), x, y, ALU.mult, r, hk("pp", h))
-            if pe_e(rnd):
-                mm([(bk(h, H), T.idf[:, :], slot(T.pp, 0, 0, 1, h))], hk("pp", h) + ["idf"], ["#%d" % h], first=False)
-        if rnd == 2 and t > 0:
-            coef2(t - 1)
-        if t == 3 or rnd == 0:
-            mm([(bk(2), T.idb[:, :], NW(t))], [kw, "idb"], ["#2"])
+            tt(Pof(rnd, t, h)[0], x, y, ALU.mult, r, Pof(rnd, t, h)[1] + (["m%d" % t] if rnd == 2 and h == 0 else []))
         if t == 3:
-            for i in (6, 5):
+            for i in ((6, 5) if rnd == 2 else (5,)):
                 mm([(bk(i), T.idb[:, :], T.zb[:, 0:K])], ["idb", "zb"], ["#%d" % i], last=False)
         if pfill:
             pfill()
-        if rnd == 2 and t < 3:
+        if rnd == 2 and t > 1:
             mreal(t)
-        if pe_e(rnd):
-            e = [(bk(h, H), "#%d" % h) for h in (0, 1)]
-        else:
-            e = [(slot(B[1], 0, 0, 1, h), "#1" + "ab"[h]) for h in (0, 1)]
-            for h in (0, 1):
-                tt(e[h][0], slot(T.pp, 0, 0, 1, h), slot(B[0], 0, 0, 1, h), ALU.subtract, hk("pp", h) + ["#0"], [e[h][1]])
-        if mid[0]:
-            mid[0]()
         for h in (0, 1):
-            tt(EA(rnd, t, h)[0], e[h][0], Aof(t, h)[0], ALU.mult, [e[h][1]] + hk(ka, h), hk(kea, h))
-        if mid[1]:
-            mid[1]()
-        if pe_e(rnd):
+            tt(slot(B[1], 0, 0, 1, h), Pof(rnd, t, h)[0], slot(B[0], 0, 0, 1, h), ALU.subtract, Pof(rnd, t, h)[1] + ["#0"], hk("#1", h))
+        if mid:
+            mid()
+        if t == 3 and rnd < 2:
             for h in (0, 1):
-                tt(EB(t, h)[0], e[h][0], Bof(rnd, t, h)[0], ALU.mult, [e[h][1]] + hk(kb, h), hk(keb, h))
+                tt(EB(t, h)[0], slot(B[1], 0, 0, 1, h), Bof(rnd, t, h)[0], ALU.mult, hk("#1", h) + hk(kb, h), hk(keb, h))
+            tt(ea, bk(1), a, ALU.mult, ["#1"] + hk(ka), hk(kea))
         else:
+            for h in (0, 1):
+                tt(EA(rnd, t, h)[0], slot(B[1], 0, 0, 1, h), Aof(t, h)[0], ALU.mult, hk("#1", h) + hk(ka, h), hk(kea, h))
             tt(eb, bk(1), b, ALU.mult, ["#1"] + hk(kb), hk(keb))
-        if mid[2]:
-            mid[2]()
         if t == 3:
             vb, kvb = VBof(rnd)
-            sq = [(bk(0), "#0"), (bk(1), "#1")] if rnd == 2 else [(blk(T.xs, 0), "xs0"), (blk(T.xs, 1), "xs1")]
-            act(sq[0][0], b, AF.Square, hk(kb), [sq[0][1]])
+            sq = [(bk(0), "#0"), (bk(1), "#1")] if rnd == 2 else [(blk(T.xs, 0), "xs0"), (bk(0), "#0")]
             act(sq[1][0], a, AF.Square, hk(ka), [sq[1][1]])
+            act(sq[0][0], b, AF.Square, hk(kb), [sq[0][1]])
             if sfill:
                 sfill()
-            tt(bk(3), ea, bk(2), ALU.mult, ["#2"] + hk(kea), ["#3"])
-            tt(bk(4), eb, bk(2), ALU.mult, ["#2"] + hk(keb), ["#4"])
             if rnd == 2:
-                mreal(3)
-            tt(bk(6), b, bk(3), ALU.add, ["#3"] + hk(kb), ["#6"])
-            mm([(bk(6), T.nib[:, :], vb)], ["nib", kvb], ["#6"], first=False)
-            tt(bk(5), a, bk(4), ALU.add, ["#4"] + hk(ka), ["#5"])
-            mm([(bk(5), T.nib[:, :], blk(T.va3, 0))], ["nib", "va"], ["#5"], first=False)
-            if rnd == 2:
-                tt(b, bk(0), NW(3), ALU.mult, ["#0", kw], hk(kb))
-                act(b, b, AF.Identity, hk(kb), hk(kb), bias=1.0)
-                tt(a, bk(1), NW(3), ALU.mult, ["#1", kw], hk(ka))
-                act(a, a, AF.Identity, hk(ka), hk(ka), bias=1.0)
-                coef2(3)
+                tt(bk(6), ea, bk(2), ALU.mult, ["#2"] + hk(kea), ["#6"])
+                mm([(bk(6), T.idf[:, :], b), (bk(6), T.nib[:, :], vb)], ["idf", "nib", kvb] + hk(kb), ["#6"], first=False)
+                tt(bk(5), eb, bk(2), ALU.mult, ["#2"] + hk(keb), ["#5"])
+                mm([(bk(5), T.idf[:, :], a), (bk(5), T.nib[:, :], blk(T.va3, 0))], ["idf", "nib", "va"] + hk(ka), ["#5"], first=False)
+                c1, c3 = DB(3, 0), DB(3, 2)
+                tt(c3, bk(1), NW(3), ALU.mult, ["#1", kw], ["db1"])
+                act(c3, c3, AF.Identity, ["db1"], ["db1"], bias=1.0)
+                tt(c1, bk(0), NW(3), ALU.mult, ["#0", kw], hk("da1"))
+                act(c1, c1, AF.Identity, hk("da1"), hk("da1"), bias=1.0)
+                tt(mw(3, 1), bk(4), NW(3), ALU.mult, ["#4", kw], ["m3"])
             else:
-                act(DB(3, 2), bk(6), AF.Copy, ["#6"], ["db1"])
-                act(DB(3, 0), bk(5), AF.Copy, ["#5"], ["da1"])
+                tt(bk(4), eb, bk(2), ALU.mult, ["#2"] + hk(keb), ["#4"])
+                tt(bk(3), ea, bk(2), ALU.mult, ["#2"] + hk(kea), ["#3"])
+                tt(bk(5), a, bk(4), ALU.add, ["#4"] + hk(ka), ["#5"])
+                mm([(bk(5), T.nib[:, :], blk(T.va3, 0))], ["nib", "va"], ["#5"], first=False)
+                mm([(bk(6), T.idf[:, :], ea)], ["idf"] + hk(kea), ["#6"])
+                act(DB(3, 0), bk(5), AF.Copy, ["#5"], hk("da1"))
+                tt(bk(3), b, bk(3), ALU.add, ["#3"] + hk(kb), ["#3"])
                 tt(mw(3, 1), bk(1), T.pp[:, :], ALU.add, ["#1", "ppa", "ppb"], ["m3"])
+                tt(DB(3, 2), bk(3), vb, ALU.subtract, ["#3", kvb], ["db1"])
             if tail:
                 tail()
             return
-        if rnd > 0:
-            need("y", [lastw[keb + "b"]])
-            prefill(t)
         if rnd == 2:
             act(bk(3), b, AF.Square, hk(kb), ["#3"])
-            act(bk(4), a, AF.Square, hk(ka), ["#4"])
+            if t > 0:
+                act(bk(4), a, AF.Square, hk(ka), ["#4"])
         if sfill:
             sfill()
         zw = T.yw[:, t * K3 + K:(t + 1) * K3]
         c = W + K3 * t
-        r = rec(rnd, t)
         if rnd == 0:
             tt(bk(3), ea, bk(2), ALU.mult, ["#2"] + hk(kea), ["#3"])
         else:
-            scan(T.tb[:, 2::3], zw, T.ea[:, r * K2:(r + 1) * K2], [kw] + hk(kea) + hk(kb), ["tb"])
-            if before_back:
-                before_back()
+            scan(T.tb[:, 2::3], zw, T.ea[:, t * K2:(t + 1) * K2], [kw] + hk(kea) + hk(kb), ["tb"])
             back(rnd, t, T.fw[:, c + K2:c + K3], "ob%d" % t)
         if between:
             between()
@@ -486,7 +471,10 @@ def rank_program(g, core, T, topo):
             tail()
         if rnd == 2:
             tt(b, bk(3), NW(t), ALU.mult, ["#3", kw], hk(kb))
-            tt(a, bk(4), NW(t), ALU.mult, ["#4", kw], hk(ka))
+            if t > 0:
+                tt(a, bk(4), NW(t), ALU.mult, ["#4", kw], hk(ka))
+            if t == 2:
+                tt(mw(2, 1), bk(5), NW(2), ALU.mult, ["#5", kw], ["m2"])
         elif t > 0:
             tt(mw(t, 1), bk(1), T.pp[:, :], ALU.add, ["#1", "ppa", "ppb"], ["m%d" % t])
 
@@ -494,15 +482,27 @@ def rank_program(g, core, T, topo):
         win, wk = fwin(t)
         return lambda h: (win.indirect(offa(t - 1, h)[0]), Bof(rnd, t, h)[0], wk + [offa(t - 1)[1]] + hk(Bof(rnd, t)[1], h))
 
-    def bgather(rnd, t):
+    def bgather(rnd, t, mid=None):
         win, wk = bwin(t)
         p = t % 2
-        gat("s", DB(t, 0), win, offa(3 + t)[0], wk + [offa(3 + t)[1]], ["da%d" % p])
-        if t > 0 or rnd == 2:
-            ob, kob = offb(rnd, 3 + t)
-            gat("s", DB(t, 2), win, ob, wk + [kob], ["db%d" % p])
-        if t > 0 and rnd < 2:
-            gcopy(DA(2), DB(t, 0), ["da%d" % p], ["ca"])
+        ka, kb = "da%d" % p, "db%d" % p
+
+        def ga(h=None):
+            gat("s", DB(t, 0, h), win, offa(3 + t, h)[0], wk + [offa(3 + t)[1]], hk(ka, h))
+
+        def gb():
+            gat("s", DB(t, 2), win, offb(rnd, 3 + t)[0], wk + [offb(rnd, 3 + t)[1]], [kb])
+        if rnd == 2:
+            ga(0), ga(1)
+            if mid:
+                mid()
+            gb()
+        elif t > 0:
+            gb(), ga(0), ga(1)
+            if t > 1:
+                gcopy(DA(0), DB(t, 2), [kb], ["cb"])
+        else:
+            ga()
 
     def ubank(rnd, t):
         return (5, 6) if t == 3 or (t == 1 and rnd < 2) else (3, 4)
@@ -515,71 +515,86 @@ def rank_program(g, core, T, topo):
             mm([(bk(b2), m_[:, :], EA(rnd, t)[0])], [km] + hk(EA(rnd, t)[1]), ["#%d" % b2])
 
     def uprod(rnd, t):
-        p = t % 2
+        p, i = t % 2, (t - 1) % 3
         b1, b2 = ubank(rnd, t)
-        x1, x2 = ((EB(3)[0], hk("eb3")), (EA(rnd, 3)[0], hk("ea3"))) if t == 3 else ((DB(t, 0), ["da%d" % p]), (DB(t, 2), ["db%d" % p]))
-        tt(blk(T.t12, 2 * p), bk(b1), x1[0], ALU.mult, ["#%d" % b1] + x1[1], ["t1_%d" % p])
-        tt(blk(T.t12, 2 * p + 1), bk(b2), x2[0], ALU.mult, ["#%d" % b2] + x2[1], ["t2_%d" % p])
+        x1 = (EB(3)[0], hk("eb3")) if t == 3 else (DB(t, 0), hk("da%d" % p))
+        x2 = (EA(rnd, 3)[0], hk("ea3")) if t == 3 and rnd == 2 else (DB(t, 2), ["db%d" % p])
+        if t == 1 and rnd < 2:
+            tt(blk(T.t12, 1), bk(b2), x2[0], ALU.mult, ["#%d" % b2] + x2[1], ["t2_0"])
+            for h in (0, 1):
+                tt(slot(T.t12, 0, 0, 1, h), slot(B[b1], 0, 0, 1, h), DB(1, 0, h), ALU.mult, ["#%d" % b1] + hk("da1", h), hk("t1_0", h))
+        else:
+            tt(blk(T.t12, 2 * i), bk(b1), x1[0], ALU.mult, ["#%d" % b1] + x1[1], hk("t1_%d" % i))
+            tt(blk(T.t12, 2 * i + 1), bk(b2), x2[0], ALU.mult, ["#%d" % b2] + x2[1], ["t2_%d" % i])
         if t > 0:
             d = (q + t) % NR
-            send([(d, topo.engines(core, cores[d]), "u%d_%d" % (rnd, t), [blk(T.t12, 2 * p), blk(T.t12, 2 * p + 1)], blk(T.ul, t - 1))],
-                 ["t1_%d" % p, "t2_%d" % p], "lu%d" % t)
+            send([(d, topo.engines(core, cores[d]), "u%d_%d" % (rnd, t), [blk(T.t12, 2 * i), blk(T.t12, 2 * i + 1)], blk(T.ul, t - 1))],
+                 hk("t1_%d" % i) + ["t2_%d" % i], "lu%d" % t)
             lands("ul%d" % t, "u%d_%d" % (rnd, t), len(topo.engines(cores[(q - t) % NR], core)))
 
-    def bscan(rnd, t, early=None, sfill=None, tail=None, between=None):
+    def bscan(rnd, t, sfill=None, tail=None, between=None):
         p = t % 2
         ka, kb = "da%d" % p, "db%d" % p
         if t == 3:
-            tt(DB(t, 1), bk(6), blk(T.xs, 1), ALU.mult, ["#6", "xs1"], ["pb_%d" % p])
-            tt(DA(1), bk(5), blk(T.xs, 0), ALU.mult, ["#5", "xs0"], ["pa"])
-        else:
-            tt(DA(1), bk(0), DB(t, 0), ALU.mult, ["#0", ka], ["pa"])
-            tt(DB(t, 1), bk(1), DB(t, 2), ALU.mult, ["#1", kb], ["pb_%d" % p])
-        if t == 3:
+            tt(DB(t, 1), bk(0), DB(t, 2), ALU.mult, ["#0", kb], ["pb_%d" % p])
+            tt(DA(1), bk(5), blk(T.xs, 0), ALU.mult, ["#5", "xs0"], hk("pa"))
             gcopy(DA(0), DB(t, 2), [kb], ["cb"])
-            act(DA(2), DB(t, 0), AF.Copy, [ka], ["ca"])
+        elif t == 2:
+            tt(DB(t, 1), bk(1), DB(t, 2), ALU.mult, ["#1", kb], ["pb_%d" % p])
+            for h in (0, 1):
+                tt(DA(1, h), slot(B[0], 0, 0, 1, h), DB(t, 0, h), ALU.mult, ["#0"] + hk(ka, h), hk("pa", h))
         else:
-            act(DA(0), DB(t, 2), AF.Copy, [kb], ["cb"])
-        if early:
-            early()
+            uprod(rnd, 1)
+            if rnd == 0:
+                gcopy(DA(0), DB(t, 2), [kb], ["cb"])
+            else:
+                act(DA(0), DB(t, 2), AF.Copy, [kb], ["cb"])
+            tt(DB(t, 1), bk(1), DB(t, 2), ALU.mult, ["#1", kb], ["pb_%d" % p])
+            tt(DA(1), bk(0), DB(t, 0), ALU.mult, ["#0"] + hk(ka), hk("pa"))
+        act(DA(2), DB(t, 0), AF.Copy, hk(ka), ["ca"])
         m = T.mw[:, t * K3:(t + 1) * K3]
         km = ["m%d" % t, "mz", "mw%d" % t]
-        scan(T.tb[:, 1::2], m, T.db[:, p * K3:(p + 1) * K3], km + [ka, kb, "pb_%d" % p], ["tb"])
+        scan(T.tb[:, 1::2], m, T.db[:, p * K3:(p + 1) * K3], km + hk(ka) + [kb, "pb_%d" % p], ["tb"])
         if t > 1:
-            act(bk(0), Bof(rnd, t - 1)[0], AF.Square, hk(Bof(rnd, t - 1)[1]), ["#0"])
             act(bk(1), Aof(t - 1)[0], AF.Square, hk(Aof(t - 1)[1]), ["#1"])
+            act(bk(0), Bof(rnd, t - 1)[0], AF.Square, hk(Bof(rnd, t - 1)[1]), ["#0"])
         if sfill:
             sfill()
         back(rnd, t, douts(t)[1], "dob%d" % t)
         if between:
             between()
         c = dpos(t)
-        scan(T.bw[:, c:c + K3], m, T.da[:, :], km + ["ca", "cb", "pa"], ["doa%d" % t])
+        scan(T.bw[:, c:c + K3], m, T.da[:, :], km + ["ca", "cb"] + hk("pa"), ["doa%d" % t])
         if tail:
             tail()
 
     def breal(t):
         p = t % 2
         if t == 3:
-            (c1, k1), (c3, k3), c2 = Bof(2, 3), Aof(3), mw(3, 1)
-            tt(blk(T.xs, 1), bk(5), c2, ALU.mult, ["#5", "m3"], ["xs1"])
+            c1, c3, c2 = DB(3, 0), DB(3, 2), mw(3, 1)
+            tt(bk(3), bk(6), c3, ALU.mult, ["#6", "db1"], ["#3"])
             tt(bk(4), bk(6), c2, ALU.mult, ["#6", "m3"], ["#4"])
-            tt(bk(3), bk(6), c3, ALU.mult, ["#6"] + hk(k3), ["#3"])
-            tt(blk(T.xs, 0), bk(5), c1, ALU.mult, ["#5"] + hk(k1), ["xs0"])
+            tt(blk(T.xs, 1), bk(5), c2, ALU.mult, ["#5", "m3"], ["xs1"])
+            tt(blk(T.xs, 0), bk(5), c1, ALU.mult, ["#5"] + hk("da1"), ["xs0"])
             ba, bb = 4, 3
         else:
             da, db, ka, kb = DB(t, 0), DB(t, 2), "da%d" % p, "db%d" % p
-            tt(bk(5), bk(0), da, ALU.mult, ["#0", ka], ["#5"])
-            tt(blk(T.xs, 1), bk(2), da, ALU.mult, ["#2", ka], ["xs1"])
+            for h in (0, 1):
+                tt(slot(B[5], 0, 0, 1, h), slot(B[0], 0, 0, 1, h), DB(t, 0, h), ALU.mult, ["#0"] + hk(ka, h), ["#5" + "ab"[h]])
+            tt(blk(T.xs, 1), bk(2), da, ALU.mult, ["#2"] + hk(ka), ["xs1"])
             tt(bk(6), bk(1), db, ALU.mult, ["#1", kb], ["#6"])
             tt(blk(T.xs, 0), bk(2), db, ALU.mult, ["#2", kb], ["xs0"])
             ba, bb = 5, 6
+        if t == 3:
+            mm([(bk(2), T.idf[:, :], mw(2, 1))], ["idf", "m2"], ["#2"])
         if t > 0:
-            mm([(bk(2), T.idf[:, :], mw(t - 1, 1))], ["idf", "m%d" % (t - 1)], ["#2"])
             act(bk(0), Bof(2, t - 1)[0], AF.Identity, hk(Bof(2, t - 1)[1]), ["#0"], bias=1.0)
-            act(bk(1), Aof(t - 1)[0], AF.Identity, hk(Aof(t - 1)[1]), ["#1"], bias=1.0)
+            act(bk(1), C3(t - 1)[0], AF.Identity, C3(t - 1)[1], ["#1"], bias=1.0)
         tt(TB, bk(bb), blk(T.xs, 1), ALU.add, ["#%d" % bb, "xs1"], ["tb"])
         back(2, t, douts(t)[1], "dob%d" % t)
+        if t == 0:
+            tt(blk(T.t12, 4), bk(3), DB(0, 0), ALU.mult, ["#3"] + hk("da0"), hk("t1_2"))
+            mm([(bk(7), T.idf[:, :], blk(T.t12, 4))], ["idf"] + hk("t1_2"), ["#7"], first=False, last=False)
         tt(douts(t)[0], bk(ba), blk(T.xs, 0), ALU.add, ["#%d" % ba, "xs0"], ["doa%d" % t])
 
     def backward(rnd, fills):
@@ -588,109 +603,128 @@ def rank_program(g, core, T, topo):
             if t == 3:
                 uload(rnd, 2)
             if t == 1:
-                act(bk(4), blk(T.ul, 2), AF.Copy, ["ul3"], ["#4"], scale=-1.0)
-            bscan(rnd, t, early=(lambda: uprod(rnd, 1)) if t == 1 else None, sfill=sf, tail=tl, between=fills.get((t, "between")))
+                mm([(bk(4), T.nif[:, :], blk(T.ul, 2))], ["nif", "ul3"], ["#4"])
+            bscan(rnd, t, sfill=sf, tail=tl, between=fills.get((t, "between")))
             if t > 1:
                 bgather(rnd, t - 1)
                 uprod(rnd, t)
                 uload(rnd, t - 2)
-            else:
-                tt(bk(4), bk(4), blk(T.ul, 1), ALU.subtract, ["#4", "ul2"], ["#4"])
             if (t, "after") in fills:
                 fills[(t, "after")]()
 
     def wrapd(b, src, c0, cen, r):
         mm([(bk(b, 24), T.idb[:, :], cen)] + [(bk(b, 24), T.ewd[:, 15 - i:143 - i], src[:, c0 + i:c0 + K:16]) for i in range(16)],
-           list(r) + ["idb", "ewd"], ["#%d" % b])
+           list(r) + ["idb", "ewd"], ["#%d" % b], last=False)
 
-    def fix(rnd, k, b):
-        t_, x_ = T.sm[:, 24 * k:24 * k + 24], T.sx[:, 24 * k:24 * k + 24]
-        o, ko = perm(rnd, k, 0)
-        return [lambda: ts(t_, bk(b, 24), INI if k == 0 else -INI, ALU.is_equal, ["#%d" % b, "lm%d" % k], ["sm%d" % k], T.lm[:, 4 * k:4 * k + 1], ALU.mult),
-                lambda: tt(x_, bk(b, 24), t_, ALU.add, ["#%d" % b, "sm%d" % k], ["sx%d" % k]),
-                (lambda: ts(o, x_, float(CEN), ALU.add, ["sx%d" % k], [ko])) if k == 0 else
-                (lambda: ts(o, x_, 6.0, ALU.mult, ["sx%d" % k], [ko], 6.0 * CEN + 5, ALU.add))]
+    def ends(k):
+        ts(T.sm[:, 24 * k:24 * k + 24], T.at[:, 24 * k:24 * k + 24], T.lm[:, 4 - 4 * k:5 - 4 * k], ALU.is_equal, ["at%d" % k, "lm0", "lm1"],
+           ["sm%d" % k], T.lm[:, 4 * k:4 * k + 1], ALU.mult)
+
+    def wrapend(k, b):
+        mm([(bk(b, 24), T.idf[:, :], T.sm[:, 24 * k:24 * k + 24])], ["idf", "sm%d" % k], ["#%d" % b], first=False)
 
     def sendperm(rnd, k):
         o, ko = perm(rnd, k, 0)
+        if k == 0:
+            ts(o, bk(7, 24), float(CEN), ALU.add, ["#7"], [ko])
+        else:
+            ts(o, bk(3, 24), 6.0, ALU.mult, ["#3"], [ko], 6.0 * CEN + 5, ALU.add)
         to_hosts(lambda t: o, lambda t: perm(rnd, k, t)[0], lambda t: "r%d_%d_%d" % (rnd - 1, k, t), [ko], lambda t: perm(rnd, k, t)[1])
 
     def vote(rnd, sfill):
         win, wk = bwin(0)
         ob, kob = offb(rnd, 3)
-        mm([(bk(1, 385), T.idb[:, :], T.zb[:, :])], ["idb", "zb"], ["#1"], last=False)
-        if not pe_e(rnd + 1):
-            loady(rnd + 1, 0)
+        for h in (0, 1):
+            mm([(bk(1 + h, H + h), T.idb[:, :], T.zb[:, 0:H + h])], ["idb", "zb"], ["#%d" % (1 + h)], last=False)
+        loady(rnd + 1, 0)
         bgather(rnd, 0)
         sfill()
-        t2 = blk(T.t12, 1)
-        tt(t2, win.indirect(ob), EA(rnd, 0)[0], ALU.mult, wk + [kob] + hk(EA(rnd, 0)[1]), ["t2_0"])
-        tt(bk(3), bk(3), DB(0, 0), ALU.mult, ["#3", "da0"], ["#3"])
-        u0 = blk(T.t12, 0)
-        tt(bk(4), bk(4), blk(T.ul, 0), ALU.subtract, ["#4", "ul1"], ["#4"])
-        tt(u0, bk(3), t2, ALU.add, ["#3", "t2_0"], ["t1_0"])
-        tt(T.sg[:, 1:385], u0, bk(4), ALU.is_lt, ["#4", "t1_0"], ["sg"])
-        mm([(bk(1, 385), T.be[:, :], T.sg[:, 1:386]), (bk(1, 385), T.bo[:, :], T.sg[:, 0:385])], ["be", "bo", "sg"], ["#1"], first=False)
-        op("v", lambda: V.tensor_tensor_scan(T.ls[:, 0:385], bk(1, 385), T.d1f[:, :], INI, ALU.max, ALU.min), ["#1", "d1f"], ["ls"])
-        wrapd(7, T.ls, 0, T.cw[:, :], ["ls", "cw"])
-        op("v", lambda: V.tensor_tensor_scan(T.nx[:, 399:14:-1], B[1][:, 384::-1], T.d1r[:, ::-1], INI, ALU.max, ALU.min), ["#1", "d1r"], ["nx"])
-        if pe_e(rnd + 1):
-            loady(rnd + 1, 0)
+        t2 = blk(T.xs, 1)
+        tt(t2, win.indirect(ob), EA(rnd, 0)[0], ALU.mult, wk + [kob] + hk(EA(rnd, 0)[1]), ["xs1"])
+        for t in range(2):
+            prefill(t)
+        tt(bk(4), bk(4), blk(T.ul, 1), ALU.subtract, ["#4", "ul2"], ["#4"])
+        b3, b4 = [[slot(B[i], 0, 0, 1, h) for h in (0, 1)] for i in (3, 4)]
+        u0 = [slot(T.xs, 0, 0, 1, h) for h in (0, 1)]
+        for h in (0, 1):
+            tt(b3[h], b3[h], DB(0, 0, h), ALU.mult, hk("#3", h) + hk("da0", h), hk("#3", h))
+        for h in (0, 1):
+            tt(u0[h], b3[h], slot(T.xs, K, 0, 1, h), ALU.add, hk("#3", h) + ["xs1"], hk("u0", h) + ["xs0"][h:])
+        for h in (0, 1):
+            tt(b4[h], b4[h], slot(T.ul, 0, 0, 1, h), ALU.subtract, hk("#4", h) + ["ul1"], hk("#4", h))
+        for h in (0, 1):
+            lo, n = h * H, H + h
+            tt(T.sg[:, 1 + lo:1 + lo + H], u0[h], b4[h], ALU.is_lt, hk("#4", h) + hk("u0", h) + ["xs0"], hk("sg", h))
+            mm([(bk(1 + h, n), T.be[:, :], T.sg[:, 1 + lo:1 + lo + n]), (bk(1 + h, n), T.bo[:, :], T.sg[:, lo:lo + n])],
+               ["be", "bo"] + hk("sg")[:h + 1], ["#%d" % (1 + h)], first=False)
+
+        def vscan(out, d0, d1, ini, r, w):
+            op("v", lambda: V.tensor_tensor_scan(out, d0, d1, ini, ALU.max, ALU.min), r, w)
+        vscan(T.ls[:, 0:H], bk(1, H), T.d1f[:, 0:H], INI, ["#1", "d1f"], ["lsa"])
+        vscan(T.nx[:, 399:14 + H:-1], B[2][:, H::-1], T.d1r[:, 384:H - 1:-1], INI, ["#2", "d1r", "nx"], ["nxb"])
+        vscan(T.ls[:, H:385], bk(2, H + 1), T.d1f[:, H:385], T.ls[:, H - 1:H], ["#2", "d1f", "lsa"], ["ls"])
+        wrapd(7, T.ls, 0, T.cw[:, 0:24], ["ls", "lsa", "cw"])
+        vscan(T.nx[:, 14 + H:14:-1], B[1][:, H - 1::-1], T.d1r[:, H - 1::-1], T.nx[:, 15 + H:16 + H], ["#1", "d1r", "nxb"], ["nx"])
         ts(T.lm[:, 0:1], T.ls[:, 384:385], -INI, ALU.add, ["ls"], ["lm0"])
-        f = fix(rnd + 1, 0, 7)
-        f[0]()
         ts(T.lm[:, 4:5], T.nx[:, 15:16], -INI, ALU.add, ["nx"], ["lm1"], -1.0, ALU.mult)
-        f[1]()
-        ts(T.r2[:, rnd * 24:rnd * 24 + 24], T.sx[:, 0:24], 2.0, ALU.mult, ["sx0"], ["r2"], 2.0 * CEN + 1, ALU.add)
-        f[2]()
+        ends(0)
+        wrapend(0, 7)
+        ends(1)
+        if rnd == 0:
+            wrapd(3, T.nx, 16, T.cw[:, :], ["nx", "nxb", "cw"])
+        else:
+            gat("s", T.gx[:, :], T.nx[:, 16:400], T.su[:, :], ["nx", "nxb", "su"], ["gx"])
+            wrapd(3, T.gx, 0, T.sx[:, :], ["gx", "sx"])
+            tt(C3(0)[0], bk(5), NW(0), ALU.mult, ["#5", "yw0"], C3(0)[1])
+        wrapend(1, 3)
         sendperm(rnd + 1, 0)
 
     dma("s", T.an32[:, :], T.an[:, :], (), ["an32"])
     dma("y", T.bn32[:, :, :], T.bn[:, :], (), ["bn32"])
-    dma("y", T.thb[:, :], T.th[:, :], (), ["thb"])
-    dma("y", T.wraw[:, :], T.wt[:, :], (), ["wraw"])
+    dma("s", T.wraw[:, :], T.wt[:, :], (), ["wraw"])
     dma("y", Y(0), T.yt[:, :], (), ["y0"])
+    dma("y", T.thb[:, :], T.th[:, :], (), ["thb"])
     dma("y", T.vab[:, :], T.va[:, :], (), ["vab"])
     iota(T.ip[:, 0:1], [[0, 1]], 0, 1, ["ip"], fl=False)
     iota(T.rt[:, 0:K], [[1, K]], POS0, 0, ["rt0"])
-    ms(T.ones[:, :], 1.0, ["ones"])
-    ms(T.e15[:, :], 0.0, ["e15"])
-    op("g", lambda: g.affine_select(T.idb[:, :], T.ones[:, :], [[-1, 128]], ALU.is_equal, 0.0, 0, 1), ["ones"], ["idb"])
+    iota(T.rt[:, K2:W], [[1, K2]], POS0 + K2, 0, ["rt2"])
+    dma("g", T.fw[:, 0:W], T.th[:, :], (), ["fth"])
+    ms(T.ew[:, :], 0.0, ["ew"])
     ts(T.ip[:, 1:2], T.ip[:, 0:1], 4, ALU.logical_shift_right, ["ip"], ["ip1"], 1, ALU.bitwise_and)
     ts(T.ip[:, 2:3], T.ip[:, 0:1], 1, ALU.bitwise_and, ["ip"], ["ip2"])
     ts(T.ip[:, 3:4], T.ip[:, 0:1], 15, ALU.bitwise_and, ["ip"], ["ip3"])
-    ms(T.e15[:, 15::16], 1.0, ["e15"])
-    op("g", lambda: g.affine_select(T.ew[:, :], T.e15[:, :], [[1, 144]], ALU.is_equal, 0.0, -15, -1), ["e15"], ["ew"])
-    cp(T.col[:, 1:4], T.ip[:, 1:4], ["ip1", "ip2", "ip3"], ["col"])
     ms(T.zb[:, :], -33792.0, ["zb"])
-    ts(T.col[:, 0:1], T.col[:, 1:2], -1.0, ALU.mult, ["col"], ["col0"], 1.0, ALU.add)
-    ts(T.col[:, 4:5], T.col[:, 2:3], -1.0, ALU.mult, ["col"], ["col4"])
-    ms(T.sg[:, :], 0.0, ["sg"])
+    cp(T.col[:, 0:4], T.ip[:, 0:4], ["ip", "ip1", "ip2", "ip3"], ["col"])
     ms(slot(T.yw, K, 0, 2), 0.0, ["z0"])
-    cs_make(1)
-    act(T.rt[:, K:K2], T.rt[:, 0:K], AF.Silu, ["rt0"], ["rt1"], bias=float(K))
-    act(T.rt[:, K2:W], T.rt[:, 0:K2], AF.Identity, ["rt0", "rt1"], ["rt"], bias=float(K2))
+    ts(T.col[:, 5:6], T.col[:, 1:2], -1.0, ALU.mult, ["col"], ["col0"], 1.0, ALU.add)
+    ts(T.col[:, 4:5], T.col[:, 2:3], -1.0, ALU.mult, ["col"], ["col4"], float(-CEN - POS0 - dpos(0)), ALU.add)
+    ts(T.idb[:, :], T.rt[:, 0:128], float(-POS0), ALU.add, ["rt0", "col"], ["idb"], T.col[:, 0:1], ALU.is_equal)
+
+    def gsel(out, pat, cmp_, fill, base, cm, key):
+        op("g", lambda: g.affine_select(out, out, pat, cmp_, fill, base, cm), [key], [key])
+    act(T.pb[:, K:K2], T.rt[:, 0:K], AF.Silu, ["rt0"], ["pb1"], bias=float(W + K2))
     act(T.pb[:, 0:K], T.rt[:, 0:K], AF.Identity, ["rt0"], ["pb0"], scale=2.0, bias=float(W + 1 - POS0))
-    act(T.pb[:, K:K2], T.rt[:, 0:K], AF.Identity, ["rt0"], ["pb1"], bias=float(W + K2))
-    ts(T.x2[:, :, 0:16], T.bn32[:, :, :], T.col[:, 0:1], ALU.mult, ["bn32", "col0"], ["x2a"])
+    ts(T.rt[:, K:K2], T.rt[:, 0:K], float(K), ALU.add, ["rt0"], ["rt1"])
+    cp(T.ew[:, 15:143:16], T.idb[:, 0::16], ["idb", "ew"], ["ew"])
+    ts(T.x2[:, :, 0:16], T.bn32[:, :, :], T.col[:, 5:6], ALU.mult, ["bn32", "col0"], ["x2a"])
     ts(T.x2[:, :, 16:32], T.bn32[:, :, :], T.col[:, 1:2], ALU.mult, ["bn32", "col"], ["x2b"])
     cp(T.nm[:, :, 0:24], T.an32[:, :], ["an32"], ["nma"])
+    act(T.rt[:, :].indirect(names(0, 0, 24)), blk(T.pb, 0), AF.Silu, ["pb0", "pb1", "nma", "rt0", "rt1", "rt2"], ["rt"])
+    act(T.pb[:, K2:2 * K2], T.pb[:, 0:K2], AF.Identity, ["pb0", "pb1"], ["pb2", "pb3"], bias=float(K3))
     op("v", lambda: V.transpose(T.y2[:, :, :], T.x2[:, :, :]), ["x2a", "x2b"], ["y2"])
+    ts(NW(0), T.wraw[:, :], -0.125, ALU.mult, ["wraw", "y0", "z0"], ["yw0"])
     tt(T.z2[:, :, :], T.y2[:, :, 0:16], T.y2[:, :, 16:32], ALU.add, ["y2"], ["z2"])
+    ms(T.ewd[:, :], 0.0, ["ewd"])
     for c in range(6):
         cp(T.nm[:, :, 24 + c:48:6], T.z2[:, c, :], ["z2"] + (["nma"] if c == 5 else []), ["n0"] if c == 5 else ["nmb%d" % c])
+    tt(T.ewd[:, 15:143:16], T.idb[:, 1::16], T.idb[:, 0::16], ALU.subtract, ["idb", "ewd"], ["ewd"])
     to_hosts(lambda t: T.nm[:, t, :], lambda t: T.ntl[:, t, :], lambda t: "nm%d" % t, ["n0"], nk)
-    scat(0)
-    ts(NW(0), T.wraw[:, :], -0.125, ALU.mult, ["wraw", "y0", "z0"], ["yw0"])
-    dma("g", T.fw[:, 0:W], T.th[:, :], (), ["fth"])
+    scat(0, 1)
     to_hosts(lambda t: T.yw[:, 0:K3], lambda t: T.yw[:, t * K3:(t + 1) * K3], lambda t: "yw%d" % t, ["yw0"], lambda t: "yw%d" % t)
     cs_make(2)
-    for t in range(3):
+    cs_make(3)
+    for t in (0, 1, 2):
         iota(slot(T.nv, t * K3, 0, 2), [[0, K]], 0, 0, ["nvz%d" % t])
-    op("g", lambda: g.affine_select(T.e2[:, :], T.e15[:, :], [[1, 144]], ALU.is_equal, 0.0, -14, -1), ["e15"], ["e2"])
-    iota(T.bi[:, :], [[-16, 8], [0, 16]], 128, 1, ["bi"], fl=False)
-    iota(T.d1i[:, :], [[1, 385]], -CEN, 0, ["d1i"])
-    iota(T.cwi[:, :], [[16, 24]], -CEN, 0, ["cwi"])
 
     def negw(t):
         gcopy(mw(t, 2), NW(t), ["yw%d" % t], ["mw%d" % t])
@@ -704,95 +738,111 @@ def rank_program(g, core, T, topo):
     gptr(1)
     wrap1(0)
     loady(0, 1)
-    for t in range(3):
-        gat("v", slot(T.nv, t * K3, 1, 2), T.vab[:, :], names(t, 0, 24), ["vab", nk(t)], ["nva%d" % t], neg=True)
-        gat("v", T.nv[:, t * K3 + K2:(t + 1) * K3], T.vab[:, :], names(t, 24, 48), ["vab", nk(t)], ["nvb%d" % t], neg=True)
+    def nvmake(t, e):
+        gat(e, slot(T.nv, t * K3, 1, 2), T.vab[:, :], names(t, 0, 24), ["vab", nk(t)], ["nva%d" % t], neg=True)
+        gat(e, T.nv[:, t * K3 + K2:(t + 1) * K3], T.vab[:, :], names(t, 24, 48), ["vab", nk(t)], ["nvb%d" % t], neg=True)
         prefill(t)
-    cs_make(3)
-    accum(0)
+    nvmake(0, "v")
+    nvmake(1, "v")
+    nvmake(2, "v")
     ts(T.nib[:, :], T.idb[:, :], -1.0, ALU.mult, ["idb"], ["nib"])
-    cp(T.idf[:, :], T.idb[:, :], ["idb"], ["idf"])
     conv1(0)
+    cp(T.idf[:, :], T.idb[:, :], ["idb"], ["idf"])
     wrap1(1, 4)
     fgather(0, 1, "v")
     fwd(0, 1, pin_win(0, 1), tail=lambda: conv1(1, 4), sfill=lambda: (scat(2), gptr(2)))
     cs_make(4)
-    accum(1)
     cs_make(5)
+    accum(0)
+    iota(T.mw[:, K3::3], [[0, K3]], 0, 0, ["mz"])
+    accum(1)
+    negw(3)
     loady(0, 2)
     wrap1(2)
 
     scat(3)
     gptr(5)
-    scat(4)
+    scat(4, 0)
 
     def consts():
-        ts(T.bi[:, :], T.bi[:, :], 127, ALU.bitwise_and, ["bi"], ["bi"])
-        ts(T.be[:, :], T.bi[:, :], 32.0, ALU.is_lt, ["bi"], ["be"], 2048.0, ALU.mult)
-        ts(T.bo[:, :], T.bi[:, :], 32.0, ALU.is_lt, ["bi"], ["bo"], 2048.0, ALU.mult)
-        ms(T.be[:, 1::2], 0.0, ["be"])
-        ms(T.bo[:, 0::2], 0.0, ["bo"])
+        both = ((T.be, "be", 0), (T.bo, "bo", 1))
+        for m_, k, c in both:
+            iota(m_[:, :], [[0, 64], [2048 * (2 * c - 1), 2]], 2048 * (1 - c), 0, [k])
+        for m_, k, c in both:
+            gsel(m_[:, 0:112], [[-16, 7], [0, 16]], ALU.is_ge, 0.0, 0, 1, k)
+        for m_, k, c in both:
+            gsel(m_[:, 0:112], [[16, 7], [0, 16]], ALU.is_ge, 0.0, 31, -1, k)
+        for m_, k, c in both:
+            gsel(m_[0:112, 112:128], [[0, 16]], ALU.is_ge, 0.0, 15, -1, k)
+
+    def consts2():
+        iota(T.cwi[:, :], [[16, 24]], -CEN, 0, ["cwi"])
     fgather(0, 2, "v")
     fwd(0, 2, pin_win(0, 2), tail=lambda: conv1(2))
     gat("v", T.va3[:, 0:K2], T.vab[:, :], names(3), ["vab", "n3"], ["va", "vb0"])
-    iota(T.mw[:, K3::3], [[0, K3]], 0, 0, ["mz"])
     accum(2)
-    for t in (3, 2, 1):
-        negw(t)
+    negw(2)
+    consts2()
+    iota(T.sg[:, 384:400], [[0, 16]], 0, 0, ["sgb"])
+    iota(T.sg[:, 0:16], [[0, 16]], 0, 0, ["sga"])
     loady(0, 3)
     wrap1(5)
     fgather(0, 3, "s")
-    gptr(4)
-    fwd(0, 3, pin_win(0, 3), tail=lambda: (conv1(5), wrap1(4)), sfill=lambda: scat(5, 0))
+    scat(4, 1)
+    fwd(0, 3, pin_win(0, 3), tail=lambda: (conv1(5), wrap1(4)), sfill=lambda: gptr(4))
 
     def s3():
-        scat(5, 1)
+        scat(5, 0)
+        negw(1)
 
-    def a3():
-        gptr(3)
+    def t3():
         cs_make(6)
 
-    def a2():
-        for s_ in (0, 4):
-            iota(slot(T.tb, 0, s_, 6), [[0, K]], 0, 0, ["tbz"])
+    def a3():
+        scat(5, 1)
 
-    def v1():
-        consts()
-        tt(T.ewd[:, :], T.e2[:, :], T.ew[:, :], ALU.subtract, ["e2", "ew"], ["ewd"])
-        ts(T.cw[:, :], T.cwi[:, :], T.col[:, 3:4], ALU.add, ["cwi", "col"], ["cw"])
+    def s2():
+        act(T.nif[:, :], T.idb[:, :], AF.Copy, ["idb"], ["nif"], scale=-1.0)
+
+    def s1():
+        act(T.d1f[:, :], T.pb[:, 0:385], AF.Identity, ["pb0", "pb1", "col4"], ["d1f"], bias=T.col[:, 4:5])
+        act(T.cw[:, :], T.cwi[:, :], AF.Identity, ["cwi", "col"], ["cw"], bias=T.col[:, 3:4])
+        act(T.d1r[:, :], T.d1f[:, :], AF.Copy, ["d1f"], ["d1r"], scale=-1.0)
+        for k in (0, 1):
+            act(T.at[:, 24 * k:24 * k + 24], T.cw[:, :], AF.Identity, ["cw"], ["at%d" % k], bias=INI * (1 - 2 * k))
 
     def late():
-        act(T.d1f[:, :], T.d1i[:, :], AF.Identity, ["d1i", "col4"], ["d1f"], bias=T.col[:, 4:5])
-        act(T.d1r[:, :], T.d1f[:, :], AF.Copy, ["d1f"], ["d1r"], scale=-1.0)
-        scat(6)
-    backward(0, {3: (s3, None), (3, "after"): a3, (2, "between"): lambda: (conv1(4), wrap1(3)), (2, "after"): a2,
-                 (1, "between"): lambda: conv1(3), 1: (None, v1)})
+        s1()
+        for i, b in enumerate((7, 6, 5)):
+            c = slice(512 * i, 512 * i + 512)
+            mm([(bk(b, 512), T.idb[:, :], T.thb[:, c]), (bk(b, 512), T.nib[:, :], T.vab[:, c])], ["idb", "nib", "thb", "vab"], ["#%d" % b])
+            act(T.bw[:, c], bk(b, 512), AF.Copy, ["#%d" % b], ["dbase%d" % i])
+        gcopy(T.b0c[:, :], Bof(0, 0)[0], hk("B0"), ["b0c"])
+        for s_ in (0, 4):
+            iota(slot(T.tb, 0, s_, 6), [[0, K]], 0, 0, ["tbz"])
+        scat(6, 0)
+    backward(0, {3: (s3, t3), (3, "after"): a3, 2: (s2, None), (2, "between"): lambda: conv1(4),
+                 (2, "after"): lambda: (gptr(3), wrap1(3)), 1: (None, lambda: conv1(3)), (1, "between"): consts})
     vote(0, late)
 
     for rnd in (1, 2):
-        old = rec(rnd - 1, 0)
-        owin, ok = T.ea[:, old * K2:(old + 1) * K2], hk("B%d" % old) + hk("ea%d" % old) + ["r2"]
-        gat("s", Bof(rnd, 0)[0], owin, half(T.r2, (rnd - 1) * 24, None), ok, hk(Bof(rnd, 0)[1]))
-        if rnd == 1:
-            wrapd(3, T.nx, 16, T.cw[:, :], ["nx", "cw"])
-        else:
-            gat("s", T.gx[:, :], T.nx[:, 16:400], T.su[:, :], ["nx", "su"], ["gx"])
-        f = fix(rnd, 1, 3 if rnd == 1 else 7)
-
-        def last_fix(f=f, rnd=rnd):
-            f[2]()
-            sendperm(rnd, 1)
+        ok = ["b0c", perm(rnd, 0, 0)[1]]
+        gat("s", Bof(rnd, 0)[0], T.b0c[:, :], perm(rnd, 0, 0)[0], ok, hk("B0"))
 
         def pin0(h):
-            return owin.indirect(half(T.r2, (rnd - 1) * 24, h)), Aof(0, h)[0], ok + hk("A0", h)
+            return T.b0c[:, :].indirect(perm(rnd, 0, 0, h)[0]), Aof(0, h)[0], ok + hk("A0", h)
         if rnd == 1:
-            fwd(rnd, 0, pin0, mid=[f[0], f[1], last_fix], pfill=lambda: (wrap(4, T.rt, 0, W, ["rt"])))
+            scat(6, 1)
+            fwd(rnd, 0, pin0, mid=lambda: sendperm(1, 1),
+                tail=lambda: (cp(T.sx[:, :], bk(3, 24), ["#3"], ["sx"]), ts(T.su[:, :], bk(3, 24), float(CEN), ALU.add, ["#3"], ["su"])))
         else:
-            fwd(rnd, 0, pin0, pfill=lambda: wrapd(7, T.gx, 0, T.sx[:, 24:48], ["gx", "sx1"]), before_back=lambda: (f[0](), f[1](), last_fix()))
+            fwd(rnd, 0, pin0, mid=lambda: sendperm(2, 1), tail=lambda: convb(1, 0, 1, 6))
         accum(0)
-        if rnd == 2:
-            dma("g", T.bw[:, 0:W], T.thb[:, :], ["thb"], ["dbase"], accum_op=ALU.add)
+        need("y", [lastw["oa0"]])
+        prefill(2)
         loady(rnd, 1)
+        if rnd == 1:
+            wrap(4, T.rt, 0, W, ["rt"])
         win, wk = fwin(1)
         rho1, krho1 = perm(rnd, 0, 1)
         gat("s", blk(T.xs, 0), win, offb(rnd - 1, 0)[0], wk + [offb(rnd - 1, 0)[1]], ["xs0"])
@@ -800,58 +850,62 @@ def rank_program(g, core, T, topo):
             gat("v", Aof(1)[0], win, offa(0)[0], wk + ["la0"], hk("A1"))
         else:
             for h in (0, 1):
-                gat("s", Aof(1, h)[0], win, offa(0, h)[0], wk + ["la0"], hk("A1", h))
+                gat("vs"[h], Aof(1, h)[0], win, offa(0, h)[0], wk + ["la0"], hk("A1", h))
         pupd(rnd, 1)
         gat("s", Bof(rnd, 1)[0], blk(T.xs, 0), rho1, ["xs0", krho1], hk("B1"))
         if rnd == 1:
             pupd(rnd, 2)
             pupd(rnd, 3)
         fwd(rnd, 1, lambda h: (blk(T.xs, 0).indirect(perm(rnd, 0, 1, h)[0]), Aof(1, h)[0], ["xs0", krho1] + hk("A1", h)),
-            pfill=lambda: wrapb(rnd, 1, 1, 7), tail=lambda: convb(rnd, 1, 1, 7),
-            between=(lambda: conv(T.fin[:, :], 4, 0, 96, 0, ["fin"])) if rnd == 1 else None)
+            pfill=lambda: wrapb(rnd, 1, 1, 7), tail=lambda: (convb(rnd, 1, 1, 7), rnd == 1 and conv(T.fin[:, :], 4, 0, 96, 0, ["fin"])), sfill=(lambda: pupd(2, 2)) if rnd == 2 else None)
         accum(1)
         loady(rnd, 2)
         fgather(rnd, 2, "s")
-        for li in ((4, 5) if rnd == 1 else (2, 3)):
+        for li in (4, 5):
             pupd(rnd, li)
-        fwd(rnd, 2, pin_win(rnd, 2), pfill=lambda: wrapb(rnd, 2, 1, 7), between=(lambda: convb(rnd, 2, 1, 7)) if rnd == 1 else None,
-            tail=(lambda: convb(rnd, 2, 1, 7)) if rnd == 2 else None)
+        fwd(rnd, 2, pin_win(rnd, 2), pfill=lambda: wrapb(rnd, 2, 1, 7), **{"between" if rnd == 1 else "tail": lambda: convb(rnd, 2, 1, 7)})
         accum(2)
         loady(rnd, 3)
         fgather(rnd, 3, "s")
         o, ko = perm(rnd, 0, 3)
         gat("s", VBof(rnd)[0], VBof(rnd - 1)[0], o, [VBof(rnd - 1)[1], ko], [VBof(rnd)[1]])
         if rnd == 2:
-            pupd(rnd, 4)
-            pupd(rnd, 5)
+            pupd(2, 3)
             fwd(rnd, 3, pin_win(rnd, 3))
             wrapb(rnd, 3, 3, 7)
         else:
             fwd(rnd, 3, pin_win(rnd, 3), pfill=lambda: wrapb(1, 3, 3, 7), tail=lambda: convb(1, 3, 3, 7), sfill=lambda: pupd(1, 0))
 
             def g1():
-                convb(1, 0, 1, 7)
-                ts(T.su[:, :], T.sx[:, 24:48], float(CEN), ALU.add, ["sx1"], ["su"])
+                act(T.at[:, 24:48], T.sx[:, :], AF.Identity, ["sx"], ["at1"], bias=-INI)
                 act(T.ni8[:, :], T.idf[:, :], AF.Copy, ["idf"], ["ni8"], scale=-0.125)
                 act(T.id2[:, :], T.idf[:, :], AF.Copy, ["idf"], ["id2"], scale=2.0)
-            backward(rnd, {(3, "after"): lambda: wrapb(1, 0, 1, 7), (1, "between"): g1})
-            vote(rnd, lambda: act(T.bw[:, 0:W], T.vab[:, :], AF.Copy, ["vab"], ["dbase"], scale=-1.0))
+                wrapb(1, 0, 1, 6)
+            backward(rnd, {(1, "between"): g1})
+
+            def late2():
+                gcopy(T.b0c[:, :], Bof(1, 0)[0], hk("B0"), ["b0c"])
+                act(bk(5), Aof(0)[0], AF.Square, hk("A0"), ["#5"])
+            vote(rnd, late2)
 
     for t in (3, 2, 1, 0):
         if t == 0:
-            mm([(bk(7), T.ni8[:, :], blk(T.ul, i - 1)) for i in (3, 2)], ["ni8", "ul3", "ul2"], ["#7"])
+            mm([(bk(7), T.ni8[:, :], blk(T.ul, i - 1)) for i in (3, 2)], ["ni8", "ul3", "ul2"], ["#7"], last=False)
+        elif t < 3:
+            mreal(t - 1)
         breal(t)
         if t == 3:
-            convb(2, 3, 3, 7)
-        if t > 0:
+            bgather(2, 2, lambda: (uprod(2, 3), convb(2, 3, 3, 7)))
+        elif t > 0:
             bgather(2, t - 1)
-        uprod(2, t)
+            uprod(2, t)
+            tt(bk(2), bk(7), NW(t - 1), ALU.mult, ["#7", "yw%d" % (t - 1)], ["#2"])
         if t > 0:
             uload(2, t - 1)
-    tt(bk(7), bk(7), blk(T.t12, 0), ALU.add, ["#7", "t1_0"], ["#7"])
-    tt(bk(7), bk(7), blk(T.t12, 1), ALU.add, ["#7", "t2_0"], ["#7"])
-    wk = ["dbase"] + ["di%d" % i for i in range(3)] + ["do%s%d" % (s, i) for i in range(4) for s in "ab"] + ["fin"]
-    for e, lo, hi in (("s", 0, 640), ("v", 1280, W), ("s", 640, 1280)):
+    tt(blk(T.t12, 5), bk(4), DB(0, 2), ALU.mult, ["#4", "db0"], ["t2_2"])
+    mm([(bk(7), T.idf[:, :], blk(T.t12, 5))], ["idf", "t2_2"], ["#7"], first=False)
+    wk = ["%s%d" % (s, i) for s in ("dbase", "di") for i in range(3)] + ["do%s%d" % (s, i) for i in range(4) for s in "ab"] + ["fin"]
+    for e, lo, hi in (("s", 0, 448), ("v", 896, W), ("s", 448, 896)):
         gat(e, T.fw[:, lo:hi], T.bw[:, :], T.fin[:, lo // 16:hi // 16], wk, ["out%d" % lo] + (["fth"] if lo == 0 else []))
         dma("y", T.yd[:, lo:hi], T.fw[:, lo:hi], ["out%d" % lo], ())
     tt(T.pp[:, :], bk(7), blk(T.ul, 0), ALU.add, ["#7", "ul1"], ["ppa", "ppb"])

from concourse.bass import DstId, RemoteDMATransfer
from concourse.mybir import AluOpType as ALU, ActivationFunctionType as AF

K, W, NR = 384, 1536, 4
K2, K3, K4, H = 2 * K, 3 * K, 4 * K, K // 2
F32, BF, I32, U16 = "float32", "bfloat16", "int32", "uint16"
POS0 = 64
CEN, INI = 192, -448.0

SCRATCH = {
    "an32": ("sbuf", [128, 96], I32), "bn32": ("sbuf", [128, 6, 16], I32),
    "x2": ("sbuf", [128, 6, 32], F32), "y2": ("sbuf", [128, 6, 32], F32), "z2": ("sbuf", [128, 6, 16], F32),
    "nm": ("sbuf", [128, 4, 48], U16), "ntl": ("sbuf", [128, 4, 48], U16),
    "thb": ("sbuf", [128, W], BF), "vab": ("sbuf", [128, W], BF),
    "wraw": ("sbuf", [128, K], BF), "yw": ("sbuf", [128, 4 * K3], BF),
    "fw": ("sbuf", [128, W + 3 * K3], F32), "bw": ("sbuf", [128, W + 3 * K3 + 3 * K4 + K2], F32),
    "mw": ("sbuf", [128, 4 * K3], F32), "db": ("sbuf", [128, 2 * K3], F32), "da": ("sbuf", [128, K3], F32),
    "tb": ("sbuf", [128, 6 * K], F32), "su": ("sbuf", [128, 24], U16), "b0c": ("sbuf", [128, K], F32),
    "nv": ("sbuf", [128, 3 * K3], F32), "va3": ("sbuf", [128, 3 * K], BF),
    "ea": ("sbuf", [128, 4 * K2], F32), "eb": ("sbuf", [128, 4 * K2], F32), "pp": ("sbuf", [128, K], F32),
    "xs": ("sbuf", [128, K2], F32),
    "t12": ("sbuf", [128, 3 * K2], F32), "ul": ("sbuf", [128, 3 * K], F32),
    "rt": ("sbuf", [128, W], F32), "pr": ("sbuf", [128, 6 * K2], F32), "pb": ("sbuf", [128, 6 * K], F32),
    "of1": ("sbuf", [128, 6 * 48], U16), "ofb": ("sbuf", [128, 12 * 24], U16), "fin": ("sbuf", [128, 96], U16),
    "rs": ("sbuf", [128, 4 * 24], U16), "rl": ("sbuf", [128, 16 * 24], U16),
    "sg": ("sbuf", [128, 400], BF), "ls": ("sbuf", [128, 400], BF), "nx": ("sbuf", [128, 400], BF), "gx": ("sbuf", [128, K], BF),
    "sm": ("sbuf", [128, 2 * 24], F32), "sx": ("sbuf", [128, 24], BF), "lm": ("sbuf", [128, 8], F32),
    "ip": ("sbuf", [128, 8], I32), "col": ("sbuf", [128, 8], F32),
    "idb": ("sbuf", [128, 128], BF), "idf": ("sbuf", [128, 128], F32), "ni8": ("sbuf", [128, 128], F32),
    "id2": ("sbuf", [128, 128], F32), "nif": ("sbuf", [128, 128], F32), "nib": ("sbuf", [128, 128], BF),
    "ew": ("sbuf", [128, 144], F32), "ewd": ("sbuf", [128, 144], BF), "be": ("sbuf", [128, 128], BF), "bo": ("sbuf", [128, 128], BF),
    "d1f": ("sbuf", [128, 385], F32), "d1r": ("sbuf", [128, 385], F32),
    "cwi": ("sbuf", [128, 24], F32), "cw": ("sbuf", [128, 24], BF), "at": ("sbuf", [128, 48], F32), "zb": ("sbuf", [128, 385], BF),
}
for _b in range(8):
    SCRATCH["b%d" % _b] = ("psum", [128, 512], F32)

SEMAPHORES = (["cv", "cs_", "cp", "cg", "loc", "lu1", "lu2", "lu3"] + ["d%d" % i for i in range(48)]
              + ["nm%d" % t for t in (1, 2, 3)] + ["yw%d" % t for t in (1, 2, 3)]
              + ["u%d_%d" % (r, t) for r in range(3) for t in (1, 2, 3)]
              + ["r%d_%d_%d" % (r, k, t) for r in range(2) for k in range(2) for t in (1, 2, 3)])


def bits(engines):
    m = 0
    for e in engines:
        m |= 1 << e
    return m


def spread(topo, cores, q, part=None):
    src = cores[q]
    eng = {t: topo.engines(src, cores[(q - t) % NR]) for t in (1, 2, 3)}
    common = [e for e in eng[1] if e in eng[2] and e in eng[3]]
    wide = [t for t in (1, 2, 3) if len(eng[t]) >= 2 * len(common)]
    calls = [[(t, common)] for t in (1, 2, 3) if t not in wide[:1]]
    if wide:
        own = [e for e in eng[wide[0]] if e not in common][:len(common)]
        if part is not None:
            own = own[part * len(own) // 2:(part + 1) * len(own) // 2]
        calls[0].append((wide[0], own))
    return calls


def rank_program(g, core, T, topo):
    q = T.rank_of(core)
    if q is None:
        return
    cores = list(T.cores)
    Q = {"v": g.vector, "s": g.scalar, "p": g.tensor, "g": g, "y": g.sync}
    CS = {"v": "cv", "s": "cs_", "p": "cp", "g": "cg"}
    cnt = {}
    seen = {e: {} for e in Q}
    lastw, reads, bank = {}, {}, {}
    nd = [0]

    def need(e, toks):
        best = {}
        for s, v in toks:
            best[s] = max(best.get(s, 0), v)
        for s, v in best.items():
            if seen[e].get(s, 0) < v:
                Q[e].wait_ge(T.sem[s], v)
                seen[e][s] = v

    def halves(keys):
        out = []
        for k in keys:
            out += [k + "a", k + "b"] if k[0] == "#" and len(k) == 2 else [k]
        return out

    def deps(e, r, w, dmaq=False):
        toks = []
        for k in r:
            if k in lastw:
                toks.append(lastw[k])
        for k in w:
            toks += ([lastw[k]] if k in lastw else []) + reads.get(k, [])
        for k in r + w:
            if k[0] == "#":
                toks += [t for o, t in bank.get(k[:2], {}).items() if o != e]
        need(e, toks)

    def done(e, tok, r, w):
        for k in r:
            reads.setdefault(k, []).append(tok)
        for k in w:
            lastw[k] = tok
            reads[k] = []
        for k in r + w:
            if k[0] == "#":
                bank.setdefault(k[:2], {})[e] = tok

    def op(e, fn, r=(), w=()):
        r, w = halves(r), halves(w)
        deps(e, r, w)
        s = CS[e]
        fn().then_inc(T.sem[s], 1)
        cnt[s] = cnt.get(s, 0) + 1
        done(e, (s, cnt[s]), r, w)

    def dma(e, out, in_, r=(), w=(), **kw):
        r, w = list(r), list(w)
        deps(e, r, w, True)
        s = "d%d" % nd[0]
        nd[0] += 1
        Q[e].dma_start(out, in_, **kw).then_inc(T.sem[s], 16)
        cnt[s] = 16
        done(e, (s, 16), r, w)

    def send(trs, r, lsem="loc"):
        deps("g", list(r), [])
        ts = []
        for d, eng, sem, srcs, dst in trs:
            rid, pid = topo.addr(cores[d], core)
            kw = dict(dst_ids=[DstId(rid=rid, pnc=pid)], dma_engine_mask=bits(eng), remote_sem=T.sem[sem])
            if len(srcs) == 1:
                ts.append(RemoteDMATransfer(src=srcs[0], dst=dst, **kw))
            else:
                ts.append(RemoteDMATransfer(srcs=srcs, dsts=[dst], alu_op=1, **kw))
            cnt[lsem] = cnt.get(lsem, 0) + len(eng)
        g.remote_dma_fused(ts, local_sem=T.sem[lsem])
        if lsem != "loc":
            done("g", (lsem, cnt[lsem]), list(r), [])

    def lands(key, sem, n):
        cnt[sem] = n
        lastw[key] = (sem, n)
        reads[key] = []

    def to_hosts(src_of, dst_of, sem_of, rkeys, key_of, only=None, part=None):
        for call in spread(topo, cores, q, part):
            call = {None: call, "near": call[1:], "far": call[:1]}[only]
            if call:
                send([((q - t) % NR, eng, sem_of(t), [src_of(t)], dst_of(t)) for t, eng in call], rkeys)
        for t in (1, 2, 3) if only != "near" else ():
            n = [len(eng) for call in spread(topo, cores, (q + t) % NR, part) for tt, eng in call if tt == t][0]
            lands(key_of(t), sem_of(t), n)

    V, S, PE = g.vector, g.scalar, g.tensor
    B = [T["b%d" % i] for i in range(8)]

    def bk(i, n=K):
        return B[i][:, 0:n]

    def blk(t, i, n=K):
        return t[:, i * K:i * K + n]

    def slot(t, c0, s, r, h=None):
        lo, hi = (0, K) if h is None else (h * H, (h + 1) * H)
        return t[:, c0 + s + r * lo:c0 + r * hi:r]

    def tt(out, a, b, o, r, w):
        op("v", lambda: V.tensor_tensor(out, a, b, o), r, w)

    def ts(out, a, s1, o0, r, w, s2=None, o1=None):
        if o1 is None:
            op("v", lambda: V.tensor_scalar(out, a, s1, None, o0), r, w)
        else:
            op("v", lambda: V.tensor_scalar(out, a, s1, s2, o0, o1), r, w)

    def cp(out, a, r, w):
        op("v", lambda: V.tensor_copy(out, a), r, w)

    def ms(ap, c, w):
        op("v", lambda: V.memset(ap, c), (), w)

    def scan(out, d0, d1, r, w):
        op("v", lambda: V.tensor_tensor_scan(out, d0, d1, 0.0, ALU.mult, ALU.add), r, w)

    def act(out, a, f, r, w, **kw):
        op("s", lambda: S.activation(out, a, f, **kw), r, w)

    def gat(e, out, win, off, r, w, neg=False):
        a = win.indirect(off)
        if e == "s":
            act(out, a, AF.Copy, r, w, **({"scale": -1.0} if neg else {}))
        elif neg:
            ts(out, a, -1.0, ALU.mult, r, w)
        else:
            cp(out, a, r, w)

    def mm(items, r, w, first=True, last=True):
        def f():
            ins = None
            for i, (o, l, x) in enumerate(items):
                ins = PE.matmul(o, l, x, first and i == 0, last and i == len(items) - 1)
            return ins
        op("p", f, r, w)

    def iota(out, pat, base, cm, w, fl=True):
        if fl:
            op("g", lambda: g.iota(out, pat, base, cm, allow_small_or_imprecise_dtypes=True), (), w)
        else:
            op("g", lambda: g.iota(out, pat, base, cm), (), w)

    def gcopy(out, a, r, w):
        op("g", lambda: g.affine_select(out, a, [[0, K]], ALU.is_ge, 0.0, 0, 0), r, w)

    def names(t, lo=0, hi=48):
        return (T.nm if t == 0 else T.ntl)[:, t, lo:hi]

    def nk(t):
        return "n%d" % t

    ORDER = [0, 1, 2, 3, 2, 1, 0]
    LBASE = [0, 0, 0, W, W, W]

    def dpos(t):
        return W + 3 * K3 + K4 * (3 - t)

    def codes(k):
        i = k % 3
        return T.pb[:, i * K2:(i + 1) * K2], ["pb%d" % (2 * i), "pb%d" % (2 * i + 1)]

    def cs_make(k):
        c, key = (k % 3) * K2, codes(k)[1]
        if k == 6:
            iota(T.pb[:, c:c + K2], [[1, K2]], POS0 + dpos(0), 0, key)
            return
        r, base = (2, W + K3 * k) if k < 3 else (3, dpos(6 - k))
        iota(T.pb[:, c:c + K], [[r, K]], POS0 + base + r - 1, 0, key[:1])
        iota(T.pb[:, c + K:c + K2], [[1, K]], POS0 + base + r * K, 0, key[1:])

    def scat(k, part=None):
        t = ORDER[k]
        if part is None:
            act(T.rt[:, :].indirect(names(t)), codes(k)[0], AF.Silu, codes(k)[1] + [nk(t)], ["rt"])
        else:
            act(T.rt[:, :].indirect(names(t, 24 * part, 24 * part + 24)), blk(T.pb, 2 * (k % 3) + part), AF.Silu, codes(k)[1] + [nk(t)], ["rt"])

    def lvisit(li):
        return li + 1 if li < 3 else li - 3

    def gptr(li):
        t = lvisit(li)
        gat("s", T.pr[:, li * K2:(li + 1) * K2], T.rt[:, :], names(t), ["rt", nk(t)], ["pr%d" % (2 * li), "pr%d" % (2 * li + 1)])

    def wrap(b, src, c0, n, r):
        mm([(bk(b, n // 16), T.ew[:, 15 - i:143 - i], src[:, c0 + i:c0 + n:16]) for i in range(16)], list(r) + ["ew"], ["#%d" % b])

    def conv(out, b, c0, n, base, w):
        ts(out, B[b][:, c0:c0 + n], 0.25 - POS0 - base, ALU.add, ["#%d" % b], w)

    def wrap1(li, b=7):
        wrap(b, T.pr, li * K2, K2, ["pr%d" % (2 * li), "pr%d" % (2 * li + 1)])

    def conv1(li, b=7):
        conv(T.of1[:, li * 48:li * 48 + 48], b, 0, 48, LBASE[li], ["la%d" % li, "lb0_%d" % li])

    def half(t, c, h):
        return t[:, c:c + 24] if h is None else t[:, c + 12 * h:c + 12 * h + 12]

    def offa(li, h=None):
        return half(T.of1, li * 48, h), "la%d" % li

    def offb(rnd, li, h=None):
        if rnd == 0:
            return half(T.of1, li * 48 + 24, h), "lb0_%d" % li
        return half(T.ofb, ((rnd - 1) * 6 + li) * 24, h), "lb%d_%d" % (rnd, li)

    def perm(rnd, k, t, h=None):
        if t == 0:
            return half(T.rs, ((rnd - 1) * 2 + k) * 24, h), "rs%d_%d" % (rnd, k)
        return half(T.rl, (((rnd - 1) * 2 + k) * 4 + t) * 24, h), "rl%d_%d_%d" % (rnd, k, t)

    def ptab(rnd, li):
        if rnd == 0:
            return T.pr, (2 * li + 1) * K, "pr%d" % (2 * li + 1)
        if rnd == 1:
            return T.pb, li * K, "pb%d" % li
        return T.pr, li * K, "pr%d" % li

    def pupd(rnd, li):
        s, c, k = ptab(rnd - 1, li)
        d, c2, k2 = ptab(rnd, li)
        o, ko = perm(rnd, 0, lvisit(li))
        gat("s", d[:, c2:c2 + K], s[:, c:c + K], o, [k, ko], [k2])

    def wrapb(rnd, li, n, b):
        d, c, k = ptab(rnd, li)
        wrap(b, d, c, n * K, [ptab(rnd, li + i)[2] for i in range(n)])

    def convb(rnd, li, n, b):
        c = ((rnd - 1) * 6 + li) * 24
        conv(T.ofb[:, c:c + 24 * n], b, 0, 24 * n, LBASE[li], [offb(rnd, li + i)[1] for i in range(n)])

    def EA(rnd, t, h=None):
        return slot(T.ea, t * K2, 0, 2, h), "ea%d" % t

    def Bof(rnd, t, h=None):
        return slot(T.ea, t * K2, 1, 2, h), "B%d" % t

    def EB(t, h=None):
        return slot(T.eb, t * K2, 0, 2, h), "eb%d" % t

    def Aof(t, h=None):
        return slot(T.eb, t * K2, 1, 2, h), "A%d" % t

    def hk(k, h=None):
        return [k + "a", k + "b"] if h is None else [k + "ab"[h]]

    def Y(t, h=None):
        return slot(T.yw, t * K3, 0, 1, h)

    def NW(t):
        return slot(T.yw, t * K3 + K, 1, 2)

    def mw(t, s):
        return slot(T.mw, t * K3, s, 3)

    def C3(t):
        return (mw(0, 0), ["c30"]) if t == 0 else (Aof(t)[0], hk(Aof(t)[1]))

    def DB(t, s, h=None):
        return slot(T.db, (t % 2) * K3, s, 3, h)

    def DA(s, h=None):
        return slot(T.da, 0, s, 3, h)

    TB = slot(T.tb, 0, 5, 6)

    def VBof(rnd):
        return blk(T.va3, 1 + rnd % 2), "vb%d" % (rnd % 2)

    def fwin(t):
        return T.fw[:, 0:W + K3 * t], ["fth"] + ["o%s%d" % (s, i) for i in range(t) for s in "ab"]

    def bwin(t):
        return T.bw[:, W:dpos(t)], ["di%d" % i for i in range(3)] + ["do%s%d" % (s, i) for i in range(t + 1, 4) for s in "ab"]

    def douts(t):
        c = dpos(t)
        if t == 0:
            return T.bw[:, c:c + K], T.bw[:, c + K:c + K2]
        return slot(T.bw, c, 2, 3), T.bw[:, c + K3:c + K4]

    def prefill(t):
        dma("y", T.bw[:, W + K3 * t:W + K3 * (t + 1)], T.nv[:, K3 * t:K3 * (t + 1)], ["nva%d" % t, "nvb%d" % t, "nvz%d" % t], ["di%d" % t])

    def accum(t):
        dma("g", T.bw[:, W + K3 * t:W + K3 * (t + 1)], T.fw[:, W + K3 * t:W + K3 * (t + 1)], ["oa%d" % t, "ob%d" % t],
            ["di%d" % t], accum_op=ALU.add)

    def back(rnd, t, out, key):
        if rnd == 0 and t > 1:
            gcopy(out, TB, ["tb"], [key])
        elif rnd == 0:
            act(out, TB, AF.Copy, ["tb"], [key])
        else:
            o, ko = perm(rnd, 1, t)
            gat("s", out, T.tb[:, :], o, ["tb", "tbz", ko], [key])

    def loady(rnd, t):
        mm([(bk(0), T.idb[:, :], Y(t))], ["yw%d" % t, "idb"], ["#0"])
        if rnd == 0 or t == 3:
            mm([(bk(2), T.idb[:, :], NW(t))], ["yw%d" % t, "idb"], ["#2"])

    def Pof(rnd, t, h=None):
        if rnd == 2 and t < 2:
            return slot(T.mw, t * K3, 1, 3, h), hk("p%d" % t, h)
        return slot(T.pp, 0, 0, 1, h), hk("pp", h)

    def fgather(rnd, t, e):
        win, wk = fwin(t)
        for h in ((0, 1) if e == "s" else (None,)):
            ob, kob = offb(rnd, t - 1, h)
            gat(e, Bof(rnd, t, h)[0], win, ob, wk + [kob], hk(Bof(rnd, t)[1], h))
        gat(e, Aof(t)[0], win, offa(t - 1)[0], wk + [offa(t - 1)[1]], hk(Aof(t)[1]))

    def mreal(t):
        i = (7, 7, 5, 4)[t]
        mm([(bk(i), T.id2[:, :], Pof(2, t)[0]), (bk(i), T.nib[:, :], Y(t))], ["id2", "nib", "yw%d" % t] + Pof(2, t)[1], ["#%d" % i])

    def fwd(rnd, t, pin, mid=None, tail=None, sfill=None, between=None, pfill=None):
        (a, ka), (b, kb) = Aof(t), Bof(rnd, t)
        (ea, kea), (eb, keb) = EA(rnd, t), EB(t)
        kw = "yw%d" % t
        for h in (0, 1):
            x, y, r = pin(h)
            tt(Pof(rnd, t, h)[0], x, y, ALU.mult, r, Pof(rnd, t, h)[1] + (["m%d" % t] if rnd == 2 and h == 0 else []))
        if t == 3:
            for i in ((6, 5) if rnd == 2 else (5,)):
                mm([(bk(i), T.idb[:, :], T.zb[:, 0:K])], ["idb", "zb"], ["#%d" % i], last=False)
        if pfill:
            pfill()
        if rnd == 2 and t > 1:
            mreal(t)
        for h in (0, 1):
            tt(slot(B[1], 0, 0, 1, h), Pof(rnd, t, h)[0], slot(B[0], 0, 0, 1, h), ALU.subtract, Pof(rnd, t, h)[1] + ["#0"], hk("#1", h))
        if mid:
            mid()
        if t == 3 and rnd < 2:
            for h in (0, 1):
                tt(EB(t, h)[0], slot(B[1], 0, 0, 1, h), Bof(rnd, t, h)[0], ALU.mult, hk("#1", h) + hk(kb, h), hk(keb, h))
            tt(ea, bk(1), a, ALU.mult, ["#1"] + hk(ka), hk(kea))
        else:
            for h in (0, 1):
                tt(EA(rnd, t, h)[0], slot(B[1], 0, 0, 1, h), Aof(t, h)[0], ALU.mult, hk("#1", h) + hk(ka, h), hk(kea, h))
            tt(eb, bk(1), b, ALU.mult, ["#1"] + hk(kb), hk(keb))
        if t == 3:
            vb, kvb = VBof(rnd)
            sq = [(bk(0), "#0"), (bk(1), "#1")] if rnd == 2 else [(blk(T.xs, 0), "xs0"), (bk(0), "#0")]
            act(sq[1][0], a, AF.Square, hk(ka), [sq[1][1]])
            act(sq[0][0], b, AF.Square, hk(kb), [sq[0][1]])
            if sfill:
                sfill()
            if rnd == 2:
                tt(bk(6), ea, bk(2), ALU.mult, ["#2"] + hk(kea), ["#6"])
                mm([(bk(6), T.idf[:, :], b), (bk(6), T.nib[:, :], vb)], ["idf", "nib", kvb] + hk(kb), ["#6"], first=False)
                tt(bk(5), eb, bk(2), ALU.mult, ["#2"] + hk(keb), ["#5"])
                mm([(bk(5), T.idf[:, :], a), (bk(5), T.nib[:, :], blk(T.va3, 0))], ["idf", "nib", "va"] + hk(ka), ["#5"], first=False)
                c1, c3 = DB(3, 0), DB(3, 2)
                tt(c3, bk(1), NW(3), ALU.mult, ["#1", kw], ["db1"])
                act(c3, c3, AF.Identity, ["db1"], ["db1"], bias=1.0)
                tt(c1, bk(0), NW(3), ALU.mult, ["#0", kw], hk("da1"))
                act(c1, c1, AF.Identity, hk("da1"), hk("da1"), bias=1.0)
                tt(mw(3, 1), bk(4), NW(3), ALU.mult, ["#4", kw], ["m3"])
            else:
                tt(bk(4), eb, bk(2), ALU.mult, ["#2"] + hk(keb), ["#4"])
                tt(bk(3), ea, bk(2), ALU.mult, ["#2"] + hk(kea), ["#3"])
                tt(bk(5), a, bk(4), ALU.add, ["#4"] + hk(ka), ["#5"])
                mm([(bk(5), T.nib[:, :], blk(T.va3, 0))], ["nib", "va"], ["#5"], first=False)
                mm([(bk(6), T.idf[:, :], ea)], ["idf"] + hk(kea), ["#6"])
                act(DB(3, 0), bk(5), AF.Copy, ["#5"], hk("da1"))
                tt(bk(3), b, bk(3), ALU.add, ["#3"] + hk(kb), ["#3"])
                tt(mw(3, 1), bk(1), T.pp[:, :], ALU.add, ["#1", "ppa", "ppb"], ["m3"])
                tt(DB(3, 2), bk(3), vb, ALU.subtract, ["#3", kvb], ["db1"])
            if tail:
                tail()
            return
        if rnd == 2:
            act(bk(3), b, AF.Square, hk(kb), ["#3"])
            if t > 0:
                act(bk(4), a, AF.Square, hk(ka), ["#4"])
        if sfill:
            sfill()
        zw = T.yw[:, t * K3 + K:(t + 1) * K3]
        c = W + K3 * t
        if rnd == 0:
            tt(bk(3), ea, bk(2), ALU.mult, ["#2"] + hk(kea), ["#3"])
        else:
            scan(T.tb[:, 2::3], zw, T.ea[:, t * K2:(t + 1) * K2], [kw] + hk(kea) + hk(kb), ["tb"])
            back(rnd, t, T.fw[:, c + K2:c + K3], "ob%d" % t)
        if between:
            between()
        scan(T.fw[:, c:c + K2], zw, T.eb[:, t * K2:(t + 1) * K2], [kw] + hk(keb) + hk(ka), ["oa%d" % t])
        if rnd == 0:
            tt(T.fw[:, c + K2:c + K3], b, bk(3), ALU.add, ["#3"] + hk(kb), ["ob%d" % t])
        if tail:
            tail()
        if rnd == 2:
            tt(b, bk(3), NW(t), ALU.mult, ["#3", kw], hk(kb))
            if t > 0:
                tt(a, bk(4), NW(t), ALU.mult, ["#4", kw], hk(ka))
            if t == 2:
                tt(mw(2, 1), bk(5), NW(2), ALU.mult, ["#5", kw], ["m2"])
        elif t > 0:
            tt(mw(t, 1), bk(1), T.pp[:, :], ALU.add, ["#1", "ppa", "ppb"], ["m%d" % t])

    def pin_win(rnd, t):
        win, wk = fwin(t)
        return lambda h: (win.indirect(offa(t - 1, h)[0]), Bof(rnd, t, h)[0], wk + [offa(t - 1)[1]] + hk(Bof(rnd, t)[1], h))

    def bgather(rnd, t, mid=None):
        win, wk = bwin(t)
        p = t % 2
        ka, kb = "da%d" % p, "db%d" % p

        def ga(h=None):
            gat("s", DB(t, 0, h), win, offa(3 + t, h)[0], wk + [offa(3 + t)[1]], hk(ka, h))

        def gb():
            gat("s", DB(t, 2), win, offb(rnd, 3 + t)[0], wk + [offb(rnd, 3 + t)[1]], [kb])
        if rnd == 2:
            ga(0), ga(1)
            if mid:
                mid()
            gb()
        elif t > 0:
            gb(), ga(0), ga(1)
            if t > 1:
                gcopy(DA(0), DB(t, 2), [kb], ["cb"])
        else:
            ga()

    def ubank(rnd, t):
        return (5, 6) if t == 3 or (t == 1 and rnd < 2) else (3, 4)

    def uload(rnd, t):
        b1, b2 = ubank(rnd, t)
        m_, km = (T.ni8, "ni8") if rnd == 2 and t < 2 else (T.idf, "idf")
        mm([(bk(b1), m_[:, :], EB(t)[0])], [km] + hk(EB(t)[1]), ["#%d" % b1])
        if t > 0 or rnd == 2:
            mm([(bk(b2), m_[:, :], EA(rnd, t)[0])], [km] + hk(EA(rnd, t)[1]), ["#%d" % b2])

    def uprod(rnd, t):
        p, i = t % 2, (t - 1) % 3
        b1, b2 = ubank(rnd, t)
        x1 = (EB(3)[0], hk("eb3")) if t == 3 else (DB(t, 0), hk("da%d" % p))
        x2 = (EA(rnd, 3)[0], hk("ea3")) if t == 3 and rnd == 2 else (DB(t, 2), ["db%d" % p])
        if t == 1 and rnd < 2:
            tt(blk(T.t12, 1), bk(b2), x2[0], ALU.mult, ["#%d" % b2] + x2[1], ["t2_0"])
            for h in (0, 1):
                tt(slot(T.t12, 0, 0, 1, h), slot(B[b1], 0, 0, 1, h), DB(1, 0, h), ALU.mult, ["#%d" % b1] + hk("da1", h), hk("t1_0", h))
        else:
            tt(blk(T.t12, 2 * i), bk(b1), x1[0], ALU.mult, ["#%d" % b1] + x1[1], hk("t1_%d" % i))
            tt(blk(T.t12, 2 * i + 1), bk(b2), x2[0], ALU.mult, ["#%d" % b2] + x2[1], ["t2_%d" % i])
        if t > 0:
            d = (q + t) % NR
            send([(d, topo.engines(core, cores[d]), "u%d_%d" % (rnd, t), [blk(T.t12, 2 * i), blk(T.t12, 2 * i + 1)], blk(T.ul, t - 1))],
                 hk("t1_%d" % i) + ["t2_%d" % i], "lu%d" % t)
            lands("ul%d" % t, "u%d_%d" % (rnd, t), len(topo.engines(cores[(q - t) % NR], core)))

    def bscan(rnd, t, sfill=None, tail=None, between=None):
        p = t % 2
        ka, kb = "da%d" % p, "db%d" % p
        if t == 3:
            tt(DB(t, 1), bk(0), DB(t, 2), ALU.mult, ["#0", kb], ["pb_%d" % p])
            tt(DA(1), bk(5), blk(T.xs, 0), ALU.mult, ["#5", "xs0"], hk("pa"))
            gcopy(DA(0), DB(t, 2), [kb], ["cb"])
        elif t == 2:
            tt(DB(t, 1), bk(1), DB(t, 2), ALU.mult, ["#1", kb], ["pb_%d" % p])
            for h in (0, 1):
                tt(DA(1, h), slot(B[0], 0, 0, 1, h), DB(t, 0, h), ALU.mult, ["#0"] + hk(ka, h), hk("pa", h))
        else:
            uprod(rnd, 1)
            if rnd == 0:
                gcopy(DA(0), DB(t, 2), [kb], ["cb"])
            else:
                act(DA(0), DB(t, 2), AF.Copy, [kb], ["cb"])
            tt(DB(t, 1), bk(1), DB(t, 2), ALU.mult, ["#1", kb], ["pb_%d" % p])
            tt(DA(1), bk(0), DB(t, 0), ALU.mult, ["#0"] + hk(ka), hk("pa"))
        act(DA(2), DB(t, 0), AF.Copy, hk(ka), ["ca"])
        m = T.mw[:, t * K3:(t + 1) * K3]
        km = ["m%d" % t, "mz", "mw%d" % t]
        scan(T.tb[:, 1::2], m, T.db[:, p * K3:(p + 1) * K3], km + hk(ka) + [kb, "pb_%d" % p], ["tb"])
        if t > 1:
            act(bk(1), Aof(t - 1)[0], AF.Square, hk(Aof(t - 1)[1]), ["#1"])
            act(bk(0), Bof(rnd, t - 1)[0], AF.Square, hk(Bof(rnd, t - 1)[1]), ["#0"])
        if sfill:
            sfill()
        back(rnd, t, douts(t)[1], "dob%d" % t)
        if between:
            between()
        c = dpos(t)
        scan(T.bw[:, c:c + K3], m, T.da[:, :], km + ["ca", "cb"] + hk("pa"), ["doa%d" % t])
        if tail:
            tail()

    def breal(t):
        p = t % 2
        if t == 3:
            c1, c3, c2 = DB(3, 0), DB(3, 2), mw(3, 1)
            tt(bk(3), bk(6), c3, ALU.mult, ["#6", "db1"], ["#3"])
            tt(bk(4), bk(6), c2, ALU.mult, ["#6", "m3"], ["#4"])
            tt(blk(T.xs, 1), bk(5), c2, ALU.mult, ["#5", "m3"], ["xs1"])
            tt(blk(T.xs, 0), bk(5), c1, ALU.mult, ["#5"] + hk("da1"), ["xs0"])
            ba, bb = 4, 3
        else:
            da, db, ka, kb = DB(t, 0), DB(t, 2), "da%d" % p, "db%d" % p
            for h in (0, 1):
                tt(slot(B[5], 0, 0, 1, h), slot(B[0], 0, 0, 1, h), DB(t, 0, h), ALU.mult, ["#0"] + hk(ka, h), ["#5" + "ab"[h]])
            tt(blk(T.xs, 1), bk(2), da, ALU.mult, ["#2"] + hk(ka), ["xs1"])
            tt(bk(6), bk(1), db, ALU.mult, ["#1", kb], ["#6"])
            tt(blk(T.xs, 0), bk(2), db, ALU.mult, ["#2", kb], ["xs0"])
            ba, bb = 5, 6
        if t == 3:
            mm([(bk(2), T.idf[:, :], mw(2, 1))], ["idf", "m2"], ["#2"])
        if t > 0:
            act(bk(0), Bof(2, t - 1)[0], AF.Identity, hk(Bof(2, t - 1)[1]), ["#0"], bias=1.0)
            act(bk(1), C3(t - 1)[0], AF.Identity, C3(t - 1)[1], ["#1"], bias=1.0)
        tt(TB, bk(bb), blk(T.xs, 1), ALU.add, ["#%d" % bb, "xs1"], ["tb"])
        back(2, t, douts(t)[1], "dob%d" % t)
        if t == 0:
            tt(blk(T.t12, 4), bk(3), DB(0, 0), ALU.mult, ["#3"] + hk("da0"), hk("t1_2"))
            mm([(bk(7), T.idf[:, :], blk(T.t12, 4))], ["idf"] + hk("t1_2"), ["#7"], first=False, last=False)
        tt(douts(t)[0], bk(ba), blk(T.xs, 0), ALU.add, ["#%d" % ba, "xs0"], ["doa%d" % t])

    def backward(rnd, fills):
        for t in (3, 2, 1):
            sf, tl = fills.get(t, (None, None))
            if t == 3:
                uload(rnd, 2)
            if t == 1:
                mm([(bk(4), T.nif[:, :], blk(T.ul, 2))], ["nif", "ul3"], ["#4"])
            bscan(rnd, t, sfill=sf, tail=tl, between=fills.get((t, "between")))
            if t > 1:
                bgather(rnd, t - 1)
                uprod(rnd, t)
                uload(rnd, t - 2)
            if (t, "after") in fills:
                fills[(t, "after")]()

    def wrapd(b, src, c0, cen, r):
        mm([(bk(b, 24), T.idb[:, :], cen)] + [(bk(b, 24), T.ewd[:, 15 - i:143 - i], src[:, c0 + i:c0 + K:16]) for i in range(16)],
           list(r) + ["idb", "ewd"], ["#%d" % b], last=False)

    def ends(k):
        ts(T.sm[:, 24 * k:24 * k + 24], T.at[:, 24 * k:24 * k + 24], T.lm[:, 4 - 4 * k:5 - 4 * k], ALU.is_equal, ["at%d" % k, "lm0", "lm1"],
           ["sm%d" % k], T.lm[:, 4 * k:4 * k + 1], ALU.mult)

    def wrapend(k, b):
        mm([(bk(b, 24), T.idf[:, :], T.sm[:, 24 * k:24 * k + 24])], ["idf", "sm%d" % k], ["#%d" % b], first=False)

    def sendperm(rnd, k):
        o, ko = perm(rnd, k, 0)
        if k == 0:
            ts(o, bk(7, 24), float(CEN), ALU.add, ["#7"], [ko])
        else:
            ts(o, bk(3, 24), 6.0, ALU.mult, ["#3"], [ko], 6.0 * CEN + 5, ALU.add)
        to_hosts(lambda t: o, lambda t: perm(rnd, k, t)[0], lambda t: "r%d_%d_%d" % (rnd - 1, k, t), [ko], lambda t: perm(rnd, k, t)[1])

    def vote(rnd, sfill):
        win, wk = bwin(0)
        ob, kob = offb(rnd, 3)
        for h in (0, 1):
            mm([(bk(1 + h, H + h), T.idb[:, :], T.zb[:, 0:H + h])], ["idb", "zb"], ["#%d" % (1 + h)], last=False)
        loady(rnd + 1, 0)
        bgather(rnd, 0)
        sfill()
        t2 = blk(T.xs, 1)
        tt(t2, win.indirect(ob), EA(rnd, 0)[0], ALU.mult, wk + [kob] + hk(EA(rnd, 0)[1]), ["xs1"])
        for t in range(2):
            prefill(t)
        tt(bk(4), bk(4), blk(T.ul, 1), ALU.subtract, ["#4", "ul2"], ["#4"])
        b3, b4 = [[slot(B[i], 0, 0, 1, h) for h in (0, 1)] for i in (3, 4)]
        u0 = [slot(T.xs, 0, 0, 1, h) for h in (0, 1)]
        for h in (0, 1):
            tt(b3[h], b3[h], DB(0, 0, h), ALU.mult, hk("#3", h) + hk("da0", h), hk("#3", h))
        for h in (0, 1):
            tt(u0[h], b3[h], slot(T.xs, K, 0, 1, h), ALU.add, hk("#3", h) + ["xs1"], hk("u0", h) + ["xs0"][h:])
        for h in (0, 1):
            tt(b4[h], b4[h], slot(T.ul, 0, 0, 1, h), ALU.subtract, hk("#4", h) + ["ul1"], hk("#4", h))
        for h in (0, 1):
            lo, n = h * H, H + h
            tt(T.sg[:, 1 + lo:1 + lo + H], u0[h], b4[h], ALU.is_lt, hk("#4", h) + hk("u0", h) + ["xs0"], hk("sg", h))
            mm([(bk(1 + h, n), T.be[:, :], T.sg[:, 1 + lo:1 + lo + n]), (bk(1 + h, n), T.bo[:, :], T.sg[:, lo:lo + n])],
               ["be", "bo"] + hk("sg")[:h + 1], ["#%d" % (1 + h)], first=False)

        def vscan(out, d0, d1, ini, r, w):
            op("v", lambda: V.tensor_tensor_scan(out, d0, d1, ini, ALU.max, ALU.min), r, w)
        vscan(T.ls[:, 0:H], bk(1, H), T.d1f[:, 0:H], INI, ["#1", "d1f"], ["lsa"])
        vscan(T.nx[:, 399:14 + H:-1], B[2][:, H::-1], T.d1r[:, 384:H - 1:-1], INI, ["#2", "d1r", "nx"], ["nxb"])
        vscan(T.ls[:, H:385], bk(2, H + 1), T.d1f[:, H:385], T.ls[:, H - 1:H], ["#2", "d1f", "lsa"], ["ls"])
        wrapd(7, T.ls, 0, T.cw[:, 0:24], ["ls", "lsa", "cw"])
        vscan(T.nx[:, 14 + H:14:-1], B[1][:, H - 1::-1], T.d1r[:, H - 1::-1], T.nx[:, 15 + H:16 + H], ["#1", "d1r", "nxb"], ["nx"])
        ts(T.lm[:, 0:1], T.ls[:, 384:385], -INI, ALU.add, ["ls"], ["lm0"])
        ts(T.lm[:, 4:5], T.nx[:, 15:16], -INI, ALU.add, ["nx"], ["lm1"], -1.0, ALU.mult)
        ends(0)
        wrapend(0, 7)
        ends(1)
        if rnd == 0:
            wrapd(3, T.nx, 16, T.cw[:, :], ["nx", "nxb", "cw"])
        else:
            gat("s", T.gx[:, :], T.nx[:, 16:400], T.su[:, :], ["nx", "nxb", "su"], ["gx"])
            wrapd(3, T.gx, 0, T.sx[:, :], ["gx", "sx"])
            tt(C3(0)[0], bk(5), NW(0), ALU.mult, ["#5", "yw0"], C3(0)[1])
        wrapend(1, 3)
        sendperm(rnd + 1, 0)

    dma("s", T.an32[:, :], T.an[:, :], (), ["an32"])
    dma("y", T.bn32[:, :, :], T.bn[:, :], (), ["bn32"])
    dma("s", T.wraw[:, :], T.wt[:, :], (), ["wraw"])
    dma("y", Y(0), T.yt[:, :], (), ["y0"])
    dma("y", T.thb[:, :], T.th[:, :], (), ["thb"])
    dma("y", T.vab[:, :], T.va[:, :], (), ["vab"])
    iota(T.ip[:, 0:1], [[0, 1]], 0, 1, ["ip"], fl=False)
    iota(T.rt[:, 0:K], [[1, K]], POS0, 0, ["rt0"])
    iota(T.rt[:, K2:W], [[1, K2]], POS0 + K2, 0, ["rt2"])
    dma("g", T.fw[:, 0:W], T.th[:, :], (), ["fth"])
    ms(T.ew[:, :], 0.0, ["ew"])
    ts(T.ip[:, 1:2], T.ip[:, 0:1], 4, ALU.logical_shift_right, ["ip"], ["ip1"], 1, ALU.bitwise_and)
    ts(T.ip[:, 2:3], T.ip[:, 0:1], 1, ALU.bitwise_and, ["ip"], ["ip2"])
    ts(T.ip[:, 3:4], T.ip[:, 0:1], 15, ALU.bitwise_and, ["ip"], ["ip3"])
    ms(T.zb[:, :], -33792.0, ["zb"])
    cp(T.col[:, 0:4], T.ip[:, 0:4], ["ip", "ip1", "ip2", "ip3"], ["col"])
    ms(slot(T.yw, K, 0, 2), 0.0, ["z0"])
    ts(T.col[:, 5:6], T.col[:, 1:2], -1.0, ALU.mult, ["col"], ["col0"], 1.0, ALU.add)
    ts(T.col[:, 4:5], T.col[:, 2:3], -1.0, ALU.mult, ["col"], ["col4"], float(-CEN - POS0 - dpos(0)), ALU.add)
    ts(T.idb[:, :], T.rt[:, 0:128], float(-POS0), ALU.add, ["rt0", "col"], ["idb"], T.col[:, 0:1], ALU.is_equal)

    def gsel(out, pat, cmp_, fill, base, cm, key):
        op("g", lambda: g.affine_select(out, out, pat, cmp_, fill, base, cm), [key], [key])
    act(T.pb[:, K:K2], T.rt[:, 0:K], AF.Silu, ["rt0"], ["pb1"], bias=float(W + K2))
    act(T.pb[:, 0:K], T.rt[:, 0:K], AF.Identity, ["rt0"], ["pb0"], scale=2.0, bias=float(W + 1 - POS0))
    ts(T.rt[:, K:K2], T.rt[:, 0:K], float(K), ALU.add, ["rt0"], ["rt1"])
    cp(T.ew[:, 15:143:16], T.idb[:, 0::16], ["idb", "ew"], ["ew"])
    ts(T.x2[:, :, 0:16], T.bn32[:, :, :], T.col[:, 5:6], ALU.mult, ["bn32", "col0"], ["x2a"])
    ts(T.x2[:, :, 16:32], T.bn32[:, :, :], T.col[:, 1:2], ALU.mult, ["bn32", "col"], ["x2b"])
    cp(T.nm[:, :, 0:24], T.an32[:, :], ["an32"], ["nma"])
    act(T.rt[:, :].indirect(names(0, 0, 24)), blk(T.pb, 0), AF.Silu, ["pb0", "pb1", "nma", "rt0", "rt1", "rt2"], ["rt"])
    act(T.pb[:, K2:2 * K2], T.pb[:, 0:K2], AF.Identity, ["pb0", "pb1"], ["pb2", "pb3"], bias=float(K3))
    op("v", lambda: V.transpose(T.y2[:, :, :], T.x2[:, :, :]), ["x2a", "x2b"], ["y2"])
    ts(NW(0), T.wraw[:, :], -0.125, ALU.mult, ["wraw", "y0", "z0"], ["yw0"])
    tt(T.z2[:, :, :], T.y2[:, :, 0:16], T.y2[:, :, 16:32], ALU.add, ["y2"], ["z2"])
    ms(T.ewd[:, :], 0.0, ["ewd"])
    for c in range(6):
        cp(T.nm[:, :, 24 + c:48:6], T.z2[:, c, :], ["z2"] + (["nma"] if c == 5 else []), ["n0"] if c == 5 else ["nmb%d" % c])
    tt(T.ewd[:, 15:143:16], T.idb[:, 1::16], T.idb[:, 0::16], ALU.subtract, ["idb", "ewd"], ["ewd"])
    to_hosts(lambda t: T.nm[:, t, :], lambda t: T.ntl[:, t, :], lambda t: "nm%d" % t, ["n0"], nk)
    scat(0, 1)
    to_hosts(lambda t: T.yw[:, 0:K3], lambda t: T.yw[:, t * K3:(t + 1) * K3], lambda t: "yw%d" % t, ["yw0"], lambda t: "yw%d" % t)
    cs_make(2)
    cs_make(3)
    for t in (0, 1, 2):
        iota(slot(T.nv, t * K3, 0, 2), [[0, K]], 0, 0, ["nvz%d" % t])

    def negw(t):
        gcopy(mw(t, 2), NW(t), ["yw%d" % t], ["mw%d" % t])

    loady(0, 0)
    gptr(0)
    gat("v", Bof(0, 0)[0], T.thb[:, :], names(0, 24, 48), ["thb", "n0"], hk("B0"))
    gat("v", Aof(0)[0], T.thb[:, :], names(0, 0, 24), ["thb", "n0"], hk("A0"))
    fwd(0, 0, lambda h: (T.thb[:, :].indirect(names(0, 12 * h, 12 * h + 12)), Bof(0, 0, h)[0], ["thb", "n0"] + hk("B0", h)))
    scat(1)
    gptr(1)
    wrap1(0)
    loady(0, 1)
    def nvmake(t, e):
        gat(e, slot(T.nv, t * K3, 1, 2), T.vab[:, :], names(t, 0, 24), ["vab", nk(t)], ["nva%d" % t], neg=True)
        gat(e, T.nv[:, t * K3 + K2:(t + 1) * K3], T.vab[:, :], names(t, 24, 48), ["vab", nk(t)], ["nvb%d" % t], neg=True)
        prefill(t)
    nvmake(0, "v")
    nvmake(1, "v")
    nvmake(2, "v")
    ts(T.nib[:, :], T.idb[:, :], -1.0, ALU.mult, ["idb"], ["nib"])
    conv1(0)
    cp(T.idf[:, :], T.idb[:, :], ["idb"], ["idf"])
    wrap1(1, 4)
    fgather(0, 1, "v")
    fwd(0, 1, pin_win(0, 1), tail=lambda: conv1(1, 4), sfill=lambda: (scat(2), gptr(2)))
    cs_make(4)
    cs_make(5)
    accum(0)
    iota(T.mw[:, K3::3], [[0, K3]], 0, 0, ["mz"])
    accum(1)
    negw(3)
    loady(0, 2)
    wrap1(2)

    scat(3)
    gptr(5)
    scat(4, 0)

    def consts():
        both = ((T.be, "be", 0), (T.bo, "bo", 1))
        for m_, k, c in both:
            iota(m_[:, :], [[0, 64], [2048 * (2 * c - 1), 2]], 2048 * (1 - c), 0, [k])
        for m_, k, c in both:
            gsel(m_[:, 0:112], [[-16, 7], [0, 16]], ALU.is_ge, 0.0, 0, 1, k)
        for m_, k, c in both:
            gsel(m_[:, 0:112], [[16, 7], [0, 16]], ALU.is_ge, 0.0, 31, -1, k)
        for m_, k, c in both:
            gsel(m_[0:112, 112:128], [[0, 16]], ALU.is_ge, 0.0, 15, -1, k)

    def consts2():
        iota(T.cwi[:, :], [[16, 24]], -CEN, 0, ["cwi"])
    fgather(0, 2, "v")
    fwd(0, 2, pin_win(0, 2), tail=lambda: conv1(2))
    gat("v", T.va3[:, 0:K2], T.vab[:, :], names(3), ["vab", "n3"], ["va", "vb0"])
    accum(2)
    negw(2)
    consts2()
    iota(T.sg[:, 384:400], [[0, 16]], 0, 0, ["sgb"])
    iota(T.sg[:, 0:16], [[0, 16]], 0, 0, ["sga"])
    loady(0, 3)
    wrap1(5)
    fgather(0, 3, "s")
    scat(4, 1)
    fwd(0, 3, pin_win(0, 3), tail=lambda: (conv1(5), wrap1(4)), sfill=lambda: gptr(4))

    def s3():
        scat(5, 0)
        negw(1)

    def t3():
        cs_make(6)

    def a3():
        scat(5, 1)

    def s2():
        act(T.nif[:, :], T.idb[:, :], AF.Copy, ["idb"], ["nif"], scale=-1.0)

    def s1():
        act(T.d1f[:, :], T.pb[:, 0:385], AF.Identity, ["pb0", "pb1", "col4"], ["d1f"], bias=T.col[:, 4:5])
        act(T.cw[:, :], T.cwi[:, :], AF.Identity, ["cwi", "col"], ["cw"], bias=T.col[:, 3:4])
        act(T.d1r[:, :], T.d1f[:, :], AF.Copy, ["d1f"], ["d1r"], scale=-1.0)
        for k in (0, 1):
            act(T.at[:, 24 * k:24 * k + 24], T.cw[:, :], AF.Identity, ["cw"], ["at%d" % k], bias=INI * (1 - 2 * k))

    def late():
        s1()
        for i, b in enumerate((7, 6, 5)):
            c = slice(512 * i, 512 * i + 512)
            mm([(bk(b, 512), T.idb[:, :], T.thb[:, c]), (bk(b, 512), T.nib[:, :], T.vab[:, c])], ["idb", "nib", "thb", "vab"], ["#%d" % b])
            act(T.bw[:, c], bk(b, 512), AF.Copy, ["#%d" % b], ["dbase%d" % i])
        gcopy(T.b0c[:, :], Bof(0, 0)[0], hk("B0"), ["b0c"])
        for s_ in (0, 4):
            iota(slot(T.tb, 0, s_, 6), [[0, K]], 0, 0, ["tbz"])
        scat(6, 0)
    backward(0, {3: (s3, t3), (3, "after"): a3, 2: (s2, None), (2, "between"): lambda: conv1(4),
                 (2, "after"): lambda: (gptr(3), wrap1(3)), 1: (None, lambda: conv1(3)), (1, "between"): consts})
    vote(0, late)

    for rnd in (1, 2):
        ok = ["b0c", perm(rnd, 0, 0)[1]]
        gat("s", Bof(rnd, 0)[0], T.b0c[:, :], perm(rnd, 0, 0)[0], ok, hk("B0"))

        def pin0(h):
            return T.b0c[:, :].indirect(perm(rnd, 0, 0, h)[0]), Aof(0, h)[0], ok + hk("A0", h)
        if rnd == 1:
            scat(6, 1)
            fwd(rnd, 0, pin0, mid=lambda: sendperm(1, 1),
                tail=lambda: (cp(T.sx[:, :], bk(3, 24), ["#3"], ["sx"]), ts(T.su[:, :], bk(3, 24), float(CEN), ALU.add, ["#3"], ["su"])))
        else:
            fwd(rnd, 0, pin0, mid=lambda: sendperm(2, 1), tail=lambda: convb(1, 0, 1, 6))
        accum(0)
        need("y", [lastw["oa0"]])
        prefill(2)
        loady(rnd, 1)
        if rnd == 1:
            wrap(4, T.rt, 0, W, ["rt"])
        win, wk = fwin(1)
        rho1, krho1 = perm(rnd, 0, 1)
        gat("s", blk(T.xs, 0), win, offb(rnd - 1, 0)[0], wk + [offb(rnd - 1, 0)[1]], ["xs0"])
        if rnd == 1:
            gat("v", Aof(1)[0], win, offa(0)[0], wk + ["la0"], hk("A1"))
        else:
            for h in (0, 1):
                gat("vs"[h], Aof(1, h)[0], win, offa(0, h)[0], wk + ["la0"], hk("A1", h))
        pupd(rnd, 1)
        gat("s", Bof(rnd, 1)[0], blk(T.xs, 0), rho1, ["xs0", krho1], hk("B1"))
        if rnd == 1:
            pupd(rnd, 2)
            pupd(rnd, 3)
        fwd(rnd, 1, lambda h: (blk(T.xs, 0).indirect(perm(rnd, 0, 1, h)[0]), Aof(1, h)[0], ["xs0", krho1] + hk("A1", h)),
            pfill=lambda: wrapb(rnd, 1, 1, 7), tail=lambda: (convb(rnd, 1, 1, 7), rnd == 1 and conv(T.fin[:, :], 4, 0, 96, 0, ["fin"])), sfill=(lambda: pupd(2, 2)) if rnd == 2 else None)
        accum(1)
        loady(rnd, 2)
        fgather(rnd, 2, "s")
        for li in (4, 5):
            pupd(rnd, li)
        fwd(rnd, 2, pin_win(rnd, 2), pfill=lambda: wrapb(rnd, 2, 1, 7), **{"between" if rnd == 1 else "tail": lambda: convb(rnd, 2, 1, 7)})
        accum(2)
        loady(rnd, 3)
        fgather(rnd, 3, "s")
        o, ko = perm(rnd, 0, 3)
        gat("s", VBof(rnd)[0], VBof(rnd - 1)[0], o, [VBof(rnd - 1)[1], ko], [VBof(rnd)[1]])
        if rnd == 2:
            pupd(2, 3)
            fwd(rnd, 3, pin_win(rnd, 3))
            wrapb(rnd, 3, 3, 7)
        else:
            fwd(rnd, 3, pin_win(rnd, 3), pfill=lambda: wrapb(1, 3, 3, 7), tail=lambda: convb(1, 3, 3, 7), sfill=lambda: pupd(1, 0))

            def g1():
                act(T.at[:, 24:48], T.sx[:, :], AF.Identity, ["sx"], ["at1"], bias=-INI)
                act(T.ni8[:, :], T.idf[:, :], AF.Copy, ["idf"], ["ni8"], scale=-0.125)
                act(T.id2[:, :], T.idf[:, :], AF.Copy, ["idf"], ["id2"], scale=2.0)
                wrapb(1, 0, 1, 6)
            backward(rnd, {(1, "between"): g1})

            def late2():
                gcopy(T.b0c[:, :], Bof(1, 0)[0], hk("B0"), ["b0c"])
                act(bk(5), Aof(0)[0], AF.Square, hk("A0"), ["#5"])
            vote(rnd, late2)

    for t in (3, 2, 1, 0):
        if t == 0:
            mm([(bk(7), T.ni8[:, :], blk(T.ul, i - 1)) for i in (3, 2)], ["ni8", "ul3", "ul2"], ["#7"], last=False)
        elif t < 3:
            mreal(t - 1)
        breal(t)
        if t == 3:
            bgather(2, 2, lambda: (uprod(2, 3), convb(2, 3, 3, 7)))
        elif t > 0:
            bgather(2, t - 1)
            uprod(2, t)
            tt(bk(2), bk(7), NW(t - 1), ALU.mult, ["#7", "yw%d" % (t - 1)], ["#2"])
        if t > 0:
            uload(2, t - 1)
    tt(blk(T.t12, 5), bk(4), DB(0, 2), ALU.mult, ["#4", "db0"], ["t2_2"])
    mm([(bk(7), T.idf[:, :], blk(T.t12, 5))], ["idf", "t2_2"], ["#7"], first=False)
    wk = ["%s%d" % (s, i) for s in ("dbase", "di") for i in range(3)] + ["do%s%d" % (s, i) for i in range(4) for s in "ab"] + ["fin"]
    for e, lo, hi in (("s", 0, 448), ("v", 896, W), ("s", 448, 896)):
        gat(e, T.fw[:, lo:hi], T.bw[:, :], T.fin[:, lo // 16:hi // 16], wk, ["out%d" % lo] + (["fth"] if lo == 0 else []))
        dma("y", T.yd[:, lo:hi], T.fw[:, lo:hi], ["out%d" % lo], ())
    tt(T.pp[:, :], bk(7), blk(T.ul, 0), ALU.add, ["#7", "ul1"], ["ppa", "ppb"])
    dma("y", T.yh[:, :], T.pp[:, :], ["ppa", "ppb"], ())
    rest = [(s, v) for s, v in cnt.items() if max(seen[e].get(s, 0) for e in seen) < v]
    need("y", rest)
